import numpy as np, ml_dtypes
CORES = [66,74,82,90,194,202,210,218]
N = 8
import mx_ref
BF = ml_dtypes.bfloat16
def gcols(t, e):
    v = np.concatenate([t.reshape(8, 16, -1, 4), np.zeros((8, 16, 1, 4), BF)], axis=2)
    return np.ascontiguousarray(np.stack([v[g][:, e[g]] for g in range(8)])).reshape(128, -1)
def tile(rs):
    return np.stack(rs, axis=2).reshape(128, -1).astype(BF)
def cut(t, i, w=512):
    return t[:, w * i:w * i + w]
def pick(q, e):
    c = np.concatenate([q[0].reshape(128, -1, 4), np.zeros((128, 1, 4), np.uint8)], axis=1); s = np.concatenate([q[1], np.ones((16, 1), np.uint8)], axis=1)
    return (np.ascontiguousarray(c[:, e].reshape(128, -1)), np.ascontiguousarray(s[:, e]))
def join(*qs):
    return (np.concatenate([q[0] for q in qs], axis=1), np.concatenate([q[1] for q in qs], axis=1))
def put(q, e, v):
    c, s = q[0].reshape(128, -1, 4).copy(), q[1].copy(); c[:, e] = v[0].reshape(128, -1, 4); s[:, e] = v[1]
    return (c.reshape(128, -1), s)
def pk(c, s):
    return (np.ascontiguousarray(c), mx_ref.live(s))
def emit(q):
    return q[0], q[1]
def packed(v, rng):
    q = [mx_ref.quantize(np.ascontiguousarray(v[r])) for r in range(N)]
    return np.stack([a for a, b in q]), np.stack([mx_ref.plane(b, rng) for a, b in q])
def values_of_codes():
    e, c = np.zeros((128, 128, 4), np.float32), np.zeros((128, 2, 4), np.uint8)
    e[np.arange(128), np.arange(128), 0] = 1
    c[:127, :, 0] = np.arange(256).reshape(2, 128).T[:127]
    return mx_ref.matmul(mx_ref.quantize(e.reshape(128, 512).astype(BF)), (c.reshape(128, 8), np.full((16, 2), 127, np.uint8))).T.reshape(-1).astype(np.float64)
CODE_VALUE, SCALE_VALUE = values_of_codes(), 2.0 ** (np.arange(256) - 127.0)
def decode(q):
    return (CODE_VALUE[q[0]].reshape(16, 8, -1, 4) * SCALE_VALUE[q[1]][:, None, :, None] + 0.0).reshape(128, -1).astype(np.float32)
def f(rng, *shape):
    return mx_ref.flush((rng.standard_normal(shape, dtype=np.float32) * np.exp2(rng.integers(-2, 3, shape[:-1] + (1,)))).astype(BF))
def wide(rng, *shape, cols=0):
    v = rng.standard_normal(shape, dtype=np.float32) * np.exp2(rng.integers(-12, 13, shape)).astype(np.float32)
    if cols: v *= np.repeat(np.exp2(rng.integers(-cols, cols + 1, shape[:-2] + (1, shape[-1] // 4))) * (rng.random(shape[:-2] + (1, shape[-1] // 4)) > 0.0625), 4, axis=-1).astype(np.float32)
    return mx_ref.flush(v.astype(BF))
C, B, F, K, R = 448, 10, 1, 2, 2
T = 2 ** B
def keys(p):
    m = (p.reshape(8, 16, C) < 0).astype(np.int64)
    return np.sum(m[:, :B] << np.arange(B)[:, None], axis=1), np.sum(m[:, B:B + F] << np.arange(F)[:, None], axis=1)
def insert(a):
    slots, free = np.full((8, T), -1), np.ones((8, C), bool)
    for k in range(K):
        for g in range(8):
            s = (a[g] + k) % T
            want = np.flatnonzero(free[g] & (slots[g][s] < 0))
            at, first = np.unique(s[want], return_index=True)
            slots[g, at] = want[first]
            free[g, want[first]] = False
    return slots
def search(slots, held, a, h):
    found = np.full((8, C), -1)
    for k in range(K):
        c = np.take_along_axis(slots, (a + k) % T, axis=1)
        hit = (found < 0) & (c >= 0) & (np.take_along_axis(held, np.maximum(c, 0), axis=1) == h)
        found[hit] = c[hit]
    return found
def numbers_of(rng):
    return {"x": np.array(f(rng, N, 128, 4 * C)), "u": np.array(f(rng, N, 128, 512)), "v": np.array(f(rng, N, 128, 512))}
def weights(rng, w):
    c, p = packed(w, rng)
    return {"wc": c, "ws": p}
def still(rng):
    w = np.zeros((N, 128, 4, 128, 4), np.float32)
    i = np.arange(128)
    for b in range(4): w[:, i, b, i, b] = 32
    return weights(rng, w.reshape(N, 128, 2048).astype(BF))
def spots(rng):
    e = np.stack([np.concatenate([[0, T - 1], 1 + rng.permutation(T - 2)[:C - 2]]) for g in range(8)])
    return rng.permuted(np.tile(e, (N, 1, 1)), axis=2)
def plant(d, rng, a, h, size, look):
    x, u = d["x"].reshape(N, 8, 16, C, 4), d["u"].reshape(N, 128, 8, 16, 4)
    k = ((a + (h << B))[..., None] >> np.arange(16)) & 1
    m = np.where(k == 1, -1.0, rng.integers(0, 2, k.shape)) * size[:, None, None, None]
    m[..., B + F:] = 0
    x[:, :, :8] = 0
    x[:, :, :4] = m.reshape(N, 8, C, 4, 4).transpose(0, 1, 3, 2, 4).astype(np.float32).astype(BF)
    u[:, :, :, :B + F] = 0
    for g in range(8):
        for i in range(B + F): u[:, 16 * g + i // 4, g, i, i % 4] = look.astype(np.float32).astype(BF)
    return {"x": x.reshape(N, 128, 4 * C), "u": u.reshape(N, 128, 512), "v": d["v"], **still(rng)}
def setup_inputs(rng):
    return {**numbers_of(rng), **weights(rng, f(rng, N, 128, 2048))}
def setup_inputs_crowd(rng):
    s = T - C // 4 - 4
    a = (s + np.repeat(np.arange(C // 2), np.tile([3, 1, 0, 4, 0, 0, 6, 2], C // 16))) % T
    a = rng.permuted(np.tile(a, (N, 8, 1)), axis=2)
    e = int(rng.integers(N))
    o = rng.permutation(8)
    m = np.where(o % 2 == 0, C // 32, rng.integers(0, C // 16, 8))
    z = (s + 3 + 8 * ((m + 1 + rng.integers(0, C // 16 - 1, 8)) % (C // 16))) % T
    a[e] = ((s + 3 + 8 * m) % T)[:, None]
    h = rng.integers(0, 2 ** F, (N, 8, C))
    b, n = (e - 1) % N, (e + 1) % N
    for g in range(8):
        if o[g] < 4:
            a[e, g, C - K:] = z[g]
            h[e, g, C - K:] = rng.permutation(2 ** F)[:K]
            j = np.flatnonzero(a[b, g] == z[g])[0]
            a[b, g, j] = a[b, g, C - 1]
            a[b, g, C - 1] = z[g]
            h[b, g, a[b, g] == z[g]] = h[e, g, C - 1]
        else:
            h[e, g, K:] = h[n, g, np.flatnonzero(a[n, g] == a[e, g, 0])[0]]
    size = np.where((np.arange(N) + rng.integers(2)) % 2 == 0, 64.0, 1.0)
    return plant(numbers_of(rng), rng, a, h, size, np.ones(N))
def setup_inputs_found(rng):
    e = int(rng.integers(N))
    a = spots(rng)
    z, c = (e + 2) % N, int(rng.integers(1, C))
    for g in range(8):
        a[z, g, np.flatnonzero(a[z, g] == 0)[0]] = a[z, g, c]
        a[z, g, c] = 0
    h = np.tile(rng.integers(0, 2 ** F, (8, 1)) * (rng.permutation(8) % 2)[:, None], (N, 1, C))
    h[e] = (h[e] + 1) % 2 ** F
    d = plant(numbers_of(rng), rng, a, h, np.ones(N), np.ones(N))
    x = d["x"].reshape(N, 128, C, 4)
    x[z, :, c] = 0
    return {**d, "x": x.reshape(N, 128, 4 * C)}
def setup_inputs_sizes(rng):
    small = (np.arange(N) + rng.integers(N)) % N < N // 2
    a = spots(rng)
    h = rng.integers(0, 2 ** F, (N, 8, C))
    return plant(numbers_of(rng), rng, a, h, np.where(small, 2.0 ** -30, 2.0 ** 27), np.where(small, 2.0 ** -30, 2.0 ** 30))
def setup_inputs_spread(rng):
    d = setup_inputs(rng)
    d["x"] = wide(rng, N, 128, 4 * C, cols=6)
    return d
def check_inputs(d):
    b = []
    for k in ("x", "u", "v"):
        a = np.abs(d[k].astype(np.float32))
        if not (np.isfinite(a).all() and ((a == 0) | (a >= 2.0 ** -30) & (a <= 2.0 ** 30)).all()): b.append("a value of " + k)
    c, s = d["wc"] & 127, np.stack([mx_ref.live(p) for p in d["ws"]])
    if (c == 127).any(): b.append("a code of wc")
    if ((s < 85) | (s > 160))[c.reshape(N, 16, 8, 512, 4).max(axis=(2, 4)) > 0].any(): b.append("a scale of ws")
    return b
def reference(x, u, v, wc, ws):
    qu = [mx_ref.quantize(u[r]) for r in range(N)]
    lay = [pk(wc[r], ws[r]) for r in range(N)]
    now = [x[r] for r in range(N)]
    for t in range(R):
        made, a, h, slots, answers = [], [], [], [], []
        for r in range(N):
            q = mx_ref.quantize(now[r])
            made.append(tile([mx_ref.matmul(pick(lay[r], np.arange(128 * b, 128 * b + 128)), q) * np.float32(0.03125) for b in range(4)]))
            mx_ref.quantize(made[r])
            i, j = keys(mx_ref.matmul(qu[r], q))
            a.append(i)
            h.append(j)
            slots.append(insert(i))
        for r in range(N):
            n = (r + 1) % N
            answers.append(mx_ref.quantize(gcols(made[n], search(slots[n], h[n], a[r], h[r]))))
        came = decode(join(*answers))
        now = [(made[r].astype(np.float32) + cut(came, r, 4 * C)).astype(BF) for r in range(N)]
    y = np.zeros((N, 128, C), np.float32)
    oc, osc = np.zeros((N, 128, 4 * C), np.uint8), np.zeros((N, 16, C), np.uint8)
    for r in range(N):
        q = mx_ref.quantize(now[r])
        y[r] = mx_ref.matmul(mx_ref.quantize(v[r]), q)
        oc[r], osc[r] = emit(q)
    return {"y": y, "oc": oc, "osc": osc}

@@ -1,0 +1,406 @@
+from concourse.mybir import dt, AluOpType as A, AxisListType, ActivationFunctionType as F
+
+C, H, K, KH = 448, 224, 28, 14
+SLOTS = 1024
+DW = 464
+GB, FB = 512, 2048
+STEP = FB - GB
+EPS = 2.0 ** -10
+MUL = -STEP / EPS
+EMPTY = -1025.0
+B4, B16, S16 = 2048.0, 2000.0, 4096
+TAIL = 128
+ROW = [16 * (c + 1) for c in range(K)]
+OFF = [sum(ROW[:c]) for c in range(K)]
+HALF = "float16"
+Q4 = "float8_e4m3fn_x4"
+
+SCRATCH = {
+    "xin": ("sbuf", [128, 4 * C], "bfloat16"), "xa": ("sbuf", [128, 4 * C], "bfloat16"), "xb": ("sbuf", [128, 4 * C], "bfloat16"),
+    "ut": ("sbuf", [128, 512], "bfloat16"), "vt": ("sbuf", [128, 512], "bfloat16"),
+    "uq": ("sbuf", [128, 128], Q4), "us": ("sbuf", [128, 128], "uint8"),
+    "vq": ("sbuf", [128, 128], Q4), "vs": ("sbuf", [128, 128], "uint8"),
+    "wq": ("sbuf", [128, 512], Q4), "wp": ("sbuf", [128, 512], "uint8"),
+    "ones": ("sbuf", [128, 512], "bfloat16"),
+    "et": ("sbuf", [128, 2048], "bfloat16"), "eq4": ("sbuf", [128, 512], Q4), "es": ("sbuf", [128, 512], "uint8"),
+    "kt": ("sbuf", [128, 1024], "bfloat16"), "kq": ("sbuf", [128, 256], Q4), "ks": ("sbuf", [128, 256], "uint8"),
+    "sign": ("sbuf", [128, H], "bfloat16"), "bits": ("sbuf", [128, 512], "bfloat16"),
+    "bq0": ("sbuf", [128, 128], Q4), "bs0": ("sbuf", [128, 128], "uint8"),
+    "bq1": ("sbuf", [128, 128], Q4), "bs1": ("sbuf", [128, 128], "uint8"),
+    "pt": ("sbuf", [128, 4 * C], "bfloat16"), "dn": ("sbuf", [128, 4 * DW], "bfloat16"),
+    "ps": ("psum", [128, 4096], "float32"),
+    "pi": ("sbuf", [128, 8], "int32"), "col": ("sbuf", [128, 16], "float32"), "k16": ("sbuf", [128, 16], "float32"),
+    "gm": ("sbuf", [128, 32], "float32"), "r16": ("sbuf", [128, 16], "float32"), "c16": ("sbuf", [128, K], "float32"),
+    "t4": ("sbuf", [128, 8 * K], "float32"), "d4": ("sbuf", [128, 8 * K], "float32"),
+    "t16": ("sbuf", [128, C], "bfloat16"), "d16": ("sbuf", [128, C], HALF),
+    "ramp": ("sbuf", [128, SLOTS], "float32"), "jw": ("sbuf", [128, K], "float32"), "jn": ("sbuf", [128, K], "float32"),
+    "mtmp": ("sbuf", [128, TAIL], "float32"), "mask": ("sbuf", [128, TAIL], "bfloat16"),
+    "z4": ("sbuf", [128, 8 * K], "float32"), "qi": ("sbuf", [128, 2 * K], "int32"), "qj": ("sbuf", [128, 2 * K], "int32"),
+    "qo": ("sbuf", [128, 2 * K], "uint16"), "hb": ("sbuf", [128, K], "float32"),
+    "af": ("sbuf", [128, K], "float32"), "ab": ("sbuf", [128, K], "float32"),
+    "rep": ("sbuf", [128, C], "uint16"), "val": ("sbuf", [128, C], "float32"),
+    "cmp": ("sbuf", [128, sum(ROW)], "bfloat16"), "zs": ("sbuf", [128, K * TAIL], "bfloat16"), "acc": ("sbuf", [128, K], "float32"),
+    "s0": ("sbuf", [128, K], "float32"), "s1": ("sbuf", [128, K], "float32"), "s2": ("sbuf", [128, K], "float32"),
+    "so": ("sbuf", [128, K], "uint16"),
+    "tf": ("sbuf", [128, 2 * C], "float32"), "look": ("sbuf", [128, 2 * C], HALF), "z16": ("sbuf", [128, 2 * C], HALF),
+    "x1": ("sbuf", [128, 2 * K], "int32"), "x2": ("sbuf", [128, 2 * K], "int32"),
+    "x3": ("sbuf", [128, K], "float32"), "x4": ("sbuf", [128, K], "float32"), "x5": ("sbuf", [128, K], "float32"),
+    "fin": ("sbuf", [128, K], "uint16"), "yo": ("sbuf", [128, C], "float32"),
+}
+for _t in range(3):
+    SCRATCH["xq%d" % _t] = ("sbuf", [128, C], Q4)
+    SCRATCH["xs%d" % _t] = ("sbuf", [128, C], "uint8")
+for _t in range(2):
+    SCRATCH["pq%d" % _t] = ("sbuf", [128, C], Q4)
+    SCRATCH["pp%d" % _t] = ("sbuf", [128, C], "uint8")
+    SCRATCH["lq%d" % _t] = ("sbuf", [128, C], Q4)
+    SCRATCH["lp%d" % _t] = ("sbuf", [128, C], "uint8")
+    SCRATCH["msg%d" % _t] = ("sbuf", [128, 2 * K], "uint16")
+    SCRATCH["key%d" % _t] = ("sbuf", [128, 2 * K], "uint16")
+    SCRATCH["tab%d" % _t] = ("sbuf", [128, FB + SLOTS], "float32")
+
+SEMAPHORES = (["cv", "ca", "ct", "cg"] + ["d%d" % i for i in range(20)] + ["l%d" % i for i in range(8)]
+              + ["r%d" % i for i in range(8)])
+
+
+def schedule(g, T, ops):
+    queue = {"v": g.vector, "a": g.scalar, "t": g.tensor, "g": g, "s": g.sync}
+    writer, readers, clock = {}, {}, {e: {} for e in queue}
+    for i, o in enumerate(ops):
+        deps = set()
+        for k in o["r"] + o["w"]:
+            if k in writer:
+                deps.add(writer[k])
+        for k in o["w"]:
+            deps.update(readers.get(k, []))
+        o["waits"] = []
+        if o["e"] is not None:
+            ck = clock[o["e"]]
+            for d in sorted(deps, reverse=True):
+                p = ops[d]
+                if ck.get(p["src"], -1) >= d:
+                    continue
+                o["waits"].append(d)
+                p["used"] = True
+                for s, n in p["snap"].items():
+                    ck[s] = max(ck.get(s, -1), n)
+            o["snap"] = dict(ck)
+        else:
+            o["snap"] = {}
+        o["snap"][o["src"]] = i
+        for k in o["w"]:
+            writer[k] = i
+            readers[k] = []
+        for k in o["r"]:
+            readers.setdefault(k, []).append(i)
+    count = {}
+    for o in ops:
+        if o["sem"] is None and o.get("used"):
+            count[o["e"]] = count.get(o["e"], 0) + 1
+            o["sem"], o["n"], o["inc"] = "c" + o["e"], count[o["e"]], 1
+    for o in ops:
+        if o["e"] is None:
+            continue
+        q = queue[o["e"]]
+        for d in o["waits"]:
+            q.wait_ge(T.sem[ops[d]["sem"]], ops[d]["n"])
+        if o["f"] is not None:
+            ins = o["f"](q)
+            if o.get("inc"):
+                ins.then_inc(T.sem[o["sem"]], o["inc"])
+
+
+def rank_program(g, core, T, topo):
+    rank = T.rank_of(core)
+    if rank is None:
+        return
+    n_ranks = len(T.cores)
+    dst = T.cores[(rank - 1) % n_ranks]
+    src = T.cores[(rank + 1) % n_ranks]
+    rid, pid = topo.addr(dst, core)
+    mask_out, n_out, n_in = topo.mask(core, dst), len(topo.engines(core, dst)), len(topo.engines(src, core))
+    ops, nd, nr, ends = [], [0], [0], []
+
+    def op(e, f, r, w):
+        ops.append({"e": e, "f": f, "r": list(r), "w": list(w), "src": e, "sem": None})
+
+    def dma(e, out, in_, r, w):
+        s = "d%d" % nd[0]
+        nd[0] += 1
+        ops.append({"e": e, "f": lambda q: q.dma_start(out, in_), "r": list(r), "w": list(w) + [s], "src": s, "sem": s, "n": 16, "inc": 16})
+        ends.append(s)
+
+    def send(out, in_, r, w):
+        i = nr[0]
+        nr[0] += 1
+        ls, rs = "l%d" % i, "r%d" % i
+        ops.append({"e": "g", "f": lambda q: q.remote_dma(out, in_, T.sem[rs], T.sem[ls], pid, rid, mask_out),
+                    "r": list(r), "w": [ls], "src": ls, "sem": ls, "n": n_out})
+        ops.append({"e": None, "f": None, "r": [], "w": list(w), "src": rs, "sem": rs, "n": n_in})
+        ends.append(ls)
+
+    def ts(out, in0, s1, op0, s2, op1, r, w):
+        if op1 is None:
+            op("v", lambda q: q.tensor_scalar(out, in0, s1, None, op0), r, w)
+        else:
+            op("v", lambda q: q.tensor_scalar(out, in0, s1, s2, op0, op1), r, w)
+
+    def tt(out, in0, in1, o, r, w):
+        op("v", lambda q: q.tensor_tensor(out, in0, in1, o), r, w)
+
+    def cp(out, in_, r, w):
+        op("v", lambda q: q.tensor_copy(out, in_), r, w)
+
+    def fill(out, c, w):
+        op("v", lambda q: q.memset(out, c), [], w)
+
+    def scan(out, d0, d1, first, op0, op1, r, w):
+        op("v", lambda q: q.tensor_tensor_scan(out, d0, d1, first, op0, op1), r, w)
+
+    def quant(qb, sb, in_, r, w):
+        op("v", lambda q: q.quantize_mx(qb, sb, in_), r, w)
+
+    def act(out, in_, r, w, func=F.Identity, **kw):
+        op("a", lambda q: q.activation(out, in_, func, **kw), r, w)
+
+    def iota(out, pattern, base, mult, w, whole=False):
+        if whole:
+            op("g", lambda q: q.iota(out, pattern, base, mult), [], w)
+        else:
+            op("g", lambda q: q.iota(out, pattern, base, mult, allow_small_or_imprecise_dtypes=True), [], w)
+
+    def bank(b, n, first=0):
+        return T.ps[:, 512 * b + first:512 * b + n]
+
+    def mm(b, n, lq, ls, rq, rs, r):
+        op("t", lambda q: q.matmul_mx(bank(b, n), lq, ls, rq, rs, True, True), r, ["b%d" % b])
+
+    col = lambda i: T.col[:, i:i + 1]
+    QC, GC, SC, PW0, PW, PH, CB4, CR4, CB16, CR16, MQ = range(11)
+    u8 = dt.uint8
+
+    dma("s", T.xin[:, 0:4 * H], T.x[:, 0:4 * H], [], ["x0h0"])
+    dma("a", T.ut[:], T.u[:], [], ["ut"])
+    dma("s", T.xin[:, 4 * H:4 * C], T.x[:, 4 * H:4 * C], [], ["x0h1"])
+    dma("s", T.wq[:].bitcast(u8), T.wc[:], [], ["wq"])
+    dma("s", T.wp[:], T.ws[:], [], ["wp"])
+    dma("s", T.vt[:], T.v[:], [], ["vt"])
+
+    iota(T.pi[:, 0:1], [[0, 1]], 0, 1, ["pi0"], whole=True)
+    iota(T.r16[:], [[1, 16]], 0, 0, ["r16"])
+    iota(T.gm[:], [[1, 8], [0, 4]], 0, 0, ["gm"])
+    iota(T.c16[:], [[16, K]], 0, 0, ["c16"])
+    iota(T.t4[:], [[0, 2 * K], [int(2 * B4), 4]], 0, 0, ["t4"])
+    iota(T.ramp[:], [[1, SLOTS]], 0, 0, ["ramp"])
+    iota(T.t16[:], [[0, K], [S16, 16]], 0, 0, ["t16"])
+    act(T.tab0[:, FB:FB + SLOTS], T.ramp[:], ["ramp"], ["tabF0"], scale=0.0, bias=EMPTY)
+    act(T.tab0[:, GB:GB + SLOTS], T.ramp[:], ["ramp"], ["tabG0"], scale=0.0, bias=EMPTY)
+    act(T.ones[:], T.ramp[:, 0:512], ["ramp"], ["ones"], scale=0.0, bias=1.0)
+    fill(T.kt[:], 0.0, ["kt"])
+    fill(T.bits[:, H:512], 0.0, ["bits1"])
+    ts(T.pi[:, 1:2], T.pi[:, 0:1], 15, A.bitwise_and, None, None, ["pi0"], ["pi1"])
+    ts(T.pi[:, 2:3], T.pi[:, 0:1], 4, A.arith_shift_right, None, None, ["pi0"], ["pi2"])
+    ts(T.pi[:, 3:4], T.pi[:, 0:1], 2, A.arith_shift_right, 3, A.bitwise_and, ["pi0"], ["pi3"])
+    cp(T.col[:, 0:3], T.pi[:, 1:4], ["pi1", "pi2", "pi3"], ["col"])
+    ts(T.k16[:], T.r16[:], col(QC), A.is_lt, 1.0, A.add, ["r16", "col"], ["k16"])
+    ts(col(PH), col(QC), 10.0, A.is_equal, 512.0, A.mult, ["col"], ["ph"])
+    op("v", lambda q: q.tensor_reduce(col(PW0), T.k16[:], AxisListType.X, A.mult), ["k16"], ["pw0"])
+    for r in range(4):
+        ts(T.kt[:, 512 + 5 * r:1024:16], T.gm[:], col(GC), A.is_equal, col(PH), A.mult, ["gm", "col", "ph", "kt"], ["kh%d" % r])
+    ts(col(PW), col(QC), 10.0, A.is_lt, col(PW0), A.mult, ["col", "pw0"], ["pw"])
+    ts(col(CB4), col(SC), -2 * B4, A.mult, B4, A.add, ["col"], ["cb4"])
+    ts(col(CR4), col(SC), B4, A.mult, -5 * B4, A.add, ["col"], ["cr4"])
+    for r in range(4):
+        ts(T.kt[:, 5 * r:512:16], T.gm[:], col(GC), A.is_equal, col(PW), A.mult, ["gm", "col", "pw", "kt"], ["ka%d" % r])
+    ts(T.jw[:], T.c16[:], col(QC), A.add, None, None, ["c16", "col"], ["jw"])
+    ts(T.d4[:], T.t4[:], col(CB4), A.add, B4, A.min, ["t4", "cb4"], ["d4"])
+    quant(T.kq[:], T.ks[:], T.kt[:], ["ka%d" % r for r in range(4)] + ["kh%d" % r for r in range(4)], ["kq"])
+    ts(T.d4[:, 3::4], T.d4[:, 3::4], col(CR4), A.add, None, None, ["cr4"], ["d4"])
+    ts(T.jn[:], T.jw[:], -1.0, A.mult, B4 + B16 + SLOTS, A.add, ["jw"], ["jn"])
+    tt(T.d4[:, 4 * K + 3::4], T.d4[:, 4 * K + 3::4], T.jw[:], A.add, ["jw"], ["d4"])
+    quant(T.uq[:], T.us[:], T.ut[:], ["ut"], ["uq"])
+
+    def late_constants():
+        ts(col(MQ), col(QC), float(TAIL - 16), A.add, None, None, ["col"], ["mq"])
+        ts(col(CB16), col(QC), -float(S16), A.mult, B16, A.add, ["col"], ["cb16"])
+        ts(col(CR16), col(QC), B16, A.mult, -17 * B16, A.add, ["col"], ["cr16"])
+        ts(T.mtmp[:], T.ramp[:, 0:TAIL], col(MQ), A.is_equal, MUL - 1.0, A.mult, ["ramp", "mq"], ["mtmp"])
+        ts(T.d16[:], T.t16[:], col(CB16), A.add, B16, A.min, ["t16", "cb16"], ["d16"])
+        ts(T.mask[:], T.mtmp[:], 1.0, A.add, None, None, ["mtmp"], ["mask"])
+        ts(T.d16[:, 15::16], T.d16[:, 15::16], col(CR16), A.add, None, None, ["cr16"], ["d16"])
+        fill(T.dn[:, C::DW], 0.0, ["dzero"])
+        fill(T.acc[:, 0:TAIL // 16], 0.0, ["acc0"])
+
+    def unit_tile(b):
+        op("g", lambda q: q.affine_select(T.et[:, 512 * b:512 * (b + 1)], T.ones[:], [[1, 512]], A.is_equal, 0.0, -b, -4), ["ones"], ["e%d" % b])
+
+    state = [T.xin, T.xa, T.xb]
+
+    def quant_state(t, h):
+        quant(T["xq%d" % t][:, H * h:H * (h + 1)], T["xs%d" % t][:, H * h:H * (h + 1)], state[t][:, 4 * H * h:4 * H * (h + 1)],
+              ["x%dh%d" % (t, h)] + ["x%dh%db%d" % (t, h, b) for b in range(4)], ["xq%dh%d" % (t, h)])
+
+    def scores(t, h):
+        cols = slice(H * h, H * (h + 1))
+        mm(h, H, T.uq[:], T.us[:], T["xq%d" % t][:, cols], T["xs%d" % t][:, cols], ["uq", "xq%dh%d" % (t, h)])
+
+    def signs(h, on_scalar):
+        if on_scalar:
+            act(T.sign[:], bank(h, H), [], ["b%d" % h, "sign"], func=F.Sign, scale=-1.0)
+            act(T.bits[:, H * h:H * (h + 1)], T.sign[:], ["sign"], ["bits%d" % h], func=F.Relu)
+        else:
+            ts(T.bits[:, H * h:H * (h + 1)], bank(h, H), 0.0, A.is_lt, None, None, [], ["b%d" % h, "bits%d" % h])
+
+    def weigh(h):
+        bq, bs = T["bq%d" % h], T["bs%d" % h]
+        quant(bq[:], bs[:], T.bits[:], ["bits0", "bits1"], ["bq%d" % h])
+        for i in range(h + 1):
+            mm(6 + i, 128, T.kq[:, 128 * i:128 * (i + 1)], T.ks[:, 128 * i:128 * (i + 1)], bq[:], bs[:], ["kq", "bq%d" % h])
+
+    def post(t, h):
+        msg, key, w = T["msg%d" % t], T["key%d" % t], 4 * KH
+        scan(T.z4[:, w * h:w * (h + 1)], bank(6, w * (h + 1), w * h), T.d4[:, w * h:w * (h + 1)], 0.0, A.max, A.add, ["d4"], ["b6", "za%d" % h])
+        if h == 0:
+            ts(msg[:, 0:KH], T.z4[:, 3:w:4], B4, A.add, None, None, ["za0"], ["msg%d0" % t])
+            send(key[:, 0:KH], msg[:, 0:KH], ["msg%d0" % t], ["key%d0" % t])
+        else:
+            scan(T.z4[:, 4 * K:8 * K], bank(7, 4 * K), T.d4[:, 4 * K:8 * K], 0.0, A.max, A.add, ["d4"], ["b7", "zv"])
+            ts(msg[:, KH:2 * K], T.z4[:, w + 3::4], B4, A.add, None, None, ["za1", "zv"], ["msg%d1" % t])
+            send(key[:, KH:2 * K], msg[:, KH:2 * K], ["msg%d1" % t], ["key%d1" % t])
+
+    quant_state(0, 0)
+    scores(0, 0)
+    signs(0, False)
+    weigh(0)
+    post(0, 0)
+    quant_state(0, 1)
+
+    for t in range(2):
+        xq, xs = T["xq%d" % t], T["xs%d" % t]
+        msg, key, tab = T["msg%d" % t], T["key%d" % t], T["tab%d" % t]
+        pq, pp, lq, lp = T["pq%d" % t], T["pp%d" % t], T["lq%d" % t], T["lp%d" % t]
+        both = ["xq%dh0" % t, "xq%dh1" % t]
+
+        def layer(b):
+            mm(2 + b, C, T.wq[:, 128 * b:128 * (b + 1)], T.wp[:, 128 * b:128 * (b + 1)], xq[:], xs[:], both + ["wq", "wp"])
+            act(T.pt[:, b::4], bank(2 + b, C), [], ["b%d" % (2 + b), "p%d" % b], scale=0.03125)
+
+        scores(t, 1)
+        if t > 0:
+            layer(0)
+        signs(1, False)
+        weigh(1)
+        for b in range(1 if t > 0 else 0, 4):
+            layer(b)
+        post(t, 1)
+
+        za, zv = T.z4[:, 3:4 * K:4], T.z4[:, 4 * K + 3::4]
+        ts(T.qi[:, 0:K], za, B4 + 1.0, A.add, None, None, ["za0", "za1"], ["qi0"])
+        ts(T.qi[:, K:2 * K], za, B4 + SLOTS - 1.0, A.add, None, None, ["za0", "za1"], ["qi1"])
+        tt(T.hb[:], zv, T.jn[:], A.add, ["zv", "jn"], ["hb"])
+        ts(T.qj[:], T.qi[:], SLOTS - 1, A.bitwise_and, None, None, ["qi0", "qi1"], ["qj"])
+        if t == 0:
+            late_constants()
+            unit_tile(0)
+            unit_tile(1)
+        else:
+            quant(T.vq[:], T.vs[:], T.vt[:], ["vt"], ["vq"])
+        cp(T.qo[:], T.qj[:], ["qj"], ["qo"])
+
+        for h in range(2):
+            kk, lists = "key%d%d" % (t, h), slice(KH * h, KH * (h + 1))
+            rows = range(KH * h, KH * (h + 1))
+            cp(T.rep[:, H * h:H * (h + 1)], T.ramp[:].indirect(key[:, lists]), ["ramp", kk], ["rep%d" % h])
+            cp(T.af[:, lists], key[:, lists], [kk], ["af%d" % h])
+            if h == 1:
+                act(T.val[:], T.ramp[:].indirect(key[:, K:2 * K]), ["ramp", kk], ["val"])
+            for c in reversed(rows):
+                ts(T.cmp[:, OFF[c]:OFF[c] + ROW[c]], T.rep[:, 0:ROW[c]], T.af[:, c:c + 1], A.is_equal, EPS, A.mult,
+                   ["rep%d" % i for i in range(h + 1)] + ["af%d" % h], ["ch%d" % c, "ct%d" % c])
+                if ROW[c] > TAIL:
+                    head = T.cmp[:, OFF[c]:OFF[c] + ROW[c] - TAIL]
+                    act(head, head, [], ["ch%d" % c, "acc%d" % c], scale=MUL, accum_out=T.acc[:, c:c + 1])
+            if h == 0:
+                quant(pq[:], pp[:], T.pt[:], ["p0", "p1", "p2", "p3"], ["pq%d" % t])
+                send(lq[:].bitcast(u8), pq[:].bitcast(u8), ["pq%d" % t], ["lq%d" % t])
+                send(lp[:], pp[:], ["pq%d" % t], ["lp%d" % t])
+                if t == 0:
+                    unit_tile(2)
+                    unit_tile(3)
+                    iota(T.tab1[:, FB:FB + SLOTS], [[0, SLOTS]], int(EMPTY), 0, ["tabF1"])
+            else:
+                ts(T.ab[:], T.af[:], float(FB), A.add, None, None, ["af0", "af1"], ["ab"])
+            for c in reversed(rows):
+                n = min(ROW[c], TAIL)
+                end = OFF[c] + ROW[c]
+                if c == KH:
+                    tt(T.s0[:], T.acc[:], T.ab[:], A.add, ["ab", "acc0"] + ["acc%d" % i for i in range(TAIL // 16, K)], ["s0"])
+                scan(T.zs[:, TAIL * (c + 1) - n:TAIL * (c + 1)], T.mask[:, TAIL - n:TAIL], T.cmp[:, end - n:end], 0.0, A.mult, A.add,
+                     ["mask", "ct%d" % c], ["zs%d" % c])
+        if t == 0:
+            act(T.tab1[:, GB:GB + SLOTS], T.ramp[:], ["ramp"], ["tabG1"], scale=0.0, bias=EMPTY)
+        tt(T.s1[:], T.zs[:, TAIL - 1::TAIL], T.s0[:], A.add, ["s0"] + ["zs%d" % c for c in range(K)], ["s1"])
+        tt(T.s2[:], T.s1[:], T.jw[:], A.max, ["s1", "jw"], ["s2"])
+        cp(T.so[:], T.s2[:], ["s2"], ["so"])
+        cp(tab[:].indirect(T.so[:]), T.val[:], ["so", "val"], ["tabF%d" % t, "tabG%d" % t])
+        if t == 0:
+            quant(T.eq4[:], T.es[:], T.et[:], ["e0", "e1", "e2", "e3"], ["eq4"])
+
+        wf, wg = tab[:, FB:FB + SLOTS], tab[:, GB:GB + SLOTS]
+        kf, kg, mk = "tabF%d" % t, "tabG%d" % t, ["msg%d0" % t, "msg%d1" % t]
+        for h in range(2):
+            act(T.tf[:, H * h:H * (h + 1)], wf.indirect(msg[:, KH * h:KH * (h + 1)]), [kf] + mk, ["tf0%d" % h], bias=float(SLOTS))
+        act(T.tf[:, C:2 * C], wf.indirect(T.qo[:, 0:K]), [kf, "qo"], ["tf1"], bias=float(SLOTS))
+        for b in range(4):
+            mm(2 + b, C, T.eq4[:, 128 * b:128 * (b + 1)], T.es[:, 128 * b:128 * (b + 1)], lq[:], lp[:], ["eq4", "lq%d" % t, "lp%d" % t])
+            act(T.dn[:, DW * b:DW * b + C], bank(2 + b, C), [], ["b%d" % (2 + b), "dn%d" % b])
+        for h in range(2):
+            tt(T.look[:, H * h:H * (h + 1)], wg.indirect(T.qo[:, K + KH * h:K + KH * (h + 1)]), T.tf[:, H * h:H * (h + 1)], A.max,
+               [kg, "qo", "tf0%d" % h], ["lk0%d" % h])
+        scan(T.z16[:, 0:C], T.look[:, 0:C], T.d16[:], -B16, A.max, A.add, ["lk00", "lk01", "d16"], ["z160"])
+        tt(T.look[:, C:2 * C], wg.indirect(msg[:, 0:K]), T.tf[:, C:2 * C], A.max, [kg, "tf1"] + mk, ["lk1"])
+        tt(T.x1[:, 0:K], T.z16[:, 15:C:16], T.hb[:], A.add, ["z160", "hb"], ["x10"])
+        scan(T.z16[:, C:2 * C], T.look[:, C:2 * C], T.d16[:], -B16, A.max, A.add, ["lk1", "d16"], ["z161"])
+        ts(T.x2[:, 0:K], T.x1[:, 0:K], SLOTS - 1, A.bitwise_and, None, None, ["x10"], ["x20"])
+        tt(T.x1[:, K:2 * K], T.z16[:, C + 15::16], T.hb[:], A.add, ["z161", "hb"], ["x11"])
+        ts(T.x3[:], T.x2[:, 0:K], float(C), A.is_lt, 4096.0, A.mult, ["x20"], ["x3"])
+        ts(T.x2[:, K:2 * K], T.x1[:, K:2 * K], SLOTS - 1, A.bitwise_and, None, None, ["x11"], ["x21"])
+        tt(T.x4[:], T.x2[:, K:2 * K], T.x3[:], A.max, ["x21", "x3"], ["x4"])
+        tt(T.x5[:], T.x2[:, 0:K], T.x4[:], A.min, ["x20", "x4"], ["x5"])
+        ts(T.fin[:], T.x5[:], float(C), A.min, None, None, ["x5"], ["fin"])
+
+        def add(h, b):
+            lo, hi = 4 * H * h + b, 4 * H * (h + 1)
+            tt(state[t + 1][:, lo:hi:4], T.dn[:, DW * b:DW * b + C + 1].indirect(T.fin[:, KH * h:KH * (h + 1)]), T.pt[:, lo:hi:4], A.add,
+               ["dn%d" % b, "dzero", "fin", "p%d" % b], ["x%dh%db%d" % (t + 1, h, b)])
+
+        def store(h):
+            cols = slice(H * h, H * (h + 1))
+            dma("s", T.oc[:, 4 * H * h:4 * H * (h + 1)], T.xq2[:, cols].bitcast(u8), ["xq2h%d" % h], [])
+            mm(h, H, T.vq[:], T.vs[:], T.xq2[:, cols], T.xs2[:, cols], ["vq", "xq2h%d" % h])
+            act(T.yo[:, cols], bank(h, H), [], ["b%d" % h, "yo%d" % h])
+            dma("a", T.y[:, cols], T.yo[:, cols], ["yo%d" % h], [])
+
+        for b in range(4):
+            add(0, b)
+        quant_state(t + 1, 0)
+        if t == 0:
+            scores(1, 0)
+            signs(0, True)
+            add(1, 0)
+            add(1, 1)
+            weigh(0)
+            add(1, 2)
+            post(1, 0)
+            add(1, 3)
+            quant_state(1, 1)
+        else:
+            store(0)
+            for b in range(4):
+                add(1, b)
+            quant_state(2, 1)
+            store(1)
+    for k in range(4):
+        dma("s", T.osc[4 * k:4 * k + 4, :], T.xs2[32 * k:32 * k + 4, :], ["xq2h0", "xq2h1"], [])
+    op("g", None, ends, [])
+    schedule(g, T, ops)

@@ -1,6 +1,8 @@
 from concourse.mybir import dt, AluOpType as A, AxisListType, ActivationFunctionType as F
 
-C, H, K, KH = 448, 224, 28, 14
+C, K = 448, 28
+KC = [0, 18, K]
+CC = [16 * k for k in KC]
 SLOTS = 1024
 DW = 464
 GB, FB = 512, 2048
@@ -8,10 +10,13 @@ STEP = FB - GB
 EPS = 2.0 ** -10
 MUL = -STEP / EPS
 EMPTY = -1025.0
+SPREAD = 0.016
 B4, B16, S16 = 2048.0, 2000.0, 4096
-TAIL = 128
+TAIL = 160
 ROW = [16 * (c + 1) for c in range(K)]
+OWN = [min(ROW[c], 128 if c < KC[1] else TAIL) for c in range(K)]
 OFF = [sum(ROW[:c]) for c in range(K)]
+AHEAD = {25: 24, 23: 21, 20: 18, 15: 14, 13: 11, 10: 8}
 HALF = "float16"
 Q4 = "float8_e4m3fn_x4"
 
@@ -24,21 +29,22 @@ SCRATCH = {
     "ones": ("sbuf", [128, 512], "bfloat16"),
     "et": ("sbuf", [128, 2048], "bfloat16"), "eq4": ("sbuf", [128, 512], Q4), "es": ("sbuf", [128, 512], "uint8"),
     "kt": ("sbuf", [128, 1024], "bfloat16"), "kq": ("sbuf", [128, 256], Q4), "ks": ("sbuf", [128, 256], "uint8"),
-    "sign": ("sbuf", [128, H], "bfloat16"), "bits": ("sbuf", [128, 512], "bfloat16"),
+    "sign": ("sbuf", [128, CC[1]], "bfloat16"), "bits": ("sbuf", [128, 512], "bfloat16"),
     "bq0": ("sbuf", [128, 128], Q4), "bs0": ("sbuf", [128, 128], "uint8"),
     "bq1": ("sbuf", [128, 128], Q4), "bs1": ("sbuf", [128, 128], "uint8"),
     "pt": ("sbuf", [128, 4 * C], "bfloat16"), "dn": ("sbuf", [128, 4 * DW], "bfloat16"),
     "ps": ("psum", [128, 4096], "float32"),
     "pi": ("sbuf", [128, 8], "int32"), "col": ("sbuf", [128, 16], "float32"), "k16": ("sbuf", [128, 16], "float32"),
     "gm": ("sbuf", [128, 32], "float32"), "r16": ("sbuf", [128, 16], "float32"), "c16": ("sbuf", [128, K], "float32"),
-    "t4": ("sbuf", [128, 8 * K], "float32"), "d4": ("sbuf", [128, 8 * K], "float32"),
-    "t16": ("sbuf", [128, C], "bfloat16"), "d16": ("sbuf", [128, C], HALF),
-    "ramp": ("sbuf", [128, SLOTS], "float32"), "jw": ("sbuf", [128, K], "float32"), "jn": ("sbuf", [128, K], "float32"),
+    "t4": ("sbuf", [128, 4 * K], "float32"), "d4": ("sbuf", [128, 8 * K], "float32"),
+    "t16": ("sbuf", [128, CC[1]], "bfloat16"), "d16": ("sbuf", [128, CC[1]], HALF),
+    "ramp": ("sbuf", [128, SLOTS], "float32"), "enc": ("sbuf", [128, SLOTS], "bfloat16"),
+    "jw": ("sbuf", [128, K], "float32"), "jn": ("sbuf", [128, K], "float32"), "jc": ("sbuf", [128, K], "float32"),
     "mtmp": ("sbuf", [128, TAIL], "float32"), "mask": ("sbuf", [128, TAIL], "bfloat16"),
     "z4": ("sbuf", [128, 8 * K], "float32"), "qi": ("sbuf", [128, 2 * K], "int32"), "qj": ("sbuf", [128, 2 * K], "int32"),
     "qo": ("sbuf", [128, 2 * K], "uint16"), "hb": ("sbuf", [128, K], "float32"),
-    "af": ("sbuf", [128, K], "float32"), "ab": ("sbuf", [128, K], "float32"),
-    "rep": ("sbuf", [128, C], "uint16"), "val": ("sbuf", [128, C], "float32"),
+    "af": ("sbuf", [128, K], "float32"), "ae": ("sbuf", [128, K], "bfloat16"), "ab": ("sbuf", [128, K], "float32"),
+    "rep": ("sbuf", [128, C], "bfloat16"), "val": ("sbuf", [128, C], "float32"),
     "cmp": ("sbuf", [128, sum(ROW)], "bfloat16"), "zs": ("sbuf", [128, K * TAIL], "bfloat16"), "acc": ("sbuf", [128, K], "float32"),
     "s0": ("sbuf", [128, K], "float32"), "s1": ("sbuf", [128, K], "float32"), "s2": ("sbuf", [128, K], "float32"),
     "so": ("sbuf", [128, K], "uint16"),
@@ -59,8 +65,8 @@ for _t in range(2):
     SCRATCH["key%d" % _t] = ("sbuf", [128, 2 * K], "uint16")
     SCRATCH["tab%d" % _t] = ("sbuf", [128, FB + SLOTS], "float32")
 
-SEMAPHORES = (["cv", "ca", "ct", "cg"] + ["d%d" % i for i in range(20)] + ["l%d" % i for i in range(8)]
-              + ["r%d" % i for i in range(8)])
+SEMAPHORES = (["cv", "ca", "ct", "cg"] + ["d%d" % i for i in range(20)] + ["l%d" % i for i in range(10)]
+              + ["r%d" % i for i in range(10)])
 
 
 def schedule(g, T, ops):
@@ -178,10 +184,15 @@ def rank_program(g, core, T, topo):
     col = lambda i: T.col[:, i:i + 1]
     QC, GC, SC, PW0, PW, PH, CB4, CR4, CB16, CR16, MQ = range(11)
     u8 = dt.uint8
+    cols = [slice(CC[h], CC[h + 1]) for h in range(2)]
+    wide = [slice(4 * CC[h], 4 * CC[h + 1]) for h in range(2)]
+    lists = [slice(KC[h], KC[h + 1]) for h in range(2)]
+    nc = [CC[h + 1] - CC[h] for h in range(2)]
+    nk = [KC[h + 1] - KC[h] for h in range(2)]
 
-    dma("s", T.xin[:, 0:4 * H], T.x[:, 0:4 * H], [], ["x0h0"])
+    dma("s", T.xin[:, wide[0]], T.x[:, wide[0]], [], ["x0h0"])
     dma("a", T.ut[:], T.u[:], [], ["ut"])
-    dma("s", T.xin[:, 4 * H:4 * C], T.x[:, 4 * H:4 * C], [], ["x0h1"])
+    dma("s", T.xin[:, wide[1]], T.x[:, wide[1]], [], ["x0h1"])
     dma("s", T.wq[:].bitcast(u8), T.wc[:], [], ["wq"])
     dma("s", T.wp[:], T.ws[:], [], ["wp"])
     dma("s", T.vt[:], T.v[:], [], ["vt"])
@@ -189,47 +200,58 @@ def rank_program(g, core, T, topo):
     iota(T.pi[:, 0:1], [[0, 1]], 0, 1, ["pi0"], whole=True)
     iota(T.r16[:], [[1, 16]], 0, 0, ["r16"])
     iota(T.gm[:], [[1, 8], [0, 4]], 0, 0, ["gm"])
+    iota(T.t4[:], [[0, K], [int(2 * B4), 4]], 0, 0, ["t4"])
     iota(T.c16[:], [[16, K]], 0, 0, ["c16"])
-    iota(T.t4[:], [[0, 2 * K], [int(2 * B4), 4]], 0, 0, ["t4"])
     iota(T.ramp[:], [[1, SLOTS]], 0, 0, ["ramp"])
-    iota(T.t16[:], [[0, K], [S16, 16]], 0, 0, ["t16"])
-    act(T.tab0[:, FB:FB + SLOTS], T.ramp[:], ["ramp"], ["tabF0"], scale=0.0, bias=EMPTY)
-    act(T.tab0[:, GB:GB + SLOTS], T.ramp[:], ["ramp"], ["tabG0"], scale=0.0, bias=EMPTY)
+    act(T.enc[:], T.ramp[:], ["ramp"], ["enc"], func=F.Exp, scale=SPREAD)
     act(T.ones[:], T.ramp[:, 0:512], ["ramp"], ["ones"], scale=0.0, bias=1.0)
     fill(T.kt[:], 0.0, ["kt"])
-    fill(T.bits[:, H:512], 0.0, ["bits1"])
     ts(T.pi[:, 1:2], T.pi[:, 0:1], 15, A.bitwise_and, None, None, ["pi0"], ["pi1"])
     ts(T.pi[:, 2:3], T.pi[:, 0:1], 4, A.arith_shift_right, None, None, ["pi0"], ["pi2"])
     ts(T.pi[:, 3:4], T.pi[:, 0:1], 2, A.arith_shift_right, 3, A.bitwise_and, ["pi0"], ["pi3"])
+    fill(T.bits[:, CC[1]:512], 0.0, ["bits1"])
     cp(T.col[:, 0:3], T.pi[:, 1:4], ["pi1", "pi2", "pi3"], ["col"])
     ts(T.k16[:], T.r16[:], col(QC), A.is_lt, 1.0, A.add, ["r16", "col"], ["k16"])
-    ts(col(PH), col(QC), 10.0, A.is_equal, 512.0, A.mult, ["col"], ["ph"])
-    op("v", lambda q: q.tensor_reduce(col(PW0), T.k16[:], AxisListType.X, A.mult), ["k16"], ["pw0"])
-    for r in range(4):
-        ts(T.kt[:, 512 + 5 * r:1024:16], T.gm[:], col(GC), A.is_equal, col(PH), A.mult, ["gm", "col", "ph", "kt"], ["kh%d" % r])
-    ts(col(PW), col(QC), 10.0, A.is_lt, col(PW0), A.mult, ["col", "pw0"], ["pw"])
     ts(col(CB4), col(SC), -2 * B4, A.mult, B4, A.add, ["col"], ["cb4"])
+    op("v", lambda q: q.tensor_reduce(col(PW0), T.k16[:], AxisListType.X, A.mult), ["k16"], ["pw0"])
     ts(col(CR4), col(SC), B4, A.mult, -5 * B4, A.add, ["col"], ["cr4"])
+    ts(col(PW), col(QC), 10.0, A.is_lt, col(PW0), A.mult, ["col", "pw0"], ["pw"])
+    ts(T.d4[:, 0:4 * K], T.t4[:], col(CB4), A.add, B4, A.min, ["t4", "cb4"], ["d4a"])
     for r in range(4):
         ts(T.kt[:, 5 * r:512:16], T.gm[:], col(GC), A.is_equal, col(PW), A.mult, ["gm", "col", "pw", "kt"], ["ka%d" % r])
-    ts(T.jw[:], T.c16[:], col(QC), A.add, None, None, ["c16", "col"], ["jw"])
-    ts(T.d4[:], T.t4[:], col(CB4), A.add, B4, A.min, ["t4", "cb4"], ["d4"])
-    quant(T.kq[:], T.ks[:], T.kt[:], ["ka%d" % r for r in range(4)] + ["kh%d" % r for r in range(4)], ["kq"])
-    ts(T.d4[:, 3::4], T.d4[:, 3::4], col(CR4), A.add, None, None, ["cr4"], ["d4"])
-    ts(T.jn[:], T.jw[:], -1.0, A.mult, B4 + B16 + SLOTS, A.add, ["jw"], ["jn"])
-    tt(T.d4[:, 4 * K + 3::4], T.d4[:, 4 * K + 3::4], T.jw[:], A.add, ["jw"], ["d4"])
+    ts(T.d4[:, 3:4 * K:4], T.d4[:, 3:4 * K:4], col(CR4), A.add, None, None, ["cr4"], ["d4a"])
+    quant(T.kq[:, 0:128], T.ks[:, 0:128], T.kt[:, 0:512], ["ka%d" % r for r in range(4)], ["kq0"])
     quant(T.uq[:], T.us[:], T.ut[:], ["ut"], ["uq"])
 
-    def late_constants():
-        ts(col(MQ), col(QC), float(TAIL - 16), A.add, None, None, ["col"], ["mq"])
-        ts(col(CB16), col(QC), -float(S16), A.mult, B16, A.add, ["col"], ["cb16"])
-        ts(col(CR16), col(QC), B16, A.mult, -17 * B16, A.add, ["col"], ["cr16"])
-        ts(T.mtmp[:], T.ramp[:, 0:TAIL], col(MQ), A.is_equal, MUL - 1.0, A.mult, ["ramp", "mq"], ["mtmp"])
-        ts(T.d16[:], T.t16[:], col(CB16), A.add, B16, A.min, ["t16", "cb16"], ["d16"])
-        ts(T.mask[:], T.mtmp[:], 1.0, A.add, None, None, ["mtmp"], ["mask"])
-        ts(T.d16[:, 15::16], T.d16[:, 15::16], col(CR16), A.add, None, None, ["cr16"], ["d16"])
-        fill(T.dn[:, C::DW], 0.0, ["dzero"])
-        fill(T.acc[:, 0:TAIL // 16], 0.0, ["acc0"])
+    def constants(i):
+        if i == 0:
+            ts(col(PH), col(QC), 10.0, A.is_equal, 512.0, A.mult, ["col"], ["ph"])
+            ts(T.jw[:], T.c16[:], col(QC), A.add, None, None, ["c16", "col"], ["jw"])
+            ts(T.d4[:, 4 * K:8 * K], T.t4[:], col(CB4), A.add, B4, A.min, ["t4", "cb4"], ["d4v"])
+        elif i == 1:
+            ts(T.jc[:], T.jw[:], col(CR4), A.add, None, None, ["jw", "cr4"], ["jc"])
+            for r in range(2):
+                ts(T.kt[:, 512 + 5 * r:1024:16], T.gm[:], col(GC), A.is_equal, col(PH), A.mult, ["gm", "col", "ph", "kt"], ["kh%d" % r])
+        elif i == 2:
+            for r in range(2, 4):
+                ts(T.kt[:, 512 + 5 * r:1024:16], T.gm[:], col(GC), A.is_equal, col(PH), A.mult, ["gm", "col", "ph", "kt"], ["kh%d" % r])
+            tt(T.d4[:, 4 * K + 3::4], T.d4[:, 4 * K + 3::4], T.jc[:], A.add, ["jc"], ["d4v"])
+        elif i == 3:
+            quant(T.kq[:, 128:256], T.ks[:, 128:256], T.kt[:, 512:1024], ["kh%d" % r for r in range(4)], ["kq1"])
+        elif i == 4:
+            ts(T.jn[:], T.jw[:], -1.0, A.mult, B4 + B16 + SLOTS, A.add, ["jw"], ["jn"])
+            ts(col(MQ), col(QC), float(TAIL - 16), A.add, None, None, ["col"], ["mq"])
+            ts(col(CB16), col(QC), -float(S16), A.mult, B16, A.add, ["col"], ["cb16"])
+        elif i == 5:
+            ts(col(CR16), col(QC), B16, A.mult, -17 * B16, A.add, ["col"], ["cr16"])
+            fill(T.dn[:, C::DW], 0.0, ["dzero"])
+        elif i == 6:
+            fill(T.acc[:, 0:8], 0.0, ["acc0"])
+            ts(T.mtmp[:], T.ramp[:, 0:TAIL], col(MQ), A.is_equal, MUL - 1.0, A.mult, ["ramp", "mq"], ["mtmp"])
+        else:
+            ts(T.d16[:], T.t16[:], col(CB16), A.add, B16, A.min, ["t16", "cb16"], ["d16"])
+            ts(T.mask[:], T.mtmp[:], 1.0, A.add, None, None, ["mtmp"], ["mask"])
+            ts(T.d16[:, 15::16], T.d16[:, 15::16], col(CR16), A.add, None, None, ["cr16"], ["d16"])
 
     def unit_tile(b):
         op("g", lambda q: q.affine_select(T.et[:, 512 * b:512 * (b + 1)], T.ones[:], [[1, 512]], A.is_equal, 0.0, -b, -4), ["ones"], ["e%d" % b])
@@ -237,104 +259,133 @@ def rank_program(g, core, T, topo):
     state = [T.xin, T.xa, T.xb]
 
     def quant_state(t, h):
-        quant(T["xq%d" % t][:, H * h:H * (h + 1)], T["xs%d" % t][:, H * h:H * (h + 1)], state[t][:, 4 * H * h:4 * H * (h + 1)],
+        quant(T["xq%d" % t][:, cols[h]], T["xs%d" % t][:, cols[h]], state[t][:, wide[h]],
               ["x%dh%d" % (t, h)] + ["x%dh%db%d" % (t, h, b) for b in range(4)], ["xq%dh%d" % (t, h)])
 
     def scores(t, h):
-        cols = slice(H * h, H * (h + 1))
-        mm(h, H, T.uq[:], T.us[:], T["xq%d" % t][:, cols], T["xs%d" % t][:, cols], ["uq", "xq%dh%d" % (t, h)])
+        mm(h, nc[h], T.uq[:], T.us[:], T["xq%d" % t][:, cols[h]], T["xs%d" % t][:, cols[h]], ["uq", "xq%dh%d" % (t, h)])
 
-    def signs(h, on_scalar):
+    def signs(h, on_scalar=False):
         if on_scalar:
-            act(T.sign[:], bank(h, H), [], ["b%d" % h, "sign"], func=F.Sign, scale=-1.0)
-            act(T.bits[:, H * h:H * (h + 1)], T.sign[:], ["sign"], ["bits%d" % h], func=F.Relu)
+            act(T.sign[:], bank(h, nc[h]), [], ["b%d" % h, "sign"], func=F.Sign, scale=-1.0)
+            act(T.bits[:, cols[h]], T.sign[:], ["sign"], ["bits%d" % h], func=F.Relu)
         else:
-            ts(T.bits[:, H * h:H * (h + 1)], bank(h, H), 0.0, A.is_lt, None, None, [], ["b%d" % h, "bits%d" % h])
+            ts(T.bits[:, cols[h]], bank(h, nc[h]), 0.0, A.is_lt, None, None, [], ["b%d" % h, "bits%d" % h])
 
     def weigh(h):
         bq, bs = T["bq%d" % h], T["bs%d" % h]
         quant(bq[:], bs[:], T.bits[:], ["bits0", "bits1"], ["bq%d" % h])
         for i in range(h + 1):
-            mm(6 + i, 128, T.kq[:, 128 * i:128 * (i + 1)], T.ks[:, 128 * i:128 * (i + 1)], bq[:], bs[:], ["kq", "bq%d" % h])
+            mm(6 + i, 128, T.kq[:, 128 * i:128 * (i + 1)], T.ks[:, 128 * i:128 * (i + 1)], bq[:], bs[:], ["kq%d" % i, "bq%d" % h])
+
+    def select(h):
+        lo, hi = 4 * KC[h], 4 * KC[h + 1]
+        scan(T.z4[:, lo:hi], bank(6, hi, lo), T.d4[:, lo:hi], 0.0, A.max, A.add, ["d4a"], ["b6", "za%d" % h])
+        if h == 1:
+            scan(T.z4[:, 4 * K:8 * K], bank(7, 4 * K), T.d4[:, 4 * K:8 * K], 0.0, A.max, A.add, ["d4v"], ["b7", "zv"])
 
     def post(t, h):
-        msg, key, w = T["msg%d" % t], T["key%d" % t], 4 * KH
-        scan(T.z4[:, w * h:w * (h + 1)], bank(6, w * (h + 1), w * h), T.d4[:, w * h:w * (h + 1)], 0.0, A.max, A.add, ["d4"], ["b6", "za%d" % h])
-        if h == 0:
-            ts(msg[:, 0:KH], T.z4[:, 3:w:4], B4, A.add, None, None, ["za0"], ["msg%d0" % t])
-            send(key[:, 0:KH], msg[:, 0:KH], ["msg%d0" % t], ["key%d0" % t])
-        else:
-            scan(T.z4[:, 4 * K:8 * K], bank(7, 4 * K), T.d4[:, 4 * K:8 * K], 0.0, A.max, A.add, ["d4"], ["b7", "zv"])
-            ts(msg[:, KH:2 * K], T.z4[:, w + 3::4], B4, A.add, None, None, ["za1", "zv"], ["msg%d1" % t])
-            send(key[:, KH:2 * K], msg[:, KH:2 * K], ["msg%d1" % t], ["key%d1" % t])
+        msg, key = T["msg%d" % t], T["key%d" % t]
+        lo, hi = (0, KC[1]) if h == 0 else (KC[1], 2 * K)
+        ts(msg[:, lo:hi], T.z4[:, 4 * lo + 3:4 * hi:4], B4, A.add, None, None, ["za%d" % h] + ["zv"] * h, ["msg%d%d" % (t, h)])
+        send(key[:, lo:hi], msg[:, lo:hi], ["msg%d%d" % (t, h)], ["key%d%d" % (t, h)])
+
+    def layer(t, h):
+        for b in range(4):
+            mm(2 + b, nc[h], T.wq[:, 128 * b:128 * (b + 1)], T.wp[:, 128 * b:128 * (b + 1)], T["xq%d" % t][:, cols[h]], T["xs%d" % t][:, cols[h]],
+               ["xq%dh%d" % (t, h), "wq", "wp"])
+            act(T.pt[:, 4 * CC[h] + b:4 * CC[h + 1]:4], bank(2 + b, nc[h]), [], ["b%d" % (2 + b), "p%d%d" % (h, b)], scale=0.03125)
+
+    def quant_p(t, h):
+        quant(T["pq%d" % t][:, cols[h]], T["pp%d" % t][:, cols[h]], T.pt[:, wide[h]], ["p%d%d" % (h, b) for b in range(4)], ["pq%d%d" % (t, h)])
+
+    def send_p(t, h):
+        send(T["lq%d" % t][:, cols[h]].bitcast(u8), T["pq%d" % t][:, cols[h]].bitcast(u8), ["pq%d%d" % (t, h)], ["lq%d%d" % (t, h)])
+        if h == 1:
+            send(T["lp%d" % t][:], T["pp%d" % t][:], ["pq%d0" % t, "pq%d1" % t], ["lp%d" % t])
 
     quant_state(0, 0)
     scores(0, 0)
-    signs(0, False)
+    constants(0)
+    signs(0)
+    constants(1)
     weigh(0)
+    constants(2)
+    select(0)
+    constants(3)
     post(0, 0)
+    iota(T.t16[:], [[0, KC[1]], [S16, 16]], 0, 0, ["t16"])
     quant_state(0, 1)
 
     for t in range(2):
-        xq, xs = T["xq%d" % t], T["xs%d" % t]
         msg, key, tab = T["msg%d" % t], T["key%d" % t], T["tab%d" % t]
-        pq, pp, lq, lp = T["pq%d" % t], T["pp%d" % t], T["lq%d" % t], T["lp%d" % t]
-        both = ["xq%dh0" % t, "xq%dh1" % t]
-
-        def layer(b):
-            mm(2 + b, C, T.wq[:, 128 * b:128 * (b + 1)], T.wp[:, 128 * b:128 * (b + 1)], xq[:], xs[:], both + ["wq", "wp"])
-            act(T.pt[:, b::4], bank(2 + b, C), [], ["b%d" % (2 + b), "p%d" % b], scale=0.03125)
+        lq, lp = T["lq%d" % t], T["lp%d" % t]
+        more = constants if t == 0 else (lambda i: None)
 
         scores(t, 1)
-        if t > 0:
-            layer(0)
-        signs(1, False)
+        more(4)
+        if t == 1:
+            quant_p(t, 0)
+        signs(1)
+        more(5)
+        if t == 1:
+            quant(T.vq[:], T.vs[:], T.vt[:], ["vt"], ["vq"])
         weigh(1)
-        for b in range(1 if t > 0 else 0, 4):
-            layer(b)
+        more(6)
+        if t == 0:
+            layer(t, 0)
+        layer(t, 1)
+        select(1)
         post(t, 1)
 
         za, zv = T.z4[:, 3:4 * K:4], T.z4[:, 4 * K + 3::4]
         ts(T.qi[:, 0:K], za, B4 + 1.0, A.add, None, None, ["za0", "za1"], ["qi0"])
         ts(T.qi[:, K:2 * K], za, B4 + SLOTS - 1.0, A.add, None, None, ["za0", "za1"], ["qi1"])
-        tt(T.hb[:], zv, T.jn[:], A.add, ["zv", "jn"], ["hb"])
-        ts(T.qj[:], T.qi[:], SLOTS - 1, A.bitwise_and, None, None, ["qi0", "qi1"], ["qj"])
+        more(7)
         if t == 0:
-            late_constants()
             unit_tile(0)
-            unit_tile(1)
-        else:
-            quant(T.vq[:], T.vs[:], T.vt[:], ["vt"], ["vq"])
-        cp(T.qo[:], T.qj[:], ["qj"], ["qo"])
+            quant_p(t, 0)
+        send_p(t, 0)
+        if t == 0:
+            quant_p(t, 1)
+            send_p(t, 1)
+            for b in range(1, 4):
+                unit_tile(b)
+            iota(T.tab1[:, FB:FB + SLOTS], [[0, SLOTS]], int(EMPTY), 0, ["tabF1"])
 
         for h in range(2):
-            kk, lists = "key%d%d" % (t, h), slice(KH * h, KH * (h + 1))
-            rows = range(KH * h, KH * (h + 1))
-            cp(T.rep[:, H * h:H * (h + 1)], T.ramp[:].indirect(key[:, lists]), ["ramp", kk], ["rep%d" % h])
-            cp(T.af[:, lists], key[:, lists], [kk], ["af%d" % h])
+            kk = "key%d%d" % (t, h)
+            rows = range(KC[h], KC[h + 1])
+            cp(T.af[:, lists[h]], key[:, lists[h]], [kk], ["af%d" % h])
             if h == 1:
+                act(T.ae[:, lists[h]], T.af[:, lists[h]], ["af%d" % h], ["ae%d" % h], func=F.Exp, scale=SPREAD)
+                cp(T.rep[:, cols[h]], T.enc[:].indirect(key[:, lists[h]]), ["enc", kk], ["rep%d" % h])
                 act(T.val[:], T.ramp[:].indirect(key[:, K:2 * K]), ["ramp", kk], ["val"])
-            for c in reversed(rows):
-                ts(T.cmp[:, OFF[c]:OFF[c] + ROW[c]], T.rep[:, 0:ROW[c]], T.af[:, c:c + 1], A.is_equal, EPS, A.mult,
-                   ["rep%d" % i for i in range(h + 1)] + ["af%d" % h], ["ch%d" % c, "ct%d" % c])
-                if ROW[c] > TAIL:
-                    head = T.cmp[:, OFF[c]:OFF[c] + ROW[c] - TAIL]
-                    act(head, head, [], ["ch%d" % c, "acc%d" % c], scale=MUL, accum_out=T.acc[:, c:c + 1])
-            if h == 0:
-                quant(pq[:], pp[:], T.pt[:], ["p0", "p1", "p2", "p3"], ["pq%d" % t])
-                send(lq[:].bitcast(u8), pq[:].bitcast(u8), ["pq%d" % t], ["lq%d" % t])
-                send(lp[:], pp[:], ["pq%d" % t], ["lp%d" % t])
-                if t == 0:
-                    unit_tile(2)
-                    unit_tile(3)
-                    iota(T.tab1[:, FB:FB + SLOTS], [[0, SLOTS]], int(EMPTY), 0, ["tabF1"])
             else:
-                ts(T.ab[:], T.af[:], float(FB), A.add, None, None, ["af0", "af1"], ["ab"])
+                act(T.rep[:, cols[h]], T.enc[:].indirect(key[:, lists[h]]), ["enc", kk], ["rep%d" % h])
+                act(T.ae[:, lists[h]], T.af[:, lists[h]], ["af%d" % h], ["ae%d" % h], func=F.Exp, scale=SPREAD)
+                ts(T.qj[:], T.qi[:], SLOTS - 1, A.bitwise_and, None, None, ["qi0", "qi1"], ["qj"])
+                tt(T.hb[:], zv, T.jn[:], A.add, ["zv", "jn"], ["hb"])
+                if t == 1:
+                    quant_p(t, 1)
+                    send_p(t, 1)
+                cp(T.qo[:], T.qj[:], ["qj"], ["qo"])
             for c in reversed(rows):
-                n = min(ROW[c], TAIL)
-                end = OFF[c] + ROW[c]
-                if c == KH:
-                    tt(T.s0[:], T.acc[:], T.ab[:], A.add, ["ab", "acc0"] + ["acc%d" % i for i in range(TAIL // 16, K)], ["s0"])
+                ts(T.cmp[:, OFF[c]:OFF[c] + ROW[c]], T.rep[:, 0:ROW[c]], T.ae[:, c:c + 1], A.is_equal, EPS, A.mult,
+                   ["rep%d" % i for i in range(h + 1)] + ["ae%d" % h], ["ch%d" % c, "ct%d" % c])
+            for c in reversed(rows):
+                if ROW[c] > OWN[c]:
+                    head = T.cmp[:, OFF[c]:OFF[c] + ROW[c] - OWN[c]]
+                    act(head, head, ["ct%d" % AHEAD.get(c, c)], ["ch%d" % c, "acc%d" % c], scale=MUL, accum_out=T.acc[:, c:c + 1])
+            if h == 0 and t == 0:
+                act(T.tab0[:, FB:FB + SLOTS], T.ramp[:], ["ramp"], ["tabF0"], scale=0.0, bias=EMPTY)
+                act(T.tab0[:, GB:GB + SLOTS], T.ramp[:], ["ramp"], ["tabG0"], scale=0.0, bias=EMPTY)
+            if h == 1:
+                ts(T.ab[:], T.af[:], float(FB), A.add, None, None, ["af0", "af1"], ["ab"])
+            for c in (list(rows) if h == 1 else [1, 0] + list(rows)[2:]):
+                n, end = OWN[c], OFF[c] + ROW[c]
+                if c == K - 1:
+                    tt(T.s0[:], T.acc[:], T.ab[:], A.add, ["ab", "acc0"] + ["acc%d" % i for i in range(8, K)], ["s0"])
                 scan(T.zs[:, TAIL * (c + 1) - n:TAIL * (c + 1)], T.mask[:, TAIL - n:TAIL], T.cmp[:, end - n:end], 0.0, A.mult, A.add,
                      ["mask", "ct%d" % c], ["zs%d" % c])
         if t == 0:
@@ -347,57 +398,100 @@ def rank_program(g, core, T, topo):
             quant(T.eq4[:], T.es[:], T.et[:], ["e0", "e1", "e2", "e3"], ["eq4"])
 
         wf, wg = tab[:, FB:FB + SLOTS], tab[:, GB:GB + SLOTS]
-        kf, kg, mk = "tabF%d" % t, "tabG%d" % t, ["msg%d0" % t, "msg%d1" % t]
+        kf, kg = "tabF%d" % t, "tabG%d" % t
+        span = lambda h, i: slice(2 * CC[h] + nc[h] * i, 2 * CC[h] + nc[h] * (i + 1))
+        few = lambda h, i: slice(2 * KC[h] + nk[h] * i, 2 * KC[h] + nk[h] * (i + 1))
         for h in range(2):
-            act(T.tf[:, H * h:H * (h + 1)], wf.indirect(msg[:, KH * h:KH * (h + 1)]), [kf] + mk, ["tf0%d" % h], bias=float(SLOTS))
-        act(T.tf[:, C:2 * C], wf.indirect(T.qo[:, 0:K]), [kf, "qo"], ["tf1"], bias=float(SLOTS))
+            act(T.tf[:, span(h, 0)], wf.indirect(msg[:, lists[h]]), [kf, "msg%d%d" % (t, h)], ["tf%d0" % h], bias=float(SLOTS))
+            act(T.tf[:, span(h, 1)], wf.indirect(T.qo[:, lists[h]]), [kf, "qo"], ["tf%d1" % h], bias=float(SLOTS))
         for b in range(4):
-            mm(2 + b, C, T.eq4[:, 128 * b:128 * (b + 1)], T.es[:, 128 * b:128 * (b + 1)], lq[:], lp[:], ["eq4", "lq%d" % t, "lp%d" % t])
+            mm(2 + b, C, T.eq4[:, 128 * b:128 * (b + 1)], T.es[:, 128 * b:128 * (b + 1)], lq[:], lp[:],
+               ["eq4", "lq%d0" % t, "lq%d1" % t, "lp%d" % t])
             act(T.dn[:, DW * b:DW * b + C], bank(2 + b, C), [], ["b%d" % (2 + b), "dn%d" % b])
-        for h in range(2):
-            tt(T.look[:, H * h:H * (h + 1)], wg.indirect(T.qo[:, K + KH * h:K + KH * (h + 1)]), T.tf[:, H * h:H * (h + 1)], A.max,
-               [kg, "qo", "tf0%d" % h], ["lk0%d" % h])
-        scan(T.z16[:, 0:C], T.look[:, 0:C], T.d16[:], -B16, A.max, A.add, ["lk00", "lk01", "d16"], ["z160"])
-        tt(T.look[:, C:2 * C], wg.indirect(msg[:, 0:K]), T.tf[:, C:2 * C], A.max, [kg, "tf1"] + mk, ["lk1"])
-        tt(T.x1[:, 0:K], T.z16[:, 15:C:16], T.hb[:], A.add, ["z160", "hb"], ["x10"])
-        scan(T.z16[:, C:2 * C], T.look[:, C:2 * C], T.d16[:], -B16, A.max, A.add, ["lk1", "d16"], ["z161"])
-        ts(T.x2[:, 0:K], T.x1[:, 0:K], SLOTS - 1, A.bitwise_and, None, None, ["x10"], ["x20"])
-        tt(T.x1[:, K:2 * K], T.z16[:, C + 15::16], T.hb[:], A.add, ["z161", "hb"], ["x11"])
-        ts(T.x3[:], T.x2[:, 0:K], float(C), A.is_lt, 4096.0, A.mult, ["x20"], ["x3"])
-        ts(T.x2[:, K:2 * K], T.x1[:, K:2 * K], SLOTS - 1, A.bitwise_and, None, None, ["x11"], ["x21"])
-        tt(T.x4[:], T.x2[:, K:2 * K], T.x3[:], A.max, ["x21", "x3"], ["x4"])
-        tt(T.x5[:], T.x2[:, 0:K], T.x4[:], A.min, ["x20", "x4"], ["x5"])
-        ts(T.fin[:], T.x5[:], float(C), A.min, None, None, ["x5"], ["fin"])
 
-        def add(h, b):
-            lo, hi = 4 * H * h + b, 4 * H * (h + 1)
-            tt(state[t + 1][:, lo:hi:4], T.dn[:, DW * b:DW * b + C + 1].indirect(T.fin[:, KH * h:KH * (h + 1)]), T.pt[:, lo:hi:4], A.add,
-               ["dn%d" % b, "dzero", "fin", "p%d" % b], ["x%dh%db%d" % (t + 1, h, b)])
+        def look(h, i):
+            at = T.qo[:, K + KC[h]:K + KC[h + 1]] if i == 0 else msg[:, lists[h]]
+            tt(T.look[:, span(h, i)], wg.indirect(at), T.tf[:, span(h, i)], A.max, [kg, "qo", "msg%d%d" % (t, h), "tf%d%d" % (h, i)], ["lk%d%d" % (h, i)])
+
+        def pick(h, i):
+            scan(T.z16[:, span(h, i)], T.look[:, span(h, i)], T.d16[:, 0:nc[h]], -B16, A.max, A.add, ["lk%d%d" % (h, i), "d16"], ["z16%d%d" % (h, i)])
+
+        def step(h, s):
+            x0, x1, ls, both = few(h, 0), few(h, 1), lists[h], slice(2 * KC[h], 2 * KC[h + 1])
+            if s < 2:
+                sp = span(h, s)
+                tt(T.x1[:, few(h, s)], T.z16[:, sp.start + 15:sp.stop:16], T.hb[:, ls], A.add, ["z16%d%d" % (h, s), "hb"], ["x1%d%d" % (h, s)])
+            elif s == 2:
+                ts(T.x2[:, both], T.x1[:, both], SLOTS - 1, A.bitwise_and, None, None, ["x1%d0" % h, "x1%d1" % h], ["x2%d" % h])
+            elif s == 3:
+                ts(T.x3[:, ls], T.x2[:, x0], float(C), A.is_lt, 4096.0, A.mult, ["x2%d" % h], ["x3%d" % h])
+            elif s == 4:
+                tt(T.x4[:, ls], T.x2[:, x1], T.x3[:, ls], A.max, ["x2%d" % h, "x3%d" % h], ["x4%d" % h])
+            elif s == 5:
+                tt(T.x5[:, ls], T.x2[:, x0], T.x4[:, ls], A.min, ["x2%d" % h, "x4%d" % h], ["x5%d" % h])
+            else:
+                ts(T.fin[:, ls], T.x5[:, ls], float(C), A.min, None, None, ["x5%d" % h], ["fin%d" % h])
+
+        def add(h):
+            for b in range(4):
+                sl = slice(4 * CC[h] + b, 4 * CC[h + 1], 4)
+                tt(state[t + 1][:, sl], T.dn[:, DW * b:DW * b + C + 1].indirect(T.fin[:, lists[h]]), T.pt[:, sl], A.add,
+                   ["dn%d" % b, "dzero", "fin%d" % h, "p%d%d" % (h, b)], ["x%dh%db%d" % (t + 1, h, b)])
 
         def store(h):
-            cols = slice(H * h, H * (h + 1))
-            dma("s", T.oc[:, 4 * H * h:4 * H * (h + 1)], T.xq2[:, cols].bitcast(u8), ["xq2h%d" % h], [])
-            mm(h, H, T.vq[:], T.vs[:], T.xq2[:, cols], T.xs2[:, cols], ["vq", "xq2h%d" % h])
-            act(T.yo[:, cols], bank(h, H), [], ["b%d" % h, "yo%d" % h])
-            dma("a", T.y[:, cols], T.yo[:, cols], ["yo%d" % h], [])
+            dma("s", T.oc[:, wide[h]], T.xq2[:, cols[h]].bitcast(u8), ["xq2h%d" % h], [])
+            mm(h, nc[h], T.vq[:], T.vs[:], T.xq2[:, cols[h]], T.xs2[:, cols[h]], ["vq", "xq2h%d" % h])
+            act(T.yo[:, cols[h]], bank(h, nc[h]), [], ["b%d" % h, "yo%d" % h])
+            dma("a", T.y[:, cols[h]], T.yo[:, cols[h]], ["yo%d" % h], [])
 
-        for b in range(4):
-            add(0, b)
-        quant_state(t + 1, 0)
+        look(0, 0)
+        look(0, 1)
+        pick(0, 0)
+        pick(0, 1)
+        step(0, 0)
+        step(0, 1)
+        look(1, 0)
+        step(0, 2)
+        look(1, 1)
         if t == 0:
+            for s in range(3, 7):
+                step(0, s)
+            add(0)
+            pick(1, 0)
+            quant_state(1, 0)
             scores(1, 0)
             signs(0, True)
-            add(1, 0)
-            add(1, 1)
+            pick(1, 1)
+            step(1, 0)
+            step(1, 1)
+            step(1, 2)
+            step(1, 3)
+            step(1, 4)
             weigh(0)
-            add(1, 2)
+            layer(1, 0)
+            step(1, 5)
+            select(0)
+            step(1, 6)
             post(1, 0)
-            add(1, 3)
+            add(1)
             quant_state(1, 1)
         else:
+            step(0, 3)
+            pick(1, 0)
+            step(0, 4)
+            pick(1, 1)
+            step(0, 5)
+            step(1, 0)
+            step(0, 6)
+            step(1, 1)
+            step(1, 2)
+            add(0)
+            step(1, 3)
+            quant_state(2, 0)
             store(0)
-            for b in range(4):
-                add(1, b)
+            for s in range(4, 7):
+                step(1, s)
+            add(1)
             quant_state(2, 1)
             store(1)
     for k in range(4):

@@ -1,22 +1,23 @@
+import numpy as np
 from concourse.mybir import dt, AluOpType as A, AxisListType, ActivationFunctionType as F
 
 C, K = 448, 28
-KC = [0, 18, K]
+KC = [0, 14, K]
 CC = [16 * k for k in KC]
+NK = [KC[1], K - KC[1]]
+NC = [16 * k for k in NK]
+WK, WC = max(NK), max(NC)
 SLOTS = 1024
 DW = 464
-GB, FB = 512, 2048
-STEP = FB - GB
-EPS = 2.0 ** -10
-MUL = -STEP / EPS
+STEP = 2048
+DUMP = STEP + SLOTS
 EMPTY = -1025.0
-SPREAD = 0.016
+BIAS = 3.0
 B4, B16, S16 = 2048.0, 2000.0, 4096
-TAIL = 160
-ROW = [16 * (c + 1) for c in range(K)]
-OWN = [min(ROW[c], 128 if c < KC[1] else TAIL) for c in range(K)]
-OFF = [sum(ROW[:c]) for c in range(K)]
-AHEAD = {25: 24, 23: 21, 20: 18, 15: 14, 13: 11, 10: 8}
+SHARP, EPS = 16.0, 2.0 ** -9
+NEAR = 64.0
+TINY = 2.0 ** -110
+ROWS = [[3, 4], [1, 3]]
 HALF = "float16"
 Q4 = "float8_e4m3fn_x4"
 
@@ -26,28 +27,31 @@ SCRATCH = {
     "uq": ("sbuf", [128, 128], Q4), "us": ("sbuf", [128, 128], "uint8"),
     "vq": ("sbuf", [128, 128], Q4), "vs": ("sbuf", [128, 128], "uint8"),
     "wq": ("sbuf", [128, 512], Q4), "wp": ("sbuf", [128, 512], "uint8"),
-    "ones": ("sbuf", [128, 512], "bfloat16"),
-    "et": ("sbuf", [128, 2048], "bfloat16"), "eq4": ("sbuf", [128, 512], Q4), "es": ("sbuf", [128, 512], "uint8"),
+    "ones": ("sbuf", [128, 516], "bfloat16"),
+    "et": ("sbuf", [128, 516], "bfloat16"), "eq4": ("sbuf", [128, 512], Q4), "es": ("sbuf", [128, 512], "uint8"),
     "kt": ("sbuf", [128, 1024], "bfloat16"), "kq": ("sbuf", [128, 256], Q4), "ks": ("sbuf", [128, 256], "uint8"),
-    "sign": ("sbuf", [128, CC[1]], "bfloat16"), "bits": ("sbuf", [128, 512], "bfloat16"),
-    "bq0": ("sbuf", [128, 128], Q4), "bs0": ("sbuf", [128, 128], "uint8"),
-    "bq1": ("sbuf", [128, 128], Q4), "bs1": ("sbuf", [128, 128], "uint8"),
-    "pt": ("sbuf", [128, 4 * C], "bfloat16"), "dn": ("sbuf", [128, 4 * DW], "bfloat16"),
+    "bits": ("sbuf", [128, CC[1] + 512], "bfloat16"),
+    "dn": ("sbuf", [128, 4 * DW], "bfloat16"),
     "ps": ("psum", [128, 4096], "float32"),
     "pi": ("sbuf", [128, 8], "int32"), "col": ("sbuf", [128, 16], "float32"), "k16": ("sbuf", [128, 16], "float32"),
     "gm": ("sbuf", [128, 32], "float32"), "r16": ("sbuf", [128, 16], "float32"), "c16": ("sbuf", [128, K], "float32"),
-    "t4": ("sbuf", [128, 4 * K], "float32"), "d4": ("sbuf", [128, 8 * K], "float32"),
-    "t16": ("sbuf", [128, CC[1]], "bfloat16"), "d16": ("sbuf", [128, CC[1]], HALF),
-    "ramp": ("sbuf", [128, SLOTS], "float32"), "enc": ("sbuf", [128, SLOTS], "bfloat16"),
-    "jw": ("sbuf", [128, K], "float32"), "jn": ("sbuf", [128, K], "float32"), "jc": ("sbuf", [128, K], "float32"),
-    "mtmp": ("sbuf", [128, TAIL], "float32"), "mask": ("sbuf", [128, TAIL], "bfloat16"),
-    "z4": ("sbuf", [128, 8 * K], "float32"), "qi": ("sbuf", [128, 2 * K], "int32"), "qj": ("sbuf", [128, 2 * K], "int32"),
-    "qo": ("sbuf", [128, 2 * K], "uint16"), "hb": ("sbuf", [128, K], "float32"),
-    "af": ("sbuf", [128, K], "float32"), "ae": ("sbuf", [128, K], "bfloat16"), "ab": ("sbuf", [128, K], "float32"),
-    "rep": ("sbuf", [128, C], "bfloat16"), "val": ("sbuf", [128, C], "float32"),
-    "cmp": ("sbuf", [128, sum(ROW)], "bfloat16"), "zs": ("sbuf", [128, K * TAIL], "bfloat16"), "acc": ("sbuf", [128, K], "float32"),
-    "s0": ("sbuf", [128, K], "float32"), "s1": ("sbuf", [128, K], "float32"), "s2": ("sbuf", [128, K], "float32"),
-    "so": ("sbuf", [128, K], "uint16"),
+    "t4": ("sbuf", [128, 8 * K], "float32"), "d4": ("sbuf", [128, 8 * K], "float32"),
+    "jx": ("sbuf", [128, 2 * K], "float32"), "jy": ("sbuf", [128, 2 * K], "float32"),
+    "t16": ("sbuf", [128, WC], "bfloat16"), "d16": ("sbuf", [128, WC], HALF),
+    "r1": ("sbuf", [128, WC], "bfloat16"), "m1": ("sbuf", [128, WC], "bfloat16"), "mask": ("sbuf", [128, WC], "bfloat16"),
+    "ramp": ("sbuf", [128, SLOTS], "float32"), "cl": ("sbuf", [128, WK], "uint16"),
+    "jd": ("sbuf", [128, K], "float32"), "jn": ("sbuf", [128, 2 * K], "float32"),
+    "z4": ("sbuf", [128, 8 * K], "float32"), "q1": ("sbuf", [128, 2 * K], "uint16"), "q7": ("sbuf", [128, 2 * K], "uint16"),
+    "hb": ("sbuf", [128, K], "float32"), "nb": ("sbuf", [128, K], "float32"),
+    "rep": ("sbuf", [128, C], "float32"), "val": ("sbuf", [128, C], "float32"),
+    "junk": ("sbuf", [128, 8 * (NK[0] ** 2 + NK[1] ** 2)], "bfloat16"), "acc": ("sbuf", [128, K], "float32"),
+    "eq": ("sbuf", [128, 16 * WC], "bfloat16"), "sums": ("sbuf", [128, 8 * WC], "bfloat16"),
+    "cmp": ("sbuf", [128, C], "bfloat16"), "zs": ("sbuf", [128, C], "bfloat16"),
+    "cf": ("sbuf", [128, WC], "float32"), "cg": ("sbuf", [128, WC], HALF), "cz": ("sbuf", [128, WC], HALF),
+    "z1": ("sbuf", [128, K], "float32"), "base": ("sbuf", [128, K], "float32"), "pen": ("sbuf", [128, K], "float32"),
+    "e1": ("sbuf", [128, K], "int32"), "e2": ("sbuf", [128, K], "int32"),
+    "s1": ("sbuf", [128, K], "float32"), "s2": ("sbuf", [128, K], "float32"), "s4": ("sbuf", [128, K], "float32"),
+    "s5": ("sbuf", [128, K], "float32"), "so": ("sbuf", [128, K], "uint16"),
     "tf": ("sbuf", [128, 2 * C], "float32"), "look": ("sbuf", [128, 2 * C], HALF), "z16": ("sbuf", [128, 2 * C], HALF),
     "x1": ("sbuf", [128, 2 * K], "int32"), "x2": ("sbuf", [128, 2 * K], "int32"),
     "x3": ("sbuf", [128, K], "float32"), "x4": ("sbuf", [128, K], "float32"), "x5": ("sbuf", [128, K], "float32"),
@@ -57,34 +61,67 @@ for _t in range(3):
     SCRATCH["xq%d" % _t] = ("sbuf", [128, C], Q4)
     SCRATCH["xs%d" % _t] = ("sbuf", [128, C], "uint8")
 for _t in range(2):
+    SCRATCH["bq%d" % _t] = ("sbuf", [128, 128], Q4)
+    SCRATCH["bs%d" % _t] = ("sbuf", [128, 128], "uint8")
+    SCRATCH["af%d" % _t] = ("sbuf", [128, WK], "float32")
+    SCRATCH["pt%d" % _t] = ("sbuf", [128, 4 * C], "bfloat16")
     SCRATCH["pq%d" % _t] = ("sbuf", [128, C], Q4)
     SCRATCH["pp%d" % _t] = ("sbuf", [128, C], "uint8")
     SCRATCH["lq%d" % _t] = ("sbuf", [128, C], Q4)
     SCRATCH["lp%d" % _t] = ("sbuf", [128, C], "uint8")
-    SCRATCH["msg%d" % _t] = ("sbuf", [128, 2 * K], "uint16")
-    SCRATCH["key%d" % _t] = ("sbuf", [128, 2 * K], "uint16")
-    SCRATCH["tab%d" % _t] = ("sbuf", [128, FB + SLOTS], "float32")
+    SCRATCH["msg%d" % _t] = ("sbuf", [128, 3 * K], "uint16")
+    SCRATCH["key%d" % _t] = ("sbuf", [128, 3 * K], "uint16")
+    SCRATCH["cnt%d" % _t] = ("sbuf", [128, NK[1]], "float32")
+    SCRATCH["got%d" % _t] = ("sbuf", [128, NK[1]], "float32")
+    SCRATCH["tab%d" % _t] = ("sbuf", [128, DUMP + C], "float32")
 
-SEMAPHORES = (["cv", "ca", "ct", "cg"] + ["d%d" % i for i in range(20)] + ["l%d" % i for i in range(10)]
-              + ["r%d" % i for i in range(10)])
+SEMAPHORES = (["cv", "ca", "ct", "cg"] + ["d%d" % i for i in range(20)] + ["l%d" % i for i in range(16)]
+              + ["r%d" % i for i in range(16)])
+
+ORDER = [7,6,9,8,13,11,10,12,14,15,19,39,18,20,21,17,26,22,24,0,1,2,3,4,5,16,38,37,66,67,41,23,34,33,25,51,30,27,29,54,28,32,35,68,45,36,31,40,42,69,70,43,92,64,71,44,55,93,94,72,74,73,75,76,125,95,98,53,56,52,48,99,96,124,97,127,100,129,156,85,81,79,83,126,50,133,134,141,142,155,139,157,138,137,140,136,135,171,82,172,80,174,84,86,168,166,169,170,167,173,143,131,128,144,132,130,175,148,145,162,146,164,147,160,149,176,150,163,177,151,46,152,77,59,61,161,158,62,178,159,63,165,78,185,87,180,153,101,65,103,109,107,105,49,108,106,110,154,102,90,179,181,182,183,186,57,58,60,188,104,88,184,187,47,189,111,190,191,192,193,194,195,119,116,118,196,117,112,114,89,91,216,197,203,199,201,220,217,113,115,223,213,221,218,224,214,222,215,225,219,226,204,198,202,200,227,228,205,206,229,230,231,207,211,209,208,212,210,232,233,235,234,240,241,242,239,243,236,251,255,253,257,244,246,247,245,248,122,123,249,238,293,237,252,256,254,258,259,264,292,294,250,265,300,301,298,303,306,266,308,299,297,304,305,302,307,295,309,267,350,268,277,270,275,279,281,271,269,310,296,272,311,314,313,322,312,315,316,317,318,321,323,332,330,339,335,331,338,337,333,334,336,260,121,273,262,319,120,326,324,328,340,327,341,342,325,329,343,345,344,274,346,347,261,320,351,290,288,276,280,282,278,348,263,353,349,368,364,366,362,367,363,352,283,289,286,284,285,287,354,355,356,357,358,359,360,361,291,381,382,378,379,385,388,374,365,369,370,376,372,375,373,377,371,383,386,389,387,390,380,391,384,392,393,394,395,396,402,403,401,404,398,410,400,397,399,411,416,417,418,405,407,406,412,413,415,408,414,409,419]
+
+
+def depend(ops):
+    writer, readers, banks = {}, {}, {}
+    for i, o in enumerate(ops):
+        deps = set(o["after"])
+        for is_out, views in ((False, o["r"]), (True, o["w"])):
+            for name, lo, hi, step in views:
+                if name == "ps":
+                    deps.update(banks.get(lo // 512, []))
+                    continue
+                if name not in writer:
+                    writer[name], readers[name] = np.full(SCRATCH[name][1][1], -1), []
+                deps.update(int(n) for n in np.unique(writer[name][lo:hi:step]) if n >= 0)
+                if is_out:
+                    mine = set(range(lo, hi, step))
+                    deps.update(n for n, seen in readers[name] if seen & mine)
+                    readers[name] = [(n, seen - mine) for n, seen in readers[name] if seen - mine]
+        o["deps"] = deps
+        for is_out, views in ((False, o["r"]), (True, o["w"])):
+            for name, lo, hi, step in views:
+                if name == "ps":
+                    banks[lo // 512] = [i]
+                elif is_out:
+                    writer[name][lo:hi:step] = i
+                else:
+                    readers[name].append((i, set(range(lo, hi, step))))
 
 
 def schedule(g, T, ops):
     queue = {"v": g.vector, "a": g.scalar, "t": g.tensor, "g": g, "s": g.sync}
-    writer, readers, clock = {}, {}, {e: {} for e in queue}
-    for i, o in enumerate(ops):
-        deps = set()
-        for k in o["r"] + o["w"]:
-            if k in writer:
-                deps.add(writer[k])
-        for k in o["w"]:
-            deps.update(readers.get(k, []))
+    depend(ops)
+    place = {i: k for k, i in enumerate(ORDER)}
+    assert sorted(ORDER) == list(range(len(ops))) and all(place[d] < place[i] for i, o in enumerate(ops) for d in o["deps"])
+    clock = {e: {} for e in queue}
+    for i in ORDER:
+        o = ops[i]
         o["waits"] = []
         if o["e"] is not None:
             ck = clock[o["e"]]
-            for d in sorted(deps, reverse=True):
+            for d in sorted(o["deps"], key=lambda d: -place[d]):
                 p = ops[d]
-                if ck.get(p["src"], -1) >= d:
+                if ck.get(p["src"], -1) >= place[d]:
                     continue
                 o["waits"].append(d)
                 p["used"] = True
@@ -93,18 +130,15 @@ def schedule(g, T, ops):
             o["snap"] = dict(ck)
         else:
             o["snap"] = {}
-        o["snap"][o["src"]] = i
-        for k in o["w"]:
-            writer[k] = i
-            readers[k] = []
-        for k in o["r"]:
-            readers.setdefault(k, []).append(i)
+        o["snap"][o["src"]] = place[i]
     count = {}
-    for o in ops:
+    for i in ORDER:
+        o = ops[i]
         if o["sem"] is None and o.get("used"):
             count[o["e"]] = count.get(o["e"], 0) + 1
             o["sem"], o["n"], o["inc"] = "c" + o["e"], count[o["e"]], 1
-    for o in ops:
+    for i in ORDER:
+        o = ops[i]
         if o["e"] is None:
             continue
         q = queue[o["e"]]
@@ -126,375 +160,298 @@ def rank_program(g, core, T, topo):
     rid, pid = topo.addr(dst, core)
     mask_out, n_out, n_in = topo.mask(core, dst), len(topo.engines(core, dst)), len(topo.engines(src, core))
     ops, nd, nr, ends = [], [0], [0], []
+    u8 = dt.uint8
 
-    def op(e, f, r, w):
-        ops.append({"e": e, "f": f, "r": list(r), "w": list(w), "src": e, "sem": None})
+    def V(name, lo=0, hi=None, step=1):
+        hi = SCRATCH[name][1][1] if hi is None else hi
+        return (T[name][:, lo:hi:step] if step > 1 else T[name][:, lo:hi], [(name, lo, hi, step)])
 
-    def dma(e, out, in_, r, w):
+    def by(win, off):
+        return (win[0].indirect(off[0]), win[1] + off[1])
+
+    def raw(v):
+        return (v[0].bitcast(u8), v[1])
+
+    def ap(v):
+        return v[0] if isinstance(v, tuple) else v
+
+    def op(e, f, ins, outs, after=()):
+        ops.append({"e": e, "f": f, "r": [k for v in ins if isinstance(v, tuple) for k in v[1]], "w": [k for v in outs for k in v[1]],
+                    "src": e, "sem": None, "after": list(after)})
+        return len(ops) - 1
+
+    def dma(e, out, in_):
         s = "d%d" % nd[0]
         nd[0] += 1
-        ops.append({"e": e, "f": lambda q: q.dma_start(out, in_), "r": list(r), "w": list(w) + [s], "src": s, "sem": s, "n": 16, "inc": 16})
-        ends.append(s)
+        i = op(e, lambda q: q.dma_start(out[0], in_[0]), [in_], [out])
+        ops[i].update({"src": s, "sem": s, "n": 16, "inc": 16})
+        ends.append(i)
 
-    def send(out, in_, r, w):
-        i = nr[0]
+    def send(out, in_):
+        k = nr[0]
         nr[0] += 1
-        ls, rs = "l%d" % i, "r%d" % i
-        ops.append({"e": "g", "f": lambda q: q.remote_dma(out, in_, T.sem[rs], T.sem[ls], pid, rid, mask_out),
-                    "r": list(r), "w": [ls], "src": ls, "sem": ls, "n": n_out})
-        ops.append({"e": None, "f": None, "r": [], "w": list(w), "src": rs, "sem": rs, "n": n_in})
-        ends.append(ls)
+        ls, rs = "l%d" % k, "r%d" % k
+        i = op("g", lambda q: q.remote_dma(out[0], in_[0], T.sem[rs], T.sem[ls], pid, rid, mask_out), [in_], [])
+        ops[i].update({"src": ls, "sem": ls, "n": n_out})
+        ends.append(i)
+        j = op(None, None, [], [out], after=[i])
+        ops[j].update({"src": rs, "sem": rs, "n": n_in})
+        return i
 
-    def ts(out, in0, s1, op0, s2, op1, r, w):
+    def ts(out, in0, s1, op0, s2=None, op1=None):
         if op1 is None:
-            op("v", lambda q: q.tensor_scalar(out, in0, s1, None, op0), r, w)
+            op("v", lambda q: q.tensor_scalar(out[0], in0[0], ap(s1), None, op0), [in0, s1], [out])
         else:
-            op("v", lambda q: q.tensor_scalar(out, in0, s1, s2, op0, op1), r, w)
+            op("v", lambda q: q.tensor_scalar(out[0], in0[0], ap(s1), ap(s2), op0, op1), [in0, s1, s2], [out])
 
-    def tt(out, in0, in1, o, r, w):
-        op("v", lambda q: q.tensor_tensor(out, in0, in1, o), r, w)
+    def tt(out, in0, in1, o):
+        op("v", lambda q: q.tensor_tensor(out[0], in0[0], in1[0], o), [in0, in1], [out])
 
-    def cp(out, in_, r, w):
-        op("v", lambda q: q.tensor_copy(out, in_), r, w)
+    def cp(out, in_):
+        op("v", lambda q: q.tensor_copy(out[0], in_[0]), [in_], [out])
 
-    def fill(out, c, w):
-        op("v", lambda q: q.memset(out, c), [], w)
+    def scatter(win, off, in_):
+        op("v", lambda q: q.tensor_copy(win[0].indirect(off[0]), in_[0]), [in_, off], [win])
 
-    def scan(out, d0, d1, first, op0, op1, r, w):
-        op("v", lambda q: q.tensor_tensor_scan(out, d0, d1, first, op0, op1), r, w)
+    def fill(out, c):
+        op("v", lambda q: q.memset(out[0], c), [], [out])
 
-    def quant(qb, sb, in_, r, w):
-        op("v", lambda q: q.quantize_mx(qb, sb, in_), r, w)
+    def scan(out, d0, d1, first, op0, op1):
+        op("v", lambda q: q.tensor_tensor_scan(out[0], d0[0], d1[0], first, op0, op1), [d0, d1], [out])
 
-    def act(out, in_, r, w, func=F.Identity, **kw):
-        op("a", lambda q: q.activation(out, in_, func, **kw), r, w)
+    def quant(qb, sb, in_):
+        op("v", lambda q: q.quantize_mx(qb[0], sb[0], in_[0]), [in_], [qb, sb])
 
-    def iota(out, pattern, base, mult, w, whole=False):
+    def act(out, in_, func=F.Identity, acc=None, after=(), **kw):
+        more = {k: ap(v) for k, v in kw.items()}
+        if acc is not None:
+            more["accum_out"] = acc[0]
+        return op("a", lambda q: q.activation(out[0], in_[0], func, **more), [in_] + list(kw.values()),
+                  [out] + ([acc] if acc is not None else []), after)
+
+    def iota(out, pattern, base, mult, whole=False, after=()):
         if whole:
-            op("g", lambda q: q.iota(out, pattern, base, mult), [], w)
+            op("g", lambda q: q.iota(out[0], pattern, base, mult), [], [out], after)
         else:
-            op("g", lambda q: q.iota(out, pattern, base, mult, allow_small_or_imprecise_dtypes=True), [], w)
+            op("g", lambda q: q.iota(out[0], pattern, base, mult, allow_small_or_imprecise_dtypes=True), [], [out], after)
 
-    def bank(b, n, first=0):
-        return T.ps[:, 512 * b + first:512 * b + n]
+    def bank(b, n):
+        return V("ps", 512 * b, 512 * b + n)
 
-    def mm(b, n, lq, ls, rq, rs, r):
-        op("t", lambda q: q.matmul_mx(bank(b, n), lq, ls, rq, rs, True, True), r, ["b%d" % b])
+    def mm(b, n, lq, ls, rq, rs):
+        out = bank(b, n)
+        op("t", lambda q: q.matmul_mx(out[0], lq[0], ls[0], rq[0], rs[0], True, True), [lq, ls, rq, rs], [out])
 
-    col = lambda i: T.col[:, i:i + 1]
-    QC, GC, SC, PW0, PW, PH, CB4, CR4, CB16, CR16, MQ = range(11)
-    u8 = dt.uint8
-    cols = [slice(CC[h], CC[h + 1]) for h in range(2)]
-    wide = [slice(4 * CC[h], 4 * CC[h + 1]) for h in range(2)]
-    lists = [slice(KC[h], KC[h + 1]) for h in range(2)]
-    nc = [CC[h + 1] - CC[h] for h in range(2)]
-    nk = [KC[h + 1] - KC[h] for h in range(2)]
+    col = lambda i: V("col", i, i + 1)
+    QC, GC, SC, PW0, PW1, PW, PH, CB4, CR4, CB16, CR16 = range(11)
+    cols = lambda name, h: V(name, CC[h], CC[h + 1])
+    wide = lambda name, h: V(name, 4 * CC[h], 4 * CC[h + 1])
+    lst = lambda name, h: V(name, KC[h], KC[h + 1])
+    half = lambda name, h, i: V(name, 2 * KC[h] + NK[h] * i, 2 * KC[h] + NK[h] * (i + 1))
+    third = lambda name, h, i, j: V(name, 3 * KC[h] + NK[h] * i, 3 * KC[h] + NK[h] * j)
+    piece = lambda name, b: V(name, 128 * b, 128 * (b + 1))
+    hbm = lambda t: (t, [])
 
-    dma("s", T.xin[:, wide[0]], T.x[:, wide[0]], [], ["x0h0"])
-    dma("a", T.ut[:], T.u[:], [], ["ut"])
-    dma("s", T.xin[:, wide[1]], T.x[:, wide[1]], [], ["x0h1"])
-    dma("s", T.wq[:].bitcast(u8), T.wc[:], [], ["wq"])
-    dma("s", T.wp[:], T.ws[:], [], ["wp"])
-    dma("s", T.vt[:], T.v[:], [], ["vt"])
+    dma("s", wide("xin", 0), hbm(T.x[:, 0:4 * CC[1]]))
+    dma("a", V("ut"), hbm(T.u[:]))
+    dma("s", wide("xin", 1), hbm(T.x[:, 4 * CC[1]:4 * C]))
+    dma("s", raw(V("wq")), hbm(T.wc[:]))
+    dma("s", V("wp"), hbm(T.ws[:]))
+    dma("s", V("vt"), hbm(T.v[:]))
 
-    iota(T.pi[:, 0:1], [[0, 1]], 0, 1, ["pi0"], whole=True)
-    iota(T.r16[:], [[1, 16]], 0, 0, ["r16"])
-    iota(T.gm[:], [[1, 8], [0, 4]], 0, 0, ["gm"])
-    iota(T.t4[:], [[0, K], [int(2 * B4), 4]], 0, 0, ["t4"])
-    iota(T.c16[:], [[16, K]], 0, 0, ["c16"])
-    iota(T.ramp[:], [[1, SLOTS]], 0, 0, ["ramp"])
-    act(T.enc[:], T.ramp[:], ["ramp"], ["enc"], func=F.Exp, scale=SPREAD)
-    act(T.ones[:], T.ramp[:, 0:512], ["ramp"], ["ones"], scale=0.0, bias=1.0)
-    fill(T.kt[:], 0.0, ["kt"])
-    ts(T.pi[:, 1:2], T.pi[:, 0:1], 15, A.bitwise_and, None, None, ["pi0"], ["pi1"])
-    ts(T.pi[:, 2:3], T.pi[:, 0:1], 4, A.arith_shift_right, None, None, ["pi0"], ["pi2"])
-    ts(T.pi[:, 3:4], T.pi[:, 0:1], 2, A.arith_shift_right, 3, A.bitwise_and, ["pi0"], ["pi3"])
-    fill(T.bits[:, CC[1]:512], 0.0, ["bits1"])
-    cp(T.col[:, 0:3], T.pi[:, 1:4], ["pi1", "pi2", "pi3"], ["col"])
-    ts(T.k16[:], T.r16[:], col(QC), A.is_lt, 1.0, A.add, ["r16", "col"], ["k16"])
-    ts(col(CB4), col(SC), -2 * B4, A.mult, B4, A.add, ["col"], ["cb4"])
-    op("v", lambda q: q.tensor_reduce(col(PW0), T.k16[:], AxisListType.X, A.mult), ["k16"], ["pw0"])
-    ts(col(CR4), col(SC), B4, A.mult, -5 * B4, A.add, ["col"], ["cr4"])
-    ts(col(PW), col(QC), 10.0, A.is_lt, col(PW0), A.mult, ["col", "pw0"], ["pw"])
-    ts(T.d4[:, 0:4 * K], T.t4[:], col(CB4), A.add, B4, A.min, ["t4", "cb4"], ["d4a"])
-    for r in range(4):
-        ts(T.kt[:, 5 * r:512:16], T.gm[:], col(GC), A.is_equal, col(PW), A.mult, ["gm", "col", "pw", "kt"], ["ka%d" % r])
-    ts(T.d4[:, 3:4 * K:4], T.d4[:, 3:4 * K:4], col(CR4), A.add, None, None, ["cr4"], ["d4a"])
-    quant(T.kq[:, 0:128], T.ks[:, 0:128], T.kt[:, 0:512], ["ka%d" % r for r in range(4)], ["kq0"])
-    quant(T.uq[:], T.us[:], T.ut[:], ["ut"], ["uq"])
+    iota(V("pi", 0, 1), [[0, 1]], 0, 1, whole=True)
+    iota(V("r16"), [[1, 16]], 0, 0)
+    iota(V("gm"), [[1, 8], [0, 4]], 0, 0)
+    iota(V("c16"), [[16, K]], 0, 0)
+    iota(V("t4"), [[0, 2 * K], [int(2 * B4), 4]], 0, 0)
+    iota(V("ramp", 0, 512), [[1, 512]], 0, 0)
+    iota(V("ramp", 512, SLOTS), [[1, 512]], 512, 0)
+    iota(V("r1"), [[0, WK], [1, 16]], 0, 0)
+    iota(V("t16"), [[0, WK], [S16, 16]], 0, 0)
+    fill(V("bits", CC[1] - 4), 0.0)
+    warm = act(V("ones"), V("bits", CC[1] - 4), func=F.Tanh, bias=SHARP)
+    fill(V("kt"), 0.0)
+    ts(V("pi", 1, 2), V("pi", 0, 1), 15, A.bitwise_and)
+    ts(V("pi", 2, 3), V("pi", 0, 1), 4, A.arith_shift_right)
+    ts(V("pi", 3, 4), V("pi", 0, 1), 2, A.arith_shift_right, 3, A.bitwise_and)
+    cp(V("col", 0, 3), V("pi", 1, 4))
+    ts(V("k16"), V("r16"), col(QC), A.is_lt, 1.0, A.add)
+    op("v", lambda q: q.tensor_reduce(T.col[:, PW0:PW0 + 1], T.k16[:], AxisListType.X, A.mult, negate=True), [V("k16")], [col(PW0)])
+    ts(col(PW1), col(QC), 10.0, A.is_lt, 0.5, A.mult)
+    ts(col(PW), col(PW1), col(PW0), A.mult)
+    ts(col(PH), col(QC), 10.0, A.is_equal, -256.0, A.mult)
+    for i, w in enumerate((PW, PH)):
+        for r in range(4):
+            ts(V("kt", 512 * i + 5 * r, 512 * (i + 1), 16), V("gm"), col(GC), A.is_equal, col(w), A.mult)
+        quant(piece("kq", i), piece("ks", i), V("kt", 512 * i, 512 * (i + 1)))
+    act(col(CB4), col(SC), scale=-2 * B4, bias=B4)
+    act(col(CR4), col(SC), scale=B4, bias=-5 * B4)
+    fill(V("jx"), 511.5)
+    for h in range(2):
+        ts(half("jx", h, 1), lst("c16", h), col(QC), A.add, 256.0 + BIAS, A.add)
+    ts(V("d4"), V("t4"), col(CB4), A.add, B4, A.min)
+    act(V("jy"), V("jx"), scale=1.0, bias=col(CR4))
+    tt(V("d4", 3, 8 * K, 4), V("d4", 3, 8 * K, 4), V("jy"), A.add)
+    quant(V("uq"), V("us"), V("ut"))
+    quant(V("vq"), V("vs"), V("vt"))
+    act(V("jn"), V("jx"), scale=-1.0, bias=B4 + B16 + SLOTS + 256.0 - BIAS)
+    ts(V("jd"), V("c16"), col(QC), A.add, float(DUMP), A.add)
+    act(col(CB16), col(QC), scale=-float(S16), bias=B16)
+    act(col(CR16), col(QC), scale=B16, bias=-17 * B16)
+    ts(V("cl"), V("c16", 0, WK), 1.0 / 16, A.mult)
+    fill(V("dn", C, 4 * DW, DW), 0.0)
+    fill(V("acc", 0, K, KC[1]), 0.0)
+    ts(V("m1"), V("r1"), col(QC), A.is_equal, STEP * NEAR, A.mult)
+    ts(V("mask"), V("m1"), 1.0, A.max)
+    fill(V("mask", 0, WC, 16), 0.0)
+    ts(V("d16"), V("t16"), col(CB16), A.add, B16, A.min)
+    ts(V("d16", 15, WC, 16), V("d16", 15, WC, 16), col(CR16), A.add)
+    op("g", lambda q: q.affine_select(T.et[:], T.ones[:], [[1, 516]], A.is_equal, 0.0, -3, -4), [V("ones")], [V("et")])
+    for b in range(4):
+        quant(piece("eq4", b), piece("es", b), V("et", 3 - b, 515 - b))
 
-    def constants(i):
-        if i == 0:
-            ts(col(PH), col(QC), 10.0, A.is_equal, 512.0, A.mult, ["col"], ["ph"])
-            ts(T.jw[:], T.c16[:], col(QC), A.add, None, None, ["c16", "col"], ["jw"])
-            ts(T.d4[:, 4 * K:8 * K], T.t4[:], col(CB4), A.add, B4, A.min, ["t4", "cb4"], ["d4v"])
-        elif i == 1:
-            ts(T.jc[:], T.jw[:], col(CR4), A.add, None, None, ["jw", "cr4"], ["jc"])
-            for r in range(2):
-                ts(T.kt[:, 512 + 5 * r:1024:16], T.gm[:], col(GC), A.is_equal, col(PH), A.mult, ["gm", "col", "ph", "kt"], ["kh%d" % r])
-        elif i == 2:
-            for r in range(2, 4):
-                ts(T.kt[:, 512 + 5 * r:1024:16], T.gm[:], col(GC), A.is_equal, col(PH), A.mult, ["gm", "col", "ph", "kt"], ["kh%d" % r])
-            tt(T.d4[:, 4 * K + 3::4], T.d4[:, 4 * K + 3::4], T.jc[:], A.add, ["jc"], ["d4v"])
-        elif i == 3:
-            quant(T.kq[:, 128:256], T.ks[:, 128:256], T.kt[:, 512:1024], ["kh%d" % r for r in range(4)], ["kq1"])
-        elif i == 4:
-            ts(T.jn[:], T.jw[:], -1.0, A.mult, B4 + B16 + SLOTS, A.add, ["jw"], ["jn"])
-            ts(col(MQ), col(QC), float(TAIL - 16), A.add, None, None, ["col"], ["mq"])
-            ts(col(CB16), col(QC), -float(S16), A.mult, B16, A.add, ["col"], ["cb16"])
-        elif i == 5:
-            ts(col(CR16), col(QC), B16, A.mult, -17 * B16, A.add, ["col"], ["cr16"])
-            fill(T.dn[:, C::DW], 0.0, ["dzero"])
-        elif i == 6:
-            fill(T.acc[:, 0:8], 0.0, ["acc0"])
-            ts(T.mtmp[:], T.ramp[:, 0:TAIL], col(MQ), A.is_equal, MUL - 1.0, A.mult, ["ramp", "mq"], ["mtmp"])
-        else:
-            ts(T.d16[:], T.t16[:], col(CB16), A.add, B16, A.min, ["t16", "cb16"], ["d16"])
-            ts(T.mask[:], T.mtmp[:], 1.0, A.add, None, None, ["mtmp"], ["mask"])
-            ts(T.d16[:, 15::16], T.d16[:, 15::16], col(CR16), A.add, None, None, ["cr16"], ["d16"])
+    def clear(t, after=()):
+        for lo, n in ((0, 512), (512, 512), (STEP - 8, 516), (STEP + 508, 516)):
+            if t == 1:
+                iota(V("tab%d" % t, lo, lo + n), [[0, n]], int(EMPTY), 0, after=after)
+            else:
+                act(V("tab%d" % t, lo, lo + n), V("ones", 0, n), scale=EMPTY)
 
-    def unit_tile(b):
-        op("g", lambda q: q.affine_select(T.et[:, 512 * b:512 * (b + 1)], T.ones[:], [[1, 512]], A.is_equal, 0.0, -b, -4), ["ones"], ["e%d" % b])
-
-    state = [T.xin, T.xa, T.xb]
+    state = ["xin", "xa", "xb"]
 
     def quant_state(t, h):
-        quant(T["xq%d" % t][:, cols[h]], T["xs%d" % t][:, cols[h]], state[t][:, wide[h]],
-              ["x%dh%d" % (t, h)] + ["x%dh%db%d" % (t, h, b) for b in range(4)], ["xq%dh%d" % (t, h)])
+        quant(cols("xq%d" % t, h), cols("xs%d" % t, h), wide(state[t], h))
 
-    def scores(t, h):
-        mm(h, nc[h], T.uq[:], T.us[:], T["xq%d" % t][:, cols[h]], T["xs%d" % t][:, cols[h]], ["uq", "xq%dh%d" % (t, h)])
+    def keys(t, h):
+        quant_state(t, h)
+        mm(h, NC[h], V("uq"), V("us"), cols("xq%d" % t, h), cols("xs%d" % t, h))
+        act(cols("bits", h), bank(h, NC[h]), func=F.Sign, bias=TINY)
+        bq, bs = V("bq%d" % h), V("bs%d" % h)
+        quant(bq, bs, V("bits", CC[h], CC[h] + 512))
+        for i in range(2):
+            lo = 8 * KC[h] + 4 * NK[h] * i
+            mm(6 + i, 128, piece("kq", i), piece("ks", i), bq, bs)
+            scan(V("z4", lo, lo + 4 * NK[h]), bank(6 + i, 4 * NK[h]), V("d4", lo, lo + 4 * NK[h]), -B4, A.max, A.add)
+        ts(third("msg%d" % t, h, 0, 2), V("z4", 8 * KC[h] + 3, 8 * KC[h + 1], 4), B4, A.add)
+        send(third("key%d" % t, h, 1 - h, 2), third("msg%d" % t, h, 1 - h, 2))
 
-    def signs(h, on_scalar=False):
-        if on_scalar:
-            act(T.sign[:], bank(h, nc[h]), [], ["b%d" % h, "sign"], func=F.Sign, scale=-1.0)
-            act(T.bits[:, cols[h]], T.sign[:], ["sign"], ["bits%d" % h], func=F.Relu)
-        else:
-            ts(T.bits[:, cols[h]], bank(h, nc[h]), 0.0, A.is_lt, None, None, [], ["b%d" % h, "bits%d" % h])
-
-    def weigh(h):
-        bq, bs = T["bq%d" % h], T["bs%d" % h]
-        quant(bq[:], bs[:], T.bits[:], ["bits0", "bits1"], ["bq%d" % h])
-        for i in range(h + 1):
-            mm(6 + i, 128, T.kq[:, 128 * i:128 * (i + 1)], T.ks[:, 128 * i:128 * (i + 1)], bq[:], bs[:], ["kq%d" % i, "bq%d" % h])
-
-    def select(h):
-        lo, hi = 4 * KC[h], 4 * KC[h + 1]
-        scan(T.z4[:, lo:hi], bank(6, hi, lo), T.d4[:, lo:hi], 0.0, A.max, A.add, ["d4a"], ["b6", "za%d" % h])
-        if h == 1:
-            scan(T.z4[:, 4 * K:8 * K], bank(7, 4 * K), T.d4[:, 4 * K:8 * K], 0.0, A.max, A.add, ["d4v"], ["b7", "zv"])
-
-    def post(t, h):
-        msg, key = T["msg%d" % t], T["key%d" % t]
-        lo, hi = (0, KC[1]) if h == 0 else (KC[1], 2 * K)
-        ts(msg[:, lo:hi], T.z4[:, 4 * lo + 3:4 * hi:4], B4, A.add, None, None, ["za%d" % h] + ["zv"] * h, ["msg%d%d" % (t, h)])
-        send(key[:, lo:hi], msg[:, lo:hi], ["msg%d%d" % (t, h)], ["key%d%d" % (t, h)])
+    def places(t):
+        ts(V("q1"), V("z4", 3, 8 * K, 4), B4 + 1.0, A.add)
+        ts(V("q7"), V("z4", 3, 8 * K, 4), B4 + 7.0, A.add)
+        for h in range(2):
+            lo = 8 * KC[h] + 4 * NK[h]
+            tt(lst("hb", h), V("z4", lo + 3, lo + 4 * NK[h], 4), half("jn", h, 1), A.add)
 
     def layer(t, h):
         for b in range(4):
-            mm(2 + b, nc[h], T.wq[:, 128 * b:128 * (b + 1)], T.wp[:, 128 * b:128 * (b + 1)], T["xq%d" % t][:, cols[h]], T["xs%d" % t][:, cols[h]],
-               ["xq%dh%d" % (t, h), "wq", "wp"])
-            act(T.pt[:, 4 * CC[h] + b:4 * CC[h + 1]:4], bank(2 + b, nc[h]), [], ["b%d" % (2 + b), "p%d%d" % (h, b)], scale=0.03125)
+            mm(2 + b, NC[h], piece("wq", b), piece("wp", b), cols("xq%d" % t, h), cols("xs%d" % t, h))
+            act(V("pt%d" % t, 4 * CC[h] + b, 4 * CC[h + 1], 4), bank(2 + b, NC[h]), scale=0.03125)
+        quant(cols("pq%d" % t, h), cols("pp%d" % t, h), wide("pt%d" % t, h))
+        send(raw(cols("lq%d" % t, h)), raw(cols("pq%d" % t, h)))
+        return send(cols("lp%d" % t, h), cols("pp%d" % t, h))
 
-    def quant_p(t, h):
-        quant(T["pq%d" % t][:, cols[h]], T["pp%d" % t][:, cols[h]], T.pt[:, wide[h]], ["p%d%d" % (h, b) for b in range(4)], ["pq%d%d" % (t, h)])
-
-    def send_p(t, h):
-        send(T["lq%d" % t][:, cols[h]].bitcast(u8), T["pq%d" % t][:, cols[h]].bitcast(u8), ["pq%d%d" % (t, h)], ["lq%d%d" % (t, h)])
-        if h == 1:
-            send(T["lp%d" % t][:], T["pp%d" % t][:], ["pq%d0" % t, "pq%d1" % t], ["lp%d" % t])
-
-    quant_state(0, 0)
-    scores(0, 0)
-    constants(0)
-    signs(0)
-    constants(1)
-    weigh(0)
-    constants(2)
-    select(0)
-    constants(3)
-    post(0, 0)
-    iota(T.t16[:], [[0, KC[1]], [S16, 16]], 0, 0, ["t16"])
-    quant_state(0, 1)
-
-    for t in range(2):
-        msg, key, tab = T["msg%d" % t], T["key%d" % t], T["tab%d" % t]
-        lq, lp = T["lq%d" % t], T["lp%d" % t]
-        more = constants if t == 0 else (lambda i: None)
-
-        scores(t, 1)
-        more(4)
-        if t == 1:
-            quant_p(t, 0)
-        signs(1)
-        more(5)
-        if t == 1:
-            quant(T.vq[:], T.vs[:], T.vt[:], ["vt"], ["vq"])
-        weigh(1)
-        more(6)
-        if t == 0:
-            layer(t, 0)
-        layer(t, 1)
-        select(1)
-        post(t, 1)
-
-        za, zv = T.z4[:, 3:4 * K:4], T.z4[:, 4 * K + 3::4]
-        ts(T.qi[:, 0:K], za, B4 + 1.0, A.add, None, None, ["za0", "za1"], ["qi0"])
-        ts(T.qi[:, K:2 * K], za, B4 + SLOTS - 1.0, A.add, None, None, ["za0", "za1"], ["qi1"])
-        more(7)
-        if t == 0:
-            unit_tile(0)
-            quant_p(t, 0)
-        send_p(t, 0)
-        if t == 0:
-            quant_p(t, 1)
-            send_p(t, 1)
-            for b in range(1, 4):
-                unit_tile(b)
-            iota(T.tab1[:, FB:FB + SLOTS], [[0, SLOTS]], int(EMPTY), 0, ["tabF1"])
-
-        for h in range(2):
-            kk = "key%d%d" % (t, h)
-            rows = range(KC[h], KC[h + 1])
-            cp(T.af[:, lists[h]], key[:, lists[h]], [kk], ["af%d" % h])
-            if h == 1:
-                act(T.ae[:, lists[h]], T.af[:, lists[h]], ["af%d" % h], ["ae%d" % h], func=F.Exp, scale=SPREAD)
-                cp(T.rep[:, cols[h]], T.enc[:].indirect(key[:, lists[h]]), ["enc", kk], ["rep%d" % h])
-                act(T.val[:], T.ramp[:].indirect(key[:, K:2 * K]), ["ramp", kk], ["val"])
-            else:
-                act(T.rep[:, cols[h]], T.enc[:].indirect(key[:, lists[h]]), ["enc", kk], ["rep%d" % h])
-                act(T.ae[:, lists[h]], T.af[:, lists[h]], ["af%d" % h], ["ae%d" % h], func=F.Exp, scale=SPREAD)
-                ts(T.qj[:], T.qi[:], SLOTS - 1, A.bitwise_and, None, None, ["qi0", "qi1"], ["qj"])
-                tt(T.hb[:], zv, T.jn[:], A.add, ["zv", "jn"], ["hb"])
-                if t == 1:
-                    quant_p(t, 1)
-                    send_p(t, 1)
-                cp(T.qo[:], T.qj[:], ["qj"], ["qo"])
-            for c in reversed(rows):
-                ts(T.cmp[:, OFF[c]:OFF[c] + ROW[c]], T.rep[:, 0:ROW[c]], T.ae[:, c:c + 1], A.is_equal, EPS, A.mult,
-                   ["rep%d" % i for i in range(h + 1)] + ["ae%d" % h], ["ch%d" % c, "ct%d" % c])
-            for c in reversed(rows):
-                if ROW[c] > OWN[c]:
-                    head = T.cmp[:, OFF[c]:OFF[c] + ROW[c] - OWN[c]]
-                    act(head, head, ["ct%d" % AHEAD.get(c, c)], ["ch%d" % c, "acc%d" % c], scale=MUL, accum_out=T.acc[:, c:c + 1])
-            if h == 0 and t == 0:
-                act(T.tab0[:, FB:FB + SLOTS], T.ramp[:], ["ramp"], ["tabF0"], scale=0.0, bias=EMPTY)
-                act(T.tab0[:, GB:GB + SLOTS], T.ramp[:], ["ramp"], ["tabG0"], scale=0.0, bias=EMPTY)
-            if h == 1:
-                ts(T.ab[:], T.af[:], float(FB), A.add, None, None, ["af0", "af1"], ["ab"])
-            for c in (list(rows) if h == 1 else [1, 0] + list(rows)[2:]):
-                n, end = OWN[c], OFF[c] + ROW[c]
-                if c == K - 1:
-                    tt(T.s0[:], T.acc[:], T.ab[:], A.add, ["ab", "acc0"] + ["acc%d" % i for i in range(8, K)], ["s0"])
-                scan(T.zs[:, TAIL * (c + 1) - n:TAIL * (c + 1)], T.mask[:, TAIL - n:TAIL], T.cmp[:, end - n:end], 0.0, A.mult, A.add,
-                     ["mask", "ct%d" % c], ["zs%d" % c])
-        if t == 0:
-            act(T.tab1[:, GB:GB + SLOTS], T.ramp[:], ["ramp"], ["tabG1"], scale=0.0, bias=EMPTY)
-        tt(T.s1[:], T.zs[:, TAIL - 1::TAIL], T.s0[:], A.add, ["s0"] + ["zs%d" % c for c in range(K)], ["s1"])
-        tt(T.s2[:], T.s1[:], T.jw[:], A.max, ["s1", "jw"], ["s2"])
-        cp(T.so[:], T.s2[:], ["s2"], ["so"])
-        cp(tab[:].indirect(T.so[:]), T.val[:], ["so", "val"], ["tabF%d" % t, "tabG%d" % t])
-        if t == 0:
-            quant(T.eq4[:], T.es[:], T.et[:], ["e0", "e1", "e2", "e3"], ["eq4"])
-
-        wf, wg = tab[:, FB:FB + SLOTS], tab[:, GB:GB + SLOTS]
-        kf, kg = "tabF%d" % t, "tabG%d" % t
-        span = lambda h, i: slice(2 * CC[h] + nc[h] * i, 2 * CC[h] + nc[h] * (i + 1))
-        few = lambda h, i: slice(2 * KC[h] + nk[h] * i, 2 * KC[h] + nk[h] * (i + 1))
-        for h in range(2):
-            act(T.tf[:, span(h, 0)], wf.indirect(msg[:, lists[h]]), [kf, "msg%d%d" % (t, h)], ["tf%d0" % h], bias=float(SLOTS))
-            act(T.tf[:, span(h, 1)], wf.indirect(T.qo[:, lists[h]]), [kf, "qo"], ["tf%d1" % h], bias=float(SLOTS))
-        for b in range(4):
-            mm(2 + b, C, T.eq4[:, 128 * b:128 * (b + 1)], T.es[:, 128 * b:128 * (b + 1)], lq[:], lp[:],
-               ["eq4", "lq%d0" % t, "lq%d1" % t, "lp%d" % t])
-            act(T.dn[:, DW * b:DW * b + C], bank(2 + b, C), [], ["b%d" % (2 + b), "dn%d" % b])
-
-        def look(h, i):
-            at = T.qo[:, K + KC[h]:K + KC[h + 1]] if i == 0 else msg[:, lists[h]]
-            tt(T.look[:, span(h, i)], wg.indirect(at), T.tf[:, span(h, i)], A.max, [kg, "qo", "msg%d%d" % (t, h), "tf%d%d" % (h, i)], ["lk%d%d" % (h, i)])
-
-        def pick(h, i):
-            scan(T.z16[:, span(h, i)], T.look[:, span(h, i)], T.d16[:, 0:nc[h]], -B16, A.max, A.add, ["lk%d%d" % (h, i), "d16"], ["z16%d%d" % (h, i)])
-
-        def step(h, s):
-            x0, x1, ls, both = few(h, 0), few(h, 1), lists[h], slice(2 * KC[h], 2 * KC[h + 1])
-            if s < 2:
-                sp = span(h, s)
-                tt(T.x1[:, few(h, s)], T.z16[:, sp.start + 15:sp.stop:16], T.hb[:, ls], A.add, ["z16%d%d" % (h, s), "hb"], ["x1%d%d" % (h, s)])
-            elif s == 2:
-                ts(T.x2[:, both], T.x1[:, both], SLOTS - 1, A.bitwise_and, None, None, ["x1%d0" % h, "x1%d1" % h], ["x2%d" % h])
-            elif s == 3:
-                ts(T.x3[:, ls], T.x2[:, x0], float(C), A.is_lt, 4096.0, A.mult, ["x2%d" % h], ["x3%d" % h])
-            elif s == 4:
-                tt(T.x4[:, ls], T.x2[:, x1], T.x3[:, ls], A.max, ["x2%d" % h, "x3%d" % h], ["x4%d" % h])
-            elif s == 5:
-                tt(T.x5[:, ls], T.x2[:, x0], T.x4[:, ls], A.min, ["x2%d" % h, "x4%d" % h], ["x5%d" % h])
-            else:
-                ts(T.fin[:, ls], T.x5[:, ls], float(C), A.min, None, None, ["x5%d" % h], ["fin%d" % h])
-
-        def add(h):
-            for b in range(4):
-                sl = slice(4 * CC[h] + b, 4 * CC[h + 1], 4)
-                tt(state[t + 1][:, sl], T.dn[:, DW * b:DW * b + C + 1].indirect(T.fin[:, lists[h]]), T.pt[:, sl], A.add,
-                   ["dn%d" % b, "dzero", "fin%d" % h, "p%d%d" % (h, b)], ["x%dh%db%d" % (t + 1, h, b)])
-
-        def store(h):
-            dma("s", T.oc[:, wide[h]], T.xq2[:, cols[h]].bitcast(u8), ["xq2h%d" % h], [])
-            mm(h, nc[h], T.vq[:], T.vs[:], T.xq2[:, cols[h]], T.xs2[:, cols[h]], ["vq", "xq2h%d" % h])
-            act(T.yo[:, cols[h]], bank(h, nc[h]), [], ["b%d" % h, "yo%d" % h])
-            dma("a", T.y[:, cols[h]], T.yo[:, cols[h]], ["yo%d" % h], [])
-
-        look(0, 0)
-        look(0, 1)
-        pick(0, 0)
-        pick(0, 1)
-        step(0, 0)
-        step(0, 1)
-        look(1, 0)
-        step(0, 2)
-        look(1, 1)
-        if t == 0:
-            for s in range(3, 7):
-                step(0, s)
-            add(0)
-            pick(1, 0)
-            quant_state(1, 0)
-            scores(1, 0)
-            signs(0, True)
-            pick(1, 1)
-            step(1, 0)
-            step(1, 1)
-            step(1, 2)
-            step(1, 3)
-            step(1, 4)
-            weigh(0)
-            layer(1, 0)
-            step(1, 5)
-            select(0)
-            step(1, 6)
-            post(1, 0)
-            add(1)
-            quant_state(1, 1)
+    def count(t, h):
+        n = NC[h]
+        at, af = third("msg%d" % t, h, 0, 1), V("af%d" % h, 0, NK[h])
+        act(cols("rep", h), by(V("ramp"), at))
+        cp(af, at)
+        act(lst("nb", h), af, scale=-SHARP, bias=EPS)
+        lo = 8 * NK[0] ** 2 * h
+        split, w = NK[h] - ROWS[t][h], WC // 2
+        for c in range(NK[h] - 1, split - 1, -1):
+            e0, s0 = WC * (8 * h + c - split), w * (8 * h + c - split + 1)
+            ts(V("eq", e0, e0 + 16 * c), V("rep", CC[h], CC[h] + 16 * c), V("af%d" % h, c, c + 1), A.is_equal, EPS, A.mult)
+            scan(V("sums", s0 - 8 * c, s0), V("eq", e0, e0 + 8 * c), V("eq", e0 + 8 * c, e0 + 16 * c), 0.0, A.add, A.add)
+        for c in range(split - 1, 0, -1):
+            k = KC[h] + c
+            act(V("junk", lo, lo + 16 * c), V("rep", CC[h], CC[h] + 16 * c), func=F.Tanh, scale=SHARP, bias=V("nb", k, k + 1),
+                acc=V("acc", k, k + 1), after=[warm])
+            lo += 16 * c
+        tt(cols("cmp", h), by(af, V("cl", 0, NK[h])), cols("rep", h), A.is_equal)
+        scan(cols("zs", h), V("mask", 0, n), cols("cmp", h), 0.0, A.mult, A.add)
+        ts(lst("z1", h), V("zs", CC[h] + 15, CC[h + 1], 16), 1.0 / NEAR, A.mult)
+        tt(lst("base", h), lst("z1", h), af, A.add)
+        ts(V("e1", KC[h], KC[h] + split), V("acc", KC[h], KC[h] + split), STEP / EPS, A.mult, 2.0 ** 28 + STEP // 2, A.add)
+        if split < NK[h]:
+            ts(V("e1", KC[h] + split, KC[h + 1]), V("sums", w * (8 * h + 1) - 1, w * (8 * h + NK[h] - split), w), STEP / EPS, A.mult)
+        ts(lst("e2", h), lst("e1", h), 511 * STEP, A.bitwise_and)
+        if h == 0:
+            tt(lst("s1", h), lst("e2", h), lst("base", h), A.add)
+            tt(lst("s2", h), lst("s1", h), lst("jd", h), A.min)
+            cp(third("msg%d" % t, h, 2, 3), lst("s2", h))
+            send(third("key%d" % t, h, 2, 3), third("msg%d" % t, h, 2, 3))
         else:
-            step(0, 3)
-            pick(1, 0)
-            step(0, 4)
-            pick(1, 1)
-            step(0, 5)
-            step(1, 0)
-            step(0, 6)
-            step(1, 1)
-            step(1, 2)
-            add(0)
-            step(1, 3)
-            quant_state(2, 0)
-            store(0)
-            for s in range(4, 7):
-                step(1, s)
-            add(1)
-            quant_state(2, 1)
-            store(1)
-    for k in range(4):
-        dma("s", T.osc[4 * k:4 * k + 4, :], T.xs2[32 * k:32 * k + 4, :], ["xq2h0", "xq2h1"], [])
-    op("g", None, ends, [])
+            tt(V("cnt%d" % t), lst("e2", h), lst("base", h), A.add)
+            send(V("got%d" % t), V("cnt%d" % t))
+
+    def build(t, h):
+        tab, key, n = "tab%d" % t, "key%d" % t, NC[h]
+        (act if h else cp)(cols("val", h), by(V("ramp"), third(key, h, 1, 2)))
+        if h == 0:
+            scatter(V(tab), third(key, h, 2, 3), cols("val", h))
+            return
+        at = third(key, h, 0, 1)
+        act(V("cf", 0, n), by(V(tab, 0, SLOTS), at), func=F.Sign)
+        tt(V("cg", 0, n), by(V(tab, STEP, DUMP), at), V("cf", 0, n), A.max)
+        scan(V("cz", 0, n), V("cg", 0, n), V("d16", 0, n), -B16, A.max, A.add)
+        ts(lst("pen", 1), V("cz", 15, n, 16), B16 + 1.0, A.add, STEP / 2.0, A.mult)
+        tt(lst("s4", h), V("got%d" % t), lst("pen", h), A.add)
+        tt(lst("s5", h), lst("s4", h), lst("jd", h), A.min)
+        cp(lst("so", h), lst("s5", h))
+        scatter(V(tab), lst("so", h), cols("val", h))
+        cp(V(tab, SLOTS, STEP, STEP - 1 - SLOTS), V(tab, 0, DUMP, DUMP - 1))
+
+    def unpack(t):
+        for h in range(2):
+            for b in range(4):
+                mm(2 + b, NC[h], piece("eq4", b), piece("es", b), cols("lq%d" % t, h), cols("lp%d" % t, h))
+                act(V("dn", DW * b + CC[h], DW * b + CC[h + 1]), bank(2 + b, NC[h]))
+
+    def search(t):
+        tab = "tab%d" % t
+        for i in range(2):
+            for h in range(2):
+                at, lo, hi = third("msg%d" % t, h, 0, 1), C * i + CC[h], C * i + CC[h + 1]
+                act(V("tf", lo, hi), by(V(tab, 0, SLOTS), at) if i == 0 else by(V(tab, 0, SLOTS + 1), half("q1", h, 0)), bias=float(SLOTS))
+                tt(V("look", lo, hi), by(V(tab, STEP - 8, DUMP), half("q7", h, 0)) if i == 0 else by(V(tab, STEP, DUMP), at), V("tf", lo, hi), A.max)
+                scan(V("z16", lo, hi), V("look", lo, hi), V("d16", 0, NC[h]), -B16, A.max, A.add)
+            tt(V("x1", K * i, K * (i + 1)), V("z16", C * i + 15, C * (i + 1), 16), V("hb"), A.add)
+        ts(V("x2"), V("x1"), SLOTS - 1, A.bitwise_and)
+        ts(V("x3"), V("x2", 0, K), float(C), A.is_lt, 4096.0, A.mult)
+        tt(V("x4"), V("x2", K, 2 * K), V("x3"), A.max)
+        tt(V("x5"), V("x2", 0, K), V("x4"), A.min)
+        ts(V("fin"), V("x5"), float(C), A.min)
+        for h in range(2):
+            for b in range(4):
+                lo, hi = 4 * CC[h] + b, 4 * CC[h + 1]
+                tt(V(state[t + 1], lo, hi, 4), by(V("dn", DW * b, DW * b + C + 1), lst("fin", h)), V("pt%d" % t, lo, hi, 4), A.add)
+
+    def store(h):
+        quant_state(2, h)
+        dma("s", hbm(T.oc[:, 4 * CC[h]:4 * CC[h + 1]]), raw(cols("xq2", h)))
+        if h == 1:
+            for k in range(4):
+                dma("sa"[k // 2], hbm(T.osc[4 * k:4 * k + 4, :]), (T.xs2[32 * k:32 * k + 4, :], V("xs2")[1]))
+        mm(h, NC[h], V("vq"), V("vs"), cols("xq2", h), cols("xs2", h))
+        act(cols("yo", h), bank(h, NC[h]))
+        dma("a", hbm(T.y[:, CC[h]:CC[h + 1]]), cols("yo", h))
+
+    clear(0)
+    for t in range(2):
+        keys(t, 0)
+        layer(t, 0)
+        keys(t, 1)
+        last = layer(t, 1)
+        places(t)
+        if t == 0:
+            clear(1, [last])
+        count(t, 0)
+        count(t, 1)
+        build(t, 0)
+        build(t, 1)
+        unpack(t)
+        search(t)
+    store(0)
+    store(1)
+    op("g", None, [], [], after=ends)
     schedule(g, T, ops)

@@ -17,7 +17,7 @@ B4, B16, S16 = 2048.0, 2000.0, 4096
 SHARP, EPS = 16.0, 2.0 ** -9
 NEAR = 64.0
 TINY = 2.0 ** -110
-ROWS = [[3, 4], [1, 3]]
+ROWS = [[4, 5], [4, 4]]
 HALF = "float16"
 Q4 = "float8_e4m3fn_x4"
 
@@ -48,10 +48,10 @@ SCRATCH = {
     "eq": ("sbuf", [128, 16 * WC], "bfloat16"), "sums": ("sbuf", [128, 8 * WC], "bfloat16"),
     "cmp": ("sbuf", [128, C], "bfloat16"), "zs": ("sbuf", [128, C], "bfloat16"),
     "cf": ("sbuf", [128, WC], "float32"), "cg": ("sbuf", [128, WC], HALF), "cz": ("sbuf", [128, WC], HALF),
-    "z1": ("sbuf", [128, K], "float32"), "base": ("sbuf", [128, K], "float32"), "pen": ("sbuf", [128, K], "float32"),
+    "z1": ("sbuf", [128, K], "float32"), "base": ("sbuf", [128, K], "float32"), "pen": ("sbuf", [128, 2 * NK[1]], "float32"),
     "e1": ("sbuf", [128, K], "int32"), "e2": ("sbuf", [128, K], "int32"),
-    "s1": ("sbuf", [128, K], "float32"), "s2": ("sbuf", [128, K], "float32"), "s4": ("sbuf", [128, K], "float32"),
-    "s5": ("sbuf", [128, K], "float32"), "so": ("sbuf", [128, K], "uint16"),
+    "s1": ("sbuf", [128, K], "float32"), "s2": ("sbuf", [128, K], "float32"), "s4": ("sbuf", [128, 2 * NK[1]], "float32"),
+    "so": ("sbuf", [128, K], "uint16"),
     "tf": ("sbuf", [128, 2 * C], "float32"), "look": ("sbuf", [128, 2 * C], HALF), "z16": ("sbuf", [128, 2 * C], HALF),
     "x1": ("sbuf", [128, 2 * K], "int32"), "x2": ("sbuf", [128, 2 * K], "int32"),
     "x3": ("sbuf", [128, K], "float32"), "x4": ("sbuf", [128, K], "float32"), "x5": ("sbuf", [128, K], "float32"),
@@ -71,14 +71,14 @@ for _t in range(2):
     SCRATCH["lp%d" % _t] = ("sbuf", [128, C], "uint8")
     SCRATCH["msg%d" % _t] = ("sbuf", [128, 3 * K], "uint16")
     SCRATCH["key%d" % _t] = ("sbuf", [128, 3 * K], "uint16")
-    SCRATCH["cnt%d" % _t] = ("sbuf", [128, NK[1]], "float32")
-    SCRATCH["got%d" % _t] = ("sbuf", [128, NK[1]], "float32")
+    SCRATCH["cnt%d" % _t] = ("sbuf", [128, 2 * NK[1]], "float32")
+    SCRATCH["got%d" % _t] = ("sbuf", [128, 2 * NK[1]], "float32")
     SCRATCH["tab%d" % _t] = ("sbuf", [128, DUMP + C], "float32")
 
 SEMAPHORES = (["cv", "ca", "ct", "cg"] + ["d%d" % i for i in range(20)] + ["l%d" % i for i in range(16)]
               + ["r%d" % i for i in range(16)])
 
-ORDER = [7,6,9,8,13,11,10,12,14,15,19,39,18,20,21,17,26,22,24,0,1,2,3,4,5,16,38,37,66,67,41,23,34,33,25,51,30,27,29,54,28,32,35,68,45,36,31,40,42,69,70,43,92,64,71,44,55,93,94,72,74,73,75,76,125,95,98,53,56,52,48,99,96,124,97,127,100,129,156,85,81,79,83,126,50,133,134,141,142,155,139,157,138,137,140,136,135,171,82,172,80,174,84,86,168,166,169,170,167,173,143,131,128,144,132,130,175,148,145,162,146,164,147,160,149,176,150,163,177,151,46,152,77,59,61,161,158,62,178,159,63,165,78,185,87,180,153,101,65,103,109,107,105,49,108,106,110,154,102,90,179,181,182,183,186,57,58,60,188,104,88,184,187,47,189,111,190,191,192,193,194,195,119,116,118,196,117,112,114,89,91,216,197,203,199,201,220,217,113,115,223,213,221,218,224,214,222,215,225,219,226,204,198,202,200,227,228,205,206,229,230,231,207,211,209,208,212,210,232,233,235,234,240,241,242,239,243,236,251,255,253,257,244,246,247,245,248,122,123,249,238,293,237,252,256,254,258,259,264,292,294,250,265,300,301,298,303,306,266,308,299,297,304,305,302,307,295,309,267,350,268,277,270,275,279,281,271,269,310,296,272,311,314,313,322,312,315,316,317,318,321,323,332,330,339,335,331,338,337,333,334,336,260,121,273,262,319,120,326,324,328,340,327,341,342,325,329,343,345,344,274,346,347,261,320,351,290,288,276,280,282,278,348,263,353,349,368,364,366,362,367,363,352,283,289,286,284,285,287,354,355,356,357,358,359,360,361,291,381,382,378,379,385,388,374,365,369,370,376,372,375,373,377,371,383,386,389,387,390,380,391,384,392,393,394,395,396,402,403,401,404,398,410,400,397,399,411,416,417,418,405,407,406,412,413,415,408,414,409,419]
+ORDER = [15,6,7,8,13,10,9,11,12,1,16,20,18,19,21,39,17,26,22,24,23,25,0,34,33,45,51,55,29,35,48,28,30,40,27,71,31,32,56,37,2,3,4,5,41,42,36,72,50,67,38,70,73,43,69,95,74,96,97,54,44,57,75,77,76,78,58,79,62,98,129,59,128,84,99,65,64,101,100,102,127,144,139,142,140,145,138,143,146,141,147,130,134,136,103,132,148,137,131,133,135,151,149,152,160,80,81,161,150,159,85,153,170,154,174,179,172,49,176,68,173,178,177,175,162,155,168,156,157,14,104,105,158,180,163,166,181,164,171,167,169,165,182,185,184,183,119,63,186,60,187,108,86,88,82,83,106,52,190,47,191,89,122,87,109,110,112,193,107,113,111,192,188,189,90,91,93,94,92,61,66,194,195,196,197,198,114,115,117,116,118,199,46,200,120,121,217,218,225,226,203,201,205,207,229,221,206,204,208,202,213,211,209,215,214,212,210,216,219,227,220,230,228,222,233,231,223,234,232,224,235,238,236,239,237,240,245,244,243,241,246,242,251,250,249,252,253,254,247,266,262,268,264,257,255,258,256,248,259,263,267,265,53,269,304,275,305,270,276,303,316,277,315,317,319,320,314,318,321,322,308,323,312,278,310,309,306,324,290,286,292,281,279,288,282,280,313,307,311,283,325,327,328,326,329,336,330,337,289,335,351,352,350,347,354,353,346,349,348,331,344,332,355,338,356,342,340,345,339,343,341,359,357,360,358,301,361,362,123,260,126,125,273,284,333,124,261,285,334,365,366,367,291,293,287,368,300,294,302,369,370,299,371,363,297,271,272,364,295,372,373,374,375,274,296,298,392,400,404,396,382,376,380,378,377,381,379,384,386,383,387,390,391,385,388,389,393,401,394,405,402,397,395,403,406,408,398,409,407,399,410,413,411,414,412,415,419,416,421,418,417,420,423,425,426,424,422,427,428,429,430,431,437,432,434,433,436,438,435,439,440]
 
 
 def depend(ops):
@@ -248,7 +248,9 @@ def rank_program(g, core, T, topo):
     wide = lambda name, h: V(name, 4 * CC[h], 4 * CC[h + 1])
     lst = lambda name, h: V(name, KC[h], KC[h + 1])
     half = lambda name, h, i: V(name, 2 * KC[h] + NK[h] * i, 2 * KC[h] + NK[h] * (i + 1))
+    both = lambda name, h: V(name, 2 * KC[h], 2 * KC[h + 1])
     third = lambda name, h, i, j: V(name, 3 * KC[h] + NK[h] * i, 3 * KC[h] + NK[h] * j)
+    pairs = lambda name, i: V(name, i, 2 * NK[1], 2)
     piece = lambda name, b: V(name, 128 * b, 128 * (b + 1))
     hbm = lambda t: (t, [])
 
@@ -298,6 +300,9 @@ def rank_program(g, core, T, topo):
     ts(V("jd"), V("c16"), col(QC), A.add, float(DUMP), A.add)
     act(col(CB16), col(QC), scale=-float(S16), bias=B16)
     act(col(CR16), col(QC), scale=B16, bias=-17 * B16)
+    fill(pairs("pen", 0), 2.0 ** 20)
+    for t in range(2):
+        act(pairs("cnt%d" % t, 1), lst("jd", 1))
     ts(V("cl"), V("c16", 0, WK), 1.0 / 16, A.mult)
     fill(V("dn", C, 4 * DW, DW), 0.0)
     fill(V("acc", 0, K, KC[1]), 0.0)
@@ -352,10 +357,10 @@ def rank_program(g, core, T, topo):
 
     def count(t, h):
         n = NC[h]
-        at, af = third("msg%d" % t, h, 0, 1), V("af%d" % h, 0, NK[h])
-        act(cols("rep", h), by(V("ramp"), at))
-        cp(af, at)
-        act(lst("nb", h), af, scale=-SHARP, bias=EPS)
+        af, za = V("af%d" % h, 0, NK[h]), V("z4", 8 * KC[h] + 3, 8 * KC[h] + 4 * NK[h], 4)
+        act(cols("rep", h), by(V("ramp"), third("msg%d" % t, h, 0, 1)))
+        ts(af, za, B4, A.add)
+        ts(lst("nb", h), za, -SHARP, A.mult, EPS - SHARP * B4, A.add)
         lo = 8 * NK[0] ** 2 * h
         split, w = NK[h] - ROWS[t][h], WC // 2
         for c in range(NK[h] - 1, split - 1, -1):
@@ -372,8 +377,7 @@ def rank_program(g, core, T, topo):
         ts(lst("z1", h), V("zs", CC[h] + 15, CC[h + 1], 16), 1.0 / NEAR, A.mult)
         tt(lst("base", h), lst("z1", h), af, A.add)
         ts(V("e1", KC[h], KC[h] + split), V("acc", KC[h], KC[h] + split), STEP / EPS, A.mult, 2.0 ** 28 + STEP // 2, A.add)
-        if split < NK[h]:
-            ts(V("e1", KC[h] + split, KC[h + 1]), V("sums", w * (8 * h + 1) - 1, w * (8 * h + NK[h] - split), w), STEP / EPS, A.mult)
+        ts(V("e1", KC[h] + split, KC[h + 1]), V("sums", w * (8 * h + 1) - 1, w * (8 * h + NK[h] - split), w), STEP / EPS, A.mult)
         ts(lst("e2", h), lst("e1", h), 511 * STEP, A.bitwise_and)
         if h == 0:
             tt(lst("s1", h), lst("e2", h), lst("base", h), A.add)
@@ -381,12 +385,12 @@ def rank_program(g, core, T, topo):
             cp(third("msg%d" % t, h, 2, 3), lst("s2", h))
             send(third("key%d" % t, h, 2, 3), third("msg%d" % t, h, 2, 3))
         else:
-            tt(V("cnt%d" % t), lst("e2", h), lst("base", h), A.add)
+            tt(pairs("cnt%d" % t, 0), lst("e2", h), lst("base", h), A.add)
             send(V("got%d" % t), V("cnt%d" % t))
 
     def build(t, h):
         tab, key, n = "tab%d" % t, "key%d" % t, NC[h]
-        (act if h else cp)(cols("val", h), by(V("ramp"), third(key, h, 1, 2)))
+        act(cols("val", h), by(V("ramp"), third(key, h, 1, 2)))
         if h == 0:
             scatter(V(tab), third(key, h, 2, 3), cols("val", h))
             return
@@ -394,10 +398,9 @@ def rank_program(g, core, T, topo):
         act(V("cf", 0, n), by(V(tab, 0, SLOTS), at), func=F.Sign)
         tt(V("cg", 0, n), by(V(tab, STEP, DUMP), at), V("cf", 0, n), A.max)
         scan(V("cz", 0, n), V("cg", 0, n), V("d16", 0, n), -B16, A.max, A.add)
-        ts(lst("pen", 1), V("cz", 15, n, 16), B16 + 1.0, A.add, STEP / 2.0, A.mult)
-        tt(lst("s4", h), V("got%d" % t), lst("pen", h), A.add)
-        tt(lst("s5", h), lst("s4", h), lst("jd", h), A.min)
-        cp(lst("so", h), lst("s5", h))
+        ts(pairs("pen", 1), V("cz", 15, n, 16), B16 + 1.0, A.add, STEP / 2.0, A.mult)
+        scan(V("s4"), V("pen"), V("got%d" % t), 0.0, A.add, A.min)
+        cp(lst("so", h), pairs("s4", 1))
         scatter(V(tab), lst("so", h), cols("val", h))
         cp(V(tab, SLOTS, STEP, STEP - 1 - SLOTS), V(tab, 0, DUMP, DUMP - 1))
 
@@ -415,12 +418,13 @@ def rank_program(g, core, T, topo):
                 act(V("tf", lo, hi), by(V(tab, 0, SLOTS), at) if i == 0 else by(V(tab, 0, SLOTS + 1), half("q1", h, 0)), bias=float(SLOTS))
                 tt(V("look", lo, hi), by(V(tab, STEP - 8, DUMP), half("q7", h, 0)) if i == 0 else by(V(tab, STEP, DUMP), at), V("tf", lo, hi), A.max)
                 scan(V("z16", lo, hi), V("look", lo, hi), V("d16", 0, NC[h]), -B16, A.max, A.add)
-            tt(V("x1", K * i, K * (i + 1)), V("z16", C * i + 15, C * (i + 1), 16), V("hb"), A.add)
-        ts(V("x2"), V("x1"), SLOTS - 1, A.bitwise_and)
-        ts(V("x3"), V("x2", 0, K), float(C), A.is_lt, 4096.0, A.mult)
-        tt(V("x4"), V("x2", K, 2 * K), V("x3"), A.max)
-        tt(V("x5"), V("x2", 0, K), V("x4"), A.min)
-        ts(V("fin"), V("x5"), float(C), A.min)
+                tt(half("x1", h, i), V("z16", lo + 15, hi, 16), lst("hb", h), A.add)
+        for h in range(2):
+            ts(both("x2", h), both("x1", h), SLOTS - 1, A.bitwise_and)
+            ts(lst("x3", h), half("x2", h, 0), float(C), A.is_lt, 4096.0, A.mult)
+            tt(lst("x4", h), half("x2", h, 1), lst("x3", h), A.max)
+            tt(lst("x5", h), half("x2", h, 0), lst("x4", h), A.min)
+            ts(lst("fin", h), lst("x5", h), float(C), A.min)
         for h in range(2):
             for b in range(4):
                 lo, hi = 4 * CC[h] + b, 4 * CC[h + 1]

@@ -9,15 +9,24 @@ NC = [16 * k for k in NK]
 WK, WC = max(NK), max(NC)
 SLOTS = 1024
 DW = 464
-STEP = 2048
+STEP = 4096
 DUMP = STEP + SLOTS
-EMPTY = -1025.0
-BIAS = 3.0
-B4, B16, S16 = 2048.0, 2000.0, 4096
+TW = 5576
 SHARP, EPS = 16.0, 2.0 ** -9
-NEAR = 64.0
+UNIT = EPS / STEP
+GROW = (STEP + 1) / STEP / UNIT
+B4 = 1536 * UNIT
+WHOLE, GRID, TUP = 3 * 2 ** 22, 3 * 2 ** 13, 10
+EMPTY = -1024.0
+BIAS = 16.0
+B16, S16 = 2000.0, 4096
+DROP = 2 * SLOTS + BIAS
+NEAR = UNIT / 128
 TINY = 2.0 ** -110
-ROWS = [[4, 5], [4, 4]]
+ROWS = [[4, 4], [4, 4]]
+CLEAR_G = ()
+SPLIT = True
+UNV = [0, 0]
 HALF = "float16"
 Q4 = "float8_e4m3fn_x4"
 
@@ -35,27 +44,25 @@ SCRATCH = {
     "ps": ("psum", [128, 4096], "float32"),
     "pi": ("sbuf", [128, 8], "int32"), "col": ("sbuf", [128, 16], "float32"), "k16": ("sbuf", [128, 16], "float32"),
     "gm": ("sbuf", [128, 32], "float32"), "r16": ("sbuf", [128, 16], "float32"), "c16": ("sbuf", [128, K], "float32"),
-    "t4": ("sbuf", [128, 8 * K], "float32"), "d4": ("sbuf", [128, 8 * K], "float32"),
+    "t4": ("sbuf", [128, 8 * K], "float32"), "t5": ("sbuf", [128, 8 * K], "float32"), "d4": ("sbuf", [128, 8 * K], "float32"),
     "jx": ("sbuf", [128, 2 * K], "float32"), "jy": ("sbuf", [128, 2 * K], "float32"),
-    "t16": ("sbuf", [128, WC], "bfloat16"), "d16": ("sbuf", [128, WC], HALF),
+    "t16": ("sbuf", [128, WC], "bfloat16"), "d16": ("sbuf", [128, WC], HALF), "d8": ("sbuf", [128, WC], HALF),
     "r1": ("sbuf", [128, WC], "bfloat16"), "m1": ("sbuf", [128, WC], "bfloat16"), "mask": ("sbuf", [128, WC], "bfloat16"),
     "ramp": ("sbuf", [128, SLOTS], "float32"), "cl": ("sbuf", [128, WK], "uint16"),
-    "jd": ("sbuf", [128, K], "float32"), "jn": ("sbuf", [128, 2 * K], "float32"),
-    "z4": ("sbuf", [128, 8 * K], "float32"), "q1": ("sbuf", [128, 2 * K], "uint16"), "q7": ("sbuf", [128, 2 * K], "uint16"),
-    "hb": ("sbuf", [128, K], "float32"), "nb": ("sbuf", [128, K], "float32"),
+    "warm": ("sbuf", [128, 16], "float32"),
+    "z4": ("sbuf", [128, 8 * K], "float32"),
+    "hb": ("sbuf", [128, 2 * K], "float32"), "nb": ("sbuf", [128, K], "float32"),
     "rep": ("sbuf", [128, C], "float32"), "val": ("sbuf", [128, C], "float32"),
-    "junk": ("sbuf", [128, 8 * (NK[0] ** 2 + NK[1] ** 2)], "bfloat16"), "acc": ("sbuf", [128, K], "float32"),
+    "junk": ("sbuf", [128, 8 * (NK[0] ** 2 + NK[1] ** 2)], "bfloat16"),
+    "acc": ("sbuf", [128, TUP * K], "float32"), "pl": ("sbuf", [128, TUP * K], "float32"),
     "eq": ("sbuf", [128, 16 * WC], "bfloat16"), "sums": ("sbuf", [128, 8 * WC], "bfloat16"),
     "cmp": ("sbuf", [128, C], "bfloat16"), "zs": ("sbuf", [128, C], "bfloat16"),
     "cf": ("sbuf", [128, WC], "float32"), "cg": ("sbuf", [128, WC], HALF), "cz": ("sbuf", [128, WC], HALF),
-    "z1": ("sbuf", [128, K], "float32"), "base": ("sbuf", [128, K], "float32"), "pen": ("sbuf", [128, 2 * NK[1]], "float32"),
-    "e1": ("sbuf", [128, K], "int32"), "e2": ("sbuf", [128, K], "int32"),
-    "s1": ("sbuf", [128, K], "float32"), "s2": ("sbuf", [128, K], "float32"), "s4": ("sbuf", [128, 2 * NK[1]], "float32"),
     "so": ("sbuf", [128, K], "uint16"),
     "tf": ("sbuf", [128, 2 * C], "float32"), "look": ("sbuf", [128, 2 * C], HALF), "z16": ("sbuf", [128, 2 * C], HALF),
     "x1": ("sbuf", [128, 2 * K], "int32"), "x2": ("sbuf", [128, 2 * K], "int32"),
-    "x3": ("sbuf", [128, K], "float32"), "x4": ("sbuf", [128, K], "float32"), "x5": ("sbuf", [128, K], "float32"),
-    "fin": ("sbuf", [128, K], "uint16"), "yo": ("sbuf", [128, C], "float32"),
+    "x3": ("sbuf", [128, 2 * K], "float32"), "x4": ("sbuf", [128, 2 * K], "float32"), "x5": ("sbuf", [128, 2 * K], "float32"),
+    "yo": ("sbuf", [128, C], "float32"),
 }
 for _t in range(3):
     SCRATCH["xq%d" % _t] = ("sbuf", [128, C], Q4)
@@ -63,7 +70,6 @@ for _t in range(3):
 for _t in range(2):
     SCRATCH["bq%d" % _t] = ("sbuf", [128, 128], Q4)
     SCRATCH["bs%d" % _t] = ("sbuf", [128, 128], "uint8")
-    SCRATCH["af%d" % _t] = ("sbuf", [128, WK], "float32")
     SCRATCH["pt%d" % _t] = ("sbuf", [128, 4 * C], "bfloat16")
     SCRATCH["pq%d" % _t] = ("sbuf", [128, C], Q4)
     SCRATCH["pp%d" % _t] = ("sbuf", [128, C], "uint8")
@@ -71,14 +77,14 @@ for _t in range(2):
     SCRATCH["lp%d" % _t] = ("sbuf", [128, C], "uint8")
     SCRATCH["msg%d" % _t] = ("sbuf", [128, 3 * K], "uint16")
     SCRATCH["key%d" % _t] = ("sbuf", [128, 3 * K], "uint16")
-    SCRATCH["cnt%d" % _t] = ("sbuf", [128, 2 * NK[1]], "float32")
-    SCRATCH["got%d" % _t] = ("sbuf", [128, 2 * NK[1]], "float32")
-    SCRATCH["tab%d" % _t] = ("sbuf", [128, DUMP + C], "float32")
+    SCRATCH["fin%d" % _t] = ("sbuf", [128, K], "uint16")
+    SCRATCH["got%d" % _t] = ("sbuf", [128, K], "uint16")
+    SCRATCH["tab%d" % _t] = ("sbuf", [128, TW], "float32")
 
 SEMAPHORES = (["cv", "ca", "ct", "cg"] + ["d%d" % i for i in range(20)] + ["l%d" % i for i in range(16)]
               + ["r%d" % i for i in range(16)])
 
-ORDER = [15,6,7,8,13,10,9,11,12,1,16,20,18,19,21,39,17,26,22,24,23,25,0,34,33,45,51,55,29,35,48,28,30,40,27,71,31,32,56,37,2,3,4,5,41,42,36,72,50,67,38,70,73,43,69,95,74,96,97,54,44,57,75,77,76,78,58,79,62,98,129,59,128,84,99,65,64,101,100,102,127,144,139,142,140,145,138,143,146,141,147,130,134,136,103,132,148,137,131,133,135,151,149,152,160,80,81,161,150,159,85,153,170,154,174,179,172,49,176,68,173,178,177,175,162,155,168,156,157,14,104,105,158,180,163,166,181,164,171,167,169,165,182,185,184,183,119,63,186,60,187,108,86,88,82,83,106,52,190,47,191,89,122,87,109,110,112,193,107,113,111,192,188,189,90,91,93,94,92,61,66,194,195,196,197,198,114,115,117,116,118,199,46,200,120,121,217,218,225,226,203,201,205,207,229,221,206,204,208,202,213,211,209,215,214,212,210,216,219,227,220,230,228,222,233,231,223,234,232,224,235,238,236,239,237,240,245,244,243,241,246,242,251,250,249,252,253,254,247,266,262,268,264,257,255,258,256,248,259,263,267,265,53,269,304,275,305,270,276,303,316,277,315,317,319,320,314,318,321,322,308,323,312,278,310,309,306,324,290,286,292,281,279,288,282,280,313,307,311,283,325,327,328,326,329,336,330,337,289,335,351,352,350,347,354,353,346,349,348,331,344,332,355,338,356,342,340,345,339,343,341,359,357,360,358,301,361,362,123,260,126,125,273,284,333,124,261,285,334,365,366,367,291,293,287,368,300,294,302,369,370,299,371,363,297,271,272,364,295,372,373,374,375,274,296,298,392,400,404,396,382,376,380,378,377,381,379,384,386,383,387,390,391,385,388,389,393,401,394,405,402,397,395,403,406,408,398,409,407,399,410,413,411,414,412,415,419,416,421,418,417,420,423,425,426,424,422,427,428,429,430,431,437,432,434,433,436,438,435,439,440]
+ORDER = [6,15,0,1,2,3,10,4,5,17,21,20,19,8,22,18,7,9,12,25,27,23,16,36,55,38,42,39,40,56,58,24,57,41,43,81,73,49,26,47,45,28,33,74,30,29,82,34,13,44,31,104,83,11,60,35,76,32,105,84,37,61,85,46,106,91,75,86,14,107,88,87,62,53,108,89,130,131,93,64,52,63,109,80,90,92,111,65,110,95,145,132,147,141,149,97,148,143,146,117,136,153,133,134,51,144,138,50,140,137,150,79,142,135,139,114,154,112,151,152,155,164,176,177,157,170,178,159,68,96,113,179,168,166,165,167,160,156,66,172,181,161,163,67,98,182,94,123,173,169,54,162,115,116,158,171,183,180,119,174,175,184,121,99,124,185,120,72,100,101,122,186,78,48,118,187,70,205,102,103,206,188,71,125,210,207,126,127,221,128,129,211,77,225,208,212,209,213,193,214,191,69,215,216,195,192,217,189,222,194,196,218,226,190,219,220,223,203,227,224,199,228,204,197,229,59,200,201,230,231,198,232,202,233,239,234,235,237,236,238,244,242,245,240,260,246,243,254,261,256,247,241,255,248,257,258,249,267,251,259,250,252,268,293,253,294,280,262,269,284,297,309,263,264,303,301,265,266,270,307,304,299,308,312,305,271,311,282,310,306,298,272,302,274,295,286,273,300,313,296,316,275,277,314,315,317,276,339,340,278,279,322,327,341,326,320,329,323,342,334,324,318,344,325,335,328,331,345,330,332,333,343,336,319,321,346,281,337,338,347,285,352,287,348,283,349,358,350,356,354,351,369,368,288,373,291,292,370,289,290,357,374,384,371,355,375,359,372,388,376,377,353,385,379,378,386,380,387,381,389,382,383,360,390,362,361,391,364,392,363,366,393,365,394,395,367,396,399,397,398,400,401,402,407,406,409,408,404,410,403,405,411,412,418,415,416,414,413,419,417,420,421]
 
 
 def depend(ops):
@@ -111,10 +117,11 @@ def depend(ops):
 def schedule(g, T, ops):
     queue = {"v": g.vector, "a": g.scalar, "t": g.tensor, "g": g, "s": g.sync}
     depend(ops)
-    place = {i: k for k, i in enumerate(ORDER)}
-    assert sorted(ORDER) == list(range(len(ops))) and all(place[d] < place[i] for i, o in enumerate(ops) for d in o["deps"])
+    order = ORDER or list(range(len(ops)))
+    place = {i: k for k, i in enumerate(order)}
+    assert sorted(order) == list(range(len(ops))) and all(place[d] < place[i] for i, o in enumerate(ops) for d in o["deps"])
     clock = {e: {} for e in queue}
-    for i in ORDER:
+    for i in order:
         o = ops[i]
         o["waits"] = []
         if o["e"] is not None:
@@ -132,12 +139,12 @@ def schedule(g, T, ops):
             o["snap"] = {}
         o["snap"][o["src"]] = place[i]
     count = {}
-    for i in ORDER:
+    for i in order:
         o = ops[i]
         if o["sem"] is None and o.get("used"):
             count[o["e"]] = count.get(o["e"], 0) + 1
             o["sem"], o["n"], o["inc"] = "c" + o["e"], count[o["e"]], 1
-    for i in ORDER:
+    for i in order:
         o = ops[i]
         if o["e"] is None:
             continue
@@ -155,10 +162,7 @@ def rank_program(g, core, T, topo):
     if rank is None:
         return
     n_ranks = len(T.cores)
-    dst = T.cores[(rank - 1) % n_ranks]
-    src = T.cores[(rank + 1) % n_ranks]
-    rid, pid = topo.addr(dst, core)
-    mask_out, n_out, n_in = topo.mask(core, dst), len(topo.engines(core, dst)), len(topo.engines(src, core))
+    near = {step: T.cores[(rank + step) % n_ranks] for step in (-1, 1)}
     ops, nd, nr, ends = [], [0], [0], []
     u8 = dt.uint8
 
@@ -187,15 +191,17 @@ def rank_program(g, core, T, topo):
         ops[i].update({"src": s, "sem": s, "n": 16, "inc": 16})
         ends.append(i)
 
-    def send(out, in_):
+    def send(step, out, in_):
         k = nr[0]
         nr[0] += 1
         ls, rs = "l%d" % k, "r%d" % k
-        i = op("g", lambda q: q.remote_dma(out[0], in_[0], T.sem[rs], T.sem[ls], pid, rid, mask_out), [in_], [])
-        ops[i].update({"src": ls, "sem": ls, "n": n_out})
+        dst, src = near[step], near[-step]
+        rid, pid = topo.addr(dst, core)
+        i = op("g", lambda q: q.remote_dma(out[0], in_[0], T.sem[rs], T.sem[ls], pid, rid, topo.mask(core, dst)), [in_], [])
+        ops[i].update({"src": ls, "sem": ls, "n": len(topo.engines(core, dst))})
         ends.append(i)
         j = op(None, None, [], [out], after=[i])
-        ops[j].update({"src": rs, "sem": rs, "n": n_in})
+        ops[j].update({"src": rs, "sem": rs, "n": len(topo.engines(src, core))})
         return i
 
     def ts(out, in0, s1, op0, s2=None, op1=None):
@@ -249,8 +255,13 @@ def rank_program(g, core, T, topo):
     lst = lambda name, h: V(name, KC[h], KC[h + 1])
     half = lambda name, h, i: V(name, 2 * KC[h] + NK[h] * i, 2 * KC[h] + NK[h] * (i + 1))
     both = lambda name, h: V(name, 2 * KC[h], 2 * KC[h + 1])
-    third = lambda name, h, i, j: V(name, 3 * KC[h] + NK[h] * i, 3 * KC[h] + NK[h] * j)
-    pairs = lambda name, i: V(name, i, 2 * NK[1], 2)
+    pair = lambda name, h, i: V(name, 2 * KC[h] + i, 2 * KC[h + 1], 2)
+    slot = lambda name, k, lo=0, hi=K: V(name, TUP * lo + k, TUP * (hi - 1) + k + 1, TUP)
+    addr = lambda name, h: half(name, h, 1 - h)
+    entry = lambda name, h: half(name, h, h)
+    beyond = lambda name, h: V(name, 2 * K + KC[h], 2 * K + KC[h + 1])
+    za = lambda h: 8 * KC[h] + 4 * NK[h] * (1 - h)
+    zaddr = lambda h: V("z4", za(h) + 3, za(h) + 4 * NK[h], 4)
     piece = lambda name, b: V(name, 128 * b, 128 * (b + 1))
     hbm = lambda t: (t, [])
 
@@ -265,13 +276,14 @@ def rank_program(g, core, T, topo):
     iota(V("r16"), [[1, 16]], 0, 0)
     iota(V("gm"), [[1, 8], [0, 4]], 0, 0)
     iota(V("c16"), [[16, K]], 0, 0)
-    iota(V("t4"), [[0, 2 * K], [int(2 * B4), 4]], 0, 0)
+    iota(V("t4"), [[0, 2 * K], [2, 4]], 0, 0)
     iota(V("ramp", 0, 512), [[1, 512]], 0, 0)
     iota(V("ramp", 512, SLOTS), [[1, 512]], 512, 0)
-    iota(V("r1"), [[0, WK], [1, 16]], 0, 0)
+    iota(V("r1"), [[0, WK], [1, 16]], 1, 0)
     iota(V("t16"), [[0, WK], [S16, 16]], 0, 0)
-    fill(V("bits", CC[1] - 4), 0.0)
-    warm = act(V("ones"), V("bits", CC[1] - 4), func=F.Tanh, bias=SHARP)
+    fill(V("bits", CC[1], 512), 0.0)
+    fill(V("ones"), 1.0)
+    warm = act(V("warm"), V("bits", CC[1], CC[1] + 16), func=F.Tanh)
     fill(V("kt"), 0.0)
     ts(V("pi", 1, 2), V("pi", 0, 1), 15, A.bitwise_and)
     ts(V("pi", 2, 3), V("pi", 0, 1), 4, A.arith_shift_right)
@@ -279,46 +291,50 @@ def rank_program(g, core, T, topo):
     cp(V("col", 0, 3), V("pi", 1, 4))
     ts(V("k16"), V("r16"), col(QC), A.is_lt, 1.0, A.add)
     op("v", lambda q: q.tensor_reduce(T.col[:, PW0:PW0 + 1], T.k16[:], AxisListType.X, A.mult, negate=True), [V("k16")], [col(PW0)])
-    ts(col(PW1), col(QC), 10.0, A.is_lt, 0.5, A.mult)
+    ts(col(PW1), col(QC), 10.0, A.is_lt, 0.5 * UNIT, A.mult)
     ts(col(PW), col(PW1), col(PW0), A.mult)
-    ts(col(PH), col(QC), 10.0, A.is_equal, -256.0, A.mult)
+    ts(col(PH), col(QC), 10.0, A.is_equal, -256.0 * UNIT, A.mult)
     for i, w in enumerate((PW, PH)):
         for r in range(4):
             ts(V("kt", 512 * i + 5 * r, 512 * (i + 1), 16), V("gm"), col(GC), A.is_equal, col(w), A.mult)
         quant(piece("kq", i), piece("ks", i), V("kt", 512 * i, 512 * (i + 1)))
     act(col(CB4), col(SC), scale=-2 * B4, bias=B4)
     act(col(CR4), col(SC), scale=B4, bias=-5 * B4)
-    fill(V("jx"), 511.5)
+    fill(V("jx", NK[0], NK[0] + K), 511.5)
     for h in range(2):
-        ts(half("jx", h, 1), lst("c16", h), col(QC), A.add, 256.0 + BIAS, A.add)
-    ts(V("d4"), V("t4"), col(CB4), A.add, B4, A.min)
-    act(V("jy"), V("jx"), scale=1.0, bias=col(CR4))
+        ts(entry("jx", h), lst("c16", h), col(QC), A.add, 256.0 + BIAS, A.add)
+    act(V("t5"), V("t4"), scale=B4, bias=col(CB4))
+    ts(V("d4"), V("t5"), B4, A.min)
+    act(V("jy"), V("jx"), scale=UNIT, bias=col(CR4))
     tt(V("d4", 3, 8 * K, 4), V("d4", 3, 8 * K, 4), V("jy"), A.add)
     quant(V("uq"), V("us"), V("ut"))
     quant(V("vq"), V("vs"), V("vt"))
-    act(V("jn"), V("jx"), scale=-1.0, bias=B4 + B16 + SLOTS + 256.0 - BIAS)
-    ts(V("jd"), V("c16"), col(QC), A.add, float(DUMP), A.add)
+    iota(V("acc"), [[0, TUP * K]], GRID, 0)
+    for k, c in ((1, -WHOLE), (2, -WHOLE), (7, WHOLE)):
+        iota(slot("acc", k), [[0, K]], c, 0)
+    for h in range(2):
+        act(slot("acc", 9, KC[h], KC[h + 1]), entry("jx", h), scale=UNIT, bias=(DUMP - 256.0 - BIAS) * UNIT - B4)
+    fill(V("x3", 0, 2 * K, 2), 4096.0)
     act(col(CB16), col(QC), scale=-float(S16), bias=B16)
-    act(col(CR16), col(QC), scale=B16, bias=-17 * B16)
-    fill(pairs("pen", 0), 2.0 ** 20)
-    for t in range(2):
-        act(pairs("cnt%d" % t, 1), lst("jd", 1))
-    ts(V("cl"), V("c16", 0, WK), 1.0 / 16, A.mult)
+    act(col(CR16), col(QC), scale=B16, bias=-16 * B16 - DROP)
+    ts(V("cl"), V("c16", 0, WK), 0.25, A.mult, 3.0, A.add)
     fill(V("dn", C, 4 * DW, DW), 0.0)
-    fill(V("acc", 0, K, KC[1]), 0.0)
-    ts(V("m1"), V("r1"), col(QC), A.is_equal, STEP * NEAR, A.mult)
+    fill(V("acc", 3, TUP * K, TUP * KC[1]), 0.0)
+    ts(V("m1"), V("r1"), col(QC), A.is_equal, EPS / NEAR, A.mult)
     ts(V("mask"), V("m1"), 1.0, A.max)
-    fill(V("mask", 0, WC, 16), 0.0)
+    ts(V("mask", 14, WC, 16), V("mask", 14, WC, 16), NEAR, A.mult)
+    fill(V("mask", 15, WC, 16), 0.0)
     ts(V("d16"), V("t16"), col(CB16), A.add, B16, A.min)
     ts(V("d16", 15, WC, 16), V("d16", 15, WC, 16), col(CR16), A.add)
+    ts(V("d8"), V("d16"), 0.5, A.mult)
     op("g", lambda q: q.affine_select(T.et[:], T.ones[:], [[1, 516]], A.is_equal, 0.0, -3, -4), [V("ones")], [V("et")])
     for b in range(4):
         quant(piece("eq4", b), piece("es", b), V("et", 3 - b, 515 - b))
 
-    def clear(t, after=()):
-        for lo, n in ((0, 512), (512, 512), (STEP - 8, 516), (STEP + 508, 516)):
-            if t == 1:
-                iota(V("tab%d" % t, lo, lo + n), [[0, n]], int(EMPTY), 0, after=after)
+    def clear(t):
+        for lo, n in ((0, 512), (512, 512), (STEP, 512), (STEP + 512, 513)):
+            if t == 1 or lo in CLEAR_G:
+                iota(V("tab%d" % t, lo, lo + n), [[0, n]], int(EMPTY), 0)
             else:
                 act(V("tab%d" % t, lo, lo + n), V("ones", 0, n), scale=EMPTY)
 
@@ -330,105 +346,93 @@ def rank_program(g, core, T, topo):
     def keys(t, h):
         quant_state(t, h)
         mm(h, NC[h], V("uq"), V("us"), cols("xq%d" % t, h), cols("xs%d" % t, h))
-        act(cols("bits", h), bank(h, NC[h]), func=F.Sign, bias=TINY)
-        bq, bs = V("bq%d" % h), V("bs%d" % h)
+        act(V("bits", 512 * h, 512 * h + NC[h]), bank(h, NC[h]), func=F.Sign, bias=TINY)
+        bq, bs, pad = V("bq%d" % h), V("bs%d" % h), (128 - 4 * NK[h]) * h
         quant(bq, bs, V("bits", CC[h], CC[h] + 512))
         for i in range(2):
-            lo = 8 * KC[h] + 4 * NK[h] * i
+            lo = 8 * KC[h] + 4 * NK[h] * (i if h else 1 - i)
             mm(6 + i, 128, piece("kq", i), piece("ks", i), bq, bs)
-            scan(V("z4", lo, lo + 4 * NK[h]), bank(6 + i, 4 * NK[h]), V("d4", lo, lo + 4 * NK[h]), -B4, A.max, A.add)
-        ts(third("msg%d" % t, h, 0, 2), V("z4", 8 * KC[h] + 3, 8 * KC[h + 1], 4), B4, A.add)
-        send(third("key%d" % t, h, 1 - h, 2), third("msg%d" % t, h, 1 - h, 2))
-
-    def places(t):
-        ts(V("q1"), V("z4", 3, 8 * K, 4), B4 + 1.0, A.add)
-        ts(V("q7"), V("z4", 3, 8 * K, 4), B4 + 7.0, A.add)
-        for h in range(2):
-            lo = 8 * KC[h] + 4 * NK[h]
-            tt(lst("hb", h), V("z4", lo + 3, lo + 4 * NK[h], 4), half("jn", h, 1), A.add)
+            scan(V("z4", lo, lo + 4 * NK[h]), V("ps", 512 * (6 + i) + pad, 512 * (6 + i) + pad + 4 * NK[h]), V("d4", lo, lo + 4 * NK[h]), -B4, A.max, A.add)
+            if SPLIT:
+                ts((entry if i else addr)("msg%d" % t, h), V("z4", lo + 3, lo + 4 * NK[h], 4), B4, A.add, 1 / UNIT, A.mult)
+        if not SPLIT:
+            ts(both("msg%d" % t, h), V("z4", 8 * KC[h] + 3, 8 * KC[h + 1], 4), B4, A.add, 1 / UNIT, A.mult)
+        if h == 1:
+            ts(V("msg%d" % t, 2 * K), V("z4", za(0) + 3, za(1) + 4 * NK[1], 4), B4 + UNIT, A.add, 1 / UNIT, A.mult)
+            send(1, V("key%d" % t), V("msg%d" % t))
 
     def layer(t, h):
         for b in range(4):
             mm(2 + b, NC[h], piece("wq", b), piece("wp", b), cols("xq%d" % t, h), cols("xs%d" % t, h))
             act(V("pt%d" % t, 4 * CC[h] + b, 4 * CC[h + 1], 4), bank(2 + b, NC[h]), scale=0.03125)
         quant(cols("pq%d" % t, h), cols("pp%d" % t, h), wide("pt%d" % t, h))
-        send(raw(cols("lq%d" % t, h)), raw(cols("pq%d" % t, h)))
-        return send(cols("lp%d" % t, h), cols("pp%d" % t, h))
+        send(-1, raw(cols("lq%d" % t, h)), raw(cols("pq%d" % t, h)))
+        send(-1, cols("lp%d" % t, h), cols("pp%d" % t, h))
 
     def count(t, h):
         n = NC[h]
-        af, za = V("af%d" % h, 0, NK[h]), V("z4", 8 * KC[h] + 3, 8 * KC[h] + 4 * NK[h], 4)
-        act(cols("rep", h), by(V("ramp"), third("msg%d" % t, h, 0, 1)))
-        ts(af, za, B4, A.add)
-        ts(lst("nb", h), za, -SHARP, A.mult, EPS - SHARP * B4, A.add)
+        act(cols("rep", h), by(V("ramp"), addr("msg%d" % t, h)), scale=UNIT, bias=-B4)
+        ts(lst("nb", h), zaddr(h), -SHARP / UNIT, A.mult, -EPS, A.add)
         lo = 8 * NK[0] ** 2 * h
         split, w = NK[h] - ROWS[t][h], WC // 2
         for c in range(NK[h] - 1, split - 1, -1):
-            e0, s0 = WC * (8 * h + c - split), w * (8 * h + c - split + 1)
-            ts(V("eq", e0, e0 + 16 * c), V("rep", CC[h], CC[h] + 16 * c), V("af%d" % h, c, c + 1), A.is_equal, EPS, A.mult)
+            e0, s0, z = WC * (8 * h + c - split), w * (8 * h + c - split + 1), za(h) + 4 * c + 3
+            ts(V("eq", e0, e0 + 16 * c), V("rep", CC[h], CC[h] + 16 * c), V("z4", z, z + 1), A.is_equal, -EPS, A.mult)
             scan(V("sums", s0 - 8 * c, s0), V("eq", e0, e0 + 8 * c), V("eq", e0 + 8 * c, e0 + 16 * c), 0.0, A.add, A.add)
         for c in range(split - 1, 0, -1):
             k = KC[h] + c
-            act(V("junk", lo, lo + 16 * c), V("rep", CC[h], CC[h] + 16 * c), func=F.Tanh, scale=SHARP, bias=V("nb", k, k + 1),
-                acc=V("acc", k, k + 1), after=[warm])
+            act(V("junk", lo, lo + 16 * c), V("rep", CC[h], CC[h] + 16 * c), func=F.Tanh, scale=SHARP / UNIT, bias=V("nb", k, k + 1),
+                acc=slot("acc", 3, k, k + 1), after=[warm])
             lo += 16 * c
-        tt(cols("cmp", h), by(af, V("cl", 0, NK[h])), cols("rep", h), A.is_equal)
-        scan(cols("zs", h), V("mask", 0, n), cols("cmp", h), 0.0, A.mult, A.add)
-        ts(lst("z1", h), V("zs", CC[h] + 15, CC[h + 1], 16), 1.0 / NEAR, A.mult)
-        tt(lst("base", h), lst("z1", h), af, A.add)
-        ts(V("e1", KC[h], KC[h] + split), V("acc", KC[h], KC[h] + split), STEP / EPS, A.mult, 2.0 ** 28 + STEP // 2, A.add)
-        ts(V("e1", KC[h] + split, KC[h + 1]), V("sums", w * (8 * h + 1) - 1, w * (8 * h + NK[h] - split), w), STEP / EPS, A.mult)
-        ts(lst("e2", h), lst("e1", h), 511 * STEP, A.bitwise_and)
-        if h == 0:
-            tt(lst("s1", h), lst("e2", h), lst("base", h), A.add)
-            tt(lst("s2", h), lst("s1", h), lst("jd", h), A.min)
-            cp(third("msg%d" % t, h, 2, 3), lst("s2", h))
-            send(third("key%d" % t, h, 2, 3), third("msg%d" % t, h, 2, 3))
-        else:
-            tt(pairs("cnt%d" % t, 0), lst("e2", h), lst("base", h), A.add)
-            send(V("got%d" % t), V("cnt%d" % t))
+        tt(cols("cmp", h), by(V("z4", za(h), za(h) + 4 * NK[h]), V("cl", 0, NK[h])), cols("rep", h), A.is_equal)
+        scan(cols("zs", h), cols("cmp", h), V("mask", 0, n), 0.0, A.add, A.mult)
+        tt(slot("acc", 6, KC[h], KC[h + 1]), V("zs", CC[h] + 14, CC[h + 1], 16), zaddr(h), A.add)
+        if split < NK[h]:
+            cp(slot("acc", 3, KC[h] + split, KC[h + 1]), V("sums", w * (8 * h + 1) - 1, w * (8 * h + NK[h] - split), w))
 
     def build(t, h):
-        tab, key, n = "tab%d" % t, "key%d" % t, NC[h]
-        act(cols("val", h), by(V("ramp"), third(key, h, 1, 2)))
-        if h == 0:
-            scatter(V(tab), third(key, h, 2, 3), cols("val", h))
-            return
-        at = third(key, h, 0, 1)
-        act(V("cf", 0, n), by(V(tab, 0, SLOTS), at), func=F.Sign)
-        tt(V("cg", 0, n), by(V(tab, STEP, DUMP), at), V("cf", 0, n), A.max)
-        scan(V("cz", 0, n), V("cg", 0, n), V("d16", 0, n), -B16, A.max, A.add)
-        ts(pairs("pen", 1), V("cz", 15, n, 16), B16 + 1.0, A.add, STEP / 2.0, A.mult)
-        scan(V("s4"), V("pen"), V("got%d" % t), 0.0, A.add, A.min)
-        cp(lst("so", h), pairs("s4", 1))
+        tab, msg, n = "tab%d" % t, "msg%d" % t, NC[h]
+        act(cols("val", h), by(V("ramp"), entry(msg, h)))
+        if h == 1:
+            act(V("cf", 0, n), by(V(tab, 0, SLOTS), addr(msg, h)), func=F.Sign)
+            tt(V("cg", 0, n), by(V(tab, STEP, DUMP + 1), beyond(msg, h)), V("cf", 0, n), A.max)
+            scan(V("cz", 0, n), V("cg", 0, n), V("d8", 0, n), -DROP, A.max, A.add)
+            ts(slot("acc", 4, KC[h], KC[h + 1]), V("cz", 15, n, 16), EPS * DROP / (2 * DROP + 4), A.mult, GRID + EPS * DROP / 4, A.add)
+        lo, hi = TUP * KC[h], TUP * KC[h + 1] - 3
+        scan(V("pl", lo, hi), V("acc", lo, hi), V("acc", lo + 3, hi + 3), -float(WHOLE), A.subtract, A.min)
+        ts(lst("so", h), slot("pl", 6, KC[h], KC[h + 1]), B4, A.add, GROW, A.mult)
         scatter(V(tab), lst("so", h), cols("val", h))
-        cp(V(tab, SLOTS, STEP, STEP - 1 - SLOTS), V(tab, 0, DUMP, DUMP - 1))
+        if h == 1:
+            cp(V(tab, SLOTS, STEP + 1, STEP - SLOTS), V(tab, 0, DUMP + 1, DUMP))
 
     def unpack(t):
         for h in range(2):
             for b in range(4):
                 mm(2 + b, NC[h], piece("eq4", b), piece("es", b), cols("lq%d" % t, h), cols("lp%d" % t, h))
-                act(V("dn", DW * b + CC[h], DW * b + CC[h + 1]), bank(2 + b, NC[h]))
+                (cp if 4 * h + b >= 8 - UNV[t] else act)(V("dn", DW * b + CC[h], DW * b + CC[h + 1]), bank(2 + b, NC[h]))
 
     def search(t):
-        tab = "tab%d" % t
-        for i in range(2):
-            for h in range(2):
-                at, lo, hi = third("msg%d" % t, h, 0, 1), C * i + CC[h], C * i + CC[h + 1]
-                act(V("tf", lo, hi), by(V(tab, 0, SLOTS), at) if i == 0 else by(V(tab, 0, SLOTS + 1), half("q1", h, 0)), bias=float(SLOTS))
-                tt(V("look", lo, hi), by(V(tab, STEP - 8, DUMP), half("q7", h, 0)) if i == 0 else by(V(tab, STEP, DUMP), at), V("tf", lo, hi), A.max)
-                scan(V("z16", lo, hi), V("look", lo, hi), V("d16", 0, NC[h]), -B16, A.max, A.add)
-                tt(half("x1", h, i), V("z16", lo + 15, hi, 16), lst("hb", h), A.add)
+        tab, key = "tab%d" % t, "key%d" % t
+        ts(V("hb"), V(key, 0, 2 * K), 512.0, A.is_ge, 512.0, A.mult)
         for h in range(2):
+            for i in range(2):
+                at, lo, hi = (beyond if i else addr)(key, h), C * i + CC[h], C * i + CC[h + 1]
+                act(V("tf", lo, hi), by(V(tab, 0, SLOTS + i), at), bias=float(SLOTS))
+                tt(V("look", lo, hi), by(V(tab, STEP, DUMP + 1), at), V("tf", lo, hi), A.max)
+                scan(V("z16", lo, hi), V("look", lo, hi), V("d16", 0, NC[h]), -DROP, A.max, A.add)
+                tt(pair("x1", h, 1 - i), V("z16", lo + 15, hi, 16), entry("hb", h), A.add)
             ts(both("x2", h), both("x1", h), SLOTS - 1, A.bitwise_and)
-            ts(lst("x3", h), half("x2", h, 0), float(C), A.is_lt, 4096.0, A.mult)
-            tt(lst("x4", h), half("x2", h, 1), lst("x3", h), A.max)
-            tt(lst("x5", h), half("x2", h, 0), lst("x4", h), A.min)
-            ts(lst("fin", h), lst("x5", h), float(C), A.min)
+            ts(pair("x3", h, 1), pair("x2", h, 1), float(C), A.is_lt, 4096.0, A.mult)
+            ts(both("x4", h), both("x2", h), float(C), A.min)
+            scan(both("x5", h), both("x3", h), both("x4", h), 0.0, A.max, A.min)
+            cp(lst("fin%d" % t, h), pair("x5", h, 1))
+            send(-1, lst("got%d" % t, h), lst("fin%d" % t, h))
+
+    def renew(t):
         for h in range(2):
             for b in range(4):
                 lo, hi = 4 * CC[h] + b, 4 * CC[h + 1]
-                tt(V(state[t + 1], lo, hi, 4), by(V("dn", DW * b, DW * b + C + 1), lst("fin", h)), V("pt%d" % t, lo, hi, 4), A.add)
+                tt(V(state[t + 1], lo, hi, 4), by(V("dn", DW * b, DW * b + C + 1), lst("got%d" % t, h)), V("pt%d" % t, lo, hi, 4), A.add)
 
     def store(h):
         quant_state(2, h)
@@ -441,20 +445,19 @@ def rank_program(g, core, T, topo):
         dma("a", hbm(T.y[:, CC[h]:CC[h + 1]]), cols("yo", h))
 
     clear(0)
+    clear(1)
     for t in range(2):
         keys(t, 0)
         layer(t, 0)
         keys(t, 1)
-        last = layer(t, 1)
-        places(t)
-        if t == 0:
-            clear(1, [last])
+        layer(t, 1)
         count(t, 0)
         count(t, 1)
         build(t, 0)
         build(t, 1)
         unpack(t)
         search(t)
+        renew(t)
     store(0)
     store(1)
     op("g", None, [], [], after=ends)

import numpy as np
from concourse.mybir import dt, AluOpType as A, AxisListType, ActivationFunctionType as F

C, K = 448, 28
KC = [0, 14, K]
CC = [16 * k for k in KC]
NK = [KC[1], K - KC[1]]
NC = [16 * k for k in NK]
WK, WC = max(NK), max(NC)
SLOTS = 1024
DW = 464
STEP = 4096
DUMP = STEP + SLOTS
TW = 5576
SHARP, EPS = 16.0, 2.0 ** -9
UNIT = EPS / STEP
GROW = (STEP + 1) / STEP / UNIT
B4 = 1536 * UNIT
WHOLE, GRID, TUP = 3 * 2 ** 22, 3 * 2 ** 13, 10
EMPTY = -1024.0
BIAS = 16.0
B16, S16 = 2000.0, 4096
DROP = 2 * SLOTS + BIAS
NEAR = UNIT / 128
TINY = 2.0 ** -110
ROWS = [[4, 4], [4, 4]]
CLEAR_G = ()
SPLIT = True
UNV = [0, 0]
HALF = "float16"
Q4 = "float8_e4m3fn_x4"

SCRATCH = {
    "xin": ("sbuf", [128, 4 * C], "bfloat16"), "xa": ("sbuf", [128, 4 * C], "bfloat16"), "xb": ("sbuf", [128, 4 * C], "bfloat16"),
    "ut": ("sbuf", [128, 512], "bfloat16"), "vt": ("sbuf", [128, 512], "bfloat16"),
    "uq": ("sbuf", [128, 128], Q4), "us": ("sbuf", [128, 128], "uint8"),
    "vq": ("sbuf", [128, 128], Q4), "vs": ("sbuf", [128, 128], "uint8"),
    "wq": ("sbuf", [128, 512], Q4), "wp": ("sbuf", [128, 512], "uint8"),
    "ones": ("sbuf", [128, 516], "bfloat16"),
    "et": ("sbuf", [128, 516], "bfloat16"), "eq4": ("sbuf", [128, 512], Q4), "es": ("sbuf", [128, 512], "uint8"),
    "kt": ("sbuf", [128, 1024], "bfloat16"), "kq": ("sbuf", [128, 256], Q4), "ks": ("sbuf", [128, 256], "uint8"),
    "bits": ("sbuf", [128, CC[1] + 512], "bfloat16"),
    "dn": ("sbuf", [128, 4 * DW], "bfloat16"),
    "ps": ("psum", [128, 4096], "float32"),
    "pi": ("sbuf", [128, 8], "int32"), "col": ("sbuf", [128, 16], "float32"), "k16": ("sbuf", [128, 16], "float32"),
    "gm": ("sbuf", [128, 32], "float32"), "r16": ("sbuf", [128, 16], "float32"), "c16": ("sbuf", [128, K], "float32"),
    "t4": ("sbuf", [128, 8 * K], "float32"), "t5": ("sbuf", [128, 8 * K], "float32"), "d4": ("sbuf", [128, 8 * K], "float32"),
    "jx": ("sbuf", [128, 2 * K], "float32"), "jy": ("sbuf", [128, 2 * K], "float32"),
    "t16": ("sbuf", [128, WC], "bfloat16"), "d16": ("sbuf", [128, WC], HALF), "d8": ("sbuf", [128, WC], HALF),
    "r1": ("sbuf", [128, WC], "bfloat16"), "m1": ("sbuf", [128, WC], "bfloat16"), "mask": ("sbuf", [128, WC], "bfloat16"),
    "ramp": ("sbuf", [128, SLOTS], "float32"), "cl": ("sbuf", [128, WK], "uint16"),
    "warm": ("sbuf", [128, 16], "float32"),
    "z4": ("sbuf", [128, 8 * K], "float32"),
    "hb": ("sbuf", [128, 2 * K], "float32"), "nb": ("sbuf", [128, K], "float32"),
    "rep": ("sbuf", [128, C], "float32"), "val": ("sbuf", [128, C], "float32"),
    "junk": ("sbuf", [128, 8 * (NK[0] ** 2 + NK[1] ** 2)], "bfloat16"),
    "acc": ("sbuf", [128, TUP * K], "float32"), "pl": ("sbuf", [128, TUP * K], "float32"),
    "eq": ("sbuf", [128, 16 * WC], "bfloat16"), "sums": ("sbuf", [128, 8 * WC], "bfloat16"),
    "cmp": ("sbuf", [128, C], "bfloat16"), "zs": ("sbuf", [128, C], "bfloat16"),
    "cf": ("sbuf", [128, WC], "float32"), "cg": ("sbuf", [128, WC], HALF), "cz": ("sbuf", [128, WC], HALF),
    "so": ("sbuf", [128, K], "uint16"),
    "tf": ("sbuf", [128, 2 * C], "float32"), "look": ("sbuf", [128, 2 * C], HALF), "z16": ("sbuf", [128, 2 * C], HALF),
    "x1": ("sbuf", [128, 2 * K], "int32"), "x2": ("sbuf", [128, 2 * K], "int32"),
    "x3": ("sbuf", [128, 2 * K], "float32"), "x4": ("sbuf", [128, 2 * K], "float32"), "x5": ("sbuf", [128, 2 * K], "float32"),
    "yo": ("sbuf", [128, C], "float32"),
}
for _t in range(3):
    SCRATCH["xq%d" % _t] = ("sbuf", [128, C], Q4)
    SCRATCH["xs%d" % _t] = ("sbuf", [128, C], "uint8")
for _t in range(2):
    SCRATCH["bq%d" % _t] = ("sbuf", [128, 128], Q4)
    SCRATCH["bs%d" % _t] = ("sbuf", [128, 128], "uint8")
    SCRATCH["pt%d" % _t] = ("sbuf", [128, 4 * C], "bfloat16")
    SCRATCH["pq%d" % _t] = ("sbuf", [128, C], Q4)
    SCRATCH["pp%d" % _t] = ("sbuf", [128, C], "uint8")
    SCRATCH["lq%d" % _t] = ("sbuf", [128, C], Q4)
    SCRATCH["lp%d" % _t] = ("sbuf", [128, C], "uint8")
    SCRATCH["msg%d" % _t] = ("sbuf", [128, 3 * K], "uint16")
    SCRATCH["key%d" % _t] = ("sbuf", [128, 3 * K], "uint16")
    SCRATCH["fin%d" % _t] = ("sbuf", [128, K], "uint16")
    SCRATCH["got%d" % _t] = ("sbuf", [128, K], "uint16")
    SCRATCH["tab%d" % _t] = ("sbuf", [128, TW], "float32")

SEMAPHORES = (["cv", "ca", "ct", "cg"] + ["d%d" % i for i in range(20)] + ["l%d" % i for i in range(16)]
              + ["r%d" % i for i in range(16)])

ORDER = [6,15,0,1,2,3,10,4,5,17,21,20,19,8,22,18,7,9,12,25,27,23,16,36,55,38,42,39,40,56,58,24,57,41,43,81,73,49,26,47,45,28,33,74,30,29,82,34,13,44,31,104,83,11,60,35,76,32,105,84,37,61,85,46,106,91,75,86,14,107,88,87,62,53,108,89,130,131,93,64,52,63,109,80,90,92,111,65,110,95,145,132,147,141,149,97,148,143,146,117,136,153,133,134,51,144,138,50,140,137,150,79,142,135,139,114,154,112,151,152,155,164,176,177,157,170,178,159,68,96,113,179,168,166,165,167,160,156,66,172,181,161,163,67,98,182,94,123,173,169,54,162,115,116,158,171,183,180,119,174,175,184,121,99,124,185,120,72,100,101,122,186,78,48,118,187,70,205,102,103,206,188,71,125,210,207,126,127,221,128,129,211,77,225,208,212,209,213,193,214,191,69,215,216,195,192,217,189,222,194,196,218,226,190,219,220,223,203,227,224,199,228,204,197,229,59,200,201,230,231,198,232,202,233,239,234,235,237,236,238,244,242,245,240,260,246,243,254,261,256,247,241,255,248,257,258,249,267,251,259,250,252,268,293,253,294,280,262,269,284,297,309,263,264,303,301,265,266,270,307,304,299,308,312,305,271,311,282,310,306,298,272,302,274,295,286,273,300,313,296,316,275,277,314,315,317,276,339,340,278,279,322,327,341,326,320,329,323,342,334,324,318,344,325,335,328,331,345,330,332,333,343,336,319,321,346,281,337,338,347,285,352,287,348,283,349,358,350,356,354,351,369,368,288,373,291,292,370,289,290,357,374,384,371,355,375,359,372,388,376,377,353,385,379,378,386,380,387,381,389,382,383,360,390,362,361,391,364,392,363,366,393,365,394,395,367,396,399,397,398,400,401,402,407,406,409,408,404,410,403,405,411,412,418,415,416,414,413,419,417,420,421]


def depend(ops):
    writer, readers, banks = {}, {}, {}
    for i, o in enumerate(ops):
        deps = set(o["after"])
        for is_out, views in ((False, o["r"]), (True, o["w"])):
            for name, lo, hi, step in views:
                if name == "ps":
                    deps.update(banks.get(lo // 512, []))
                    continue
                if name not in writer:
                    writer[name], readers[name] = np.full(SCRATCH[name][1][1], -1), []
                deps.update(int(n) for n in np.unique(writer[name][lo:hi:step]) if n >= 0)
                if is_out:
                    mine = set(range(lo, hi, step))
                    deps.update(n for n, seen in readers[name] if seen & mine)
                    readers[name] = [(n, seen - mine) for n, seen in readers[name] if seen - mine]
        o["deps"] = deps
        for is_out, views in ((False, o["r"]), (True, o["w"])):
            for name, lo, hi, step in views:
                if name == "ps":
                    banks[lo // 512] = [i]
                elif is_out:
                    writer[name][lo:hi:step] = i
                else:
                    readers[name].append((i, set(range(lo, hi, step))))


def schedule(g, T, ops):
    queue = {"v": g.vector, "a": g.scalar, "t": g.tensor, "g": g, "s": g.sync}
    depend(ops)
    order = ORDER or list(range(len(ops)))
    place = {i: k for k, i in enumerate(order)}
    assert sorted(order) == list(range(len(ops))) and all(place[d] < place[i] for i, o in enumerate(ops) for d in o["deps"])
    clock = {e: {} for e in queue}
    for i in order:
        o = ops[i]
        o["waits"] = []
        if o["e"] is not None:
            ck = clock[o["e"]]
            for d in sorted(o["deps"], key=lambda d: -place[d]):
                p = ops[d]
                if ck.get(p["src"], -1) >= place[d]:
                    continue
                o["waits"].append(d)
                p["used"] = True
                for s, n in p["snap"].items():
                    ck[s] = max(ck.get(s, -1), n)
            o["snap"] = dict(ck)
        else:
            o["snap"] = {}
        o["snap"][o["src"]] = place[i]
    count = {}
    for i in order:
        o = ops[i]
        if o["sem"] is None and o.get("used"):
            count[o["e"]] = count.get(o["e"], 0) + 1
            o["sem"], o["n"], o["inc"] = "c" + o["e"], count[o["e"]], 1
    for i in order:
        o = ops[i]
        if o["e"] is None:
            continue
        q = queue[o["e"]]
        for d in o["waits"]:
            q.wait_ge(T.sem[ops[d]["sem"]], ops[d]["n"])
        if o["f"] is not None:
            ins = o["f"](q)
            if o.get("inc"):
                ins.then_inc(T.sem[o["sem"]], o["inc"])


def rank_program(g, core, T, topo):
    rank = T.rank_of(core)
    if rank is None:
        return
    n_ranks = len(T.cores)
    near = {step: T.cores[(rank + step) % n_ranks] for step in (-1, 1)}
    ops, nd, nr, ends = [], [0], [0], []
    u8 = dt.uint8

    def V(name, lo=0, hi=None, step=1):
        hi = SCRATCH[name][1][1] if hi is None else hi
        return (T[name][:, lo:hi:step] if step > 1 else T[name][:, lo:hi], [(name, lo, hi, step)])

    def by(win, off):
        return (win[0].indirect(off[0]), win[1] + off[1])

    def raw(v):
        return (v[0].bitcast(u8), v[1])

    def ap(v):
        return v[0] if isinstance(v, tuple) else v

    def op(e, f, ins, outs, after=()):
        ops.append({"e": e, "f": f, "r": [k for v in ins if isinstance(v, tuple) for k in v[1]], "w": [k for v in outs for k in v[1]],
                    "src": e, "sem": None, "after": list(after)})
        return len(ops) - 1

    def dma(e, out, in_):
        s = "d%d" % nd[0]
        nd[0] += 1
        i = op(e, lambda q: q.dma_start(out[0], in_[0]), [in_], [out])
        ops[i].update({"src": s, "sem": s, "n": 16, "inc": 16})
        ends.append(i)

    def send(step, out, in_):
        k = nr[0]
        nr[0] += 1
        ls, rs = "l%d" % k, "r%d" % k
        dst, src = near[step], near[-step]
        rid, pid = topo.addr(dst, core)
        i = op("g", lambda q: q.remote_dma(out[0], in_[0], T.sem[rs], T.sem[ls], pid, rid, topo.mask(core, dst)), [in_], [])
        ops[i].update({"src": ls, "sem": ls, "n": len(topo.engines(core, dst))})
        ends.append(i)
        j = op(None, None, [], [out], after=[i])
        ops[j].update({"src": rs, "sem": rs, "n": len(topo.engines(src, core))})
        return i

    def ts(out, in0, s1, op0, s2=None, op1=None):
        if op1 is None:
            op("v", lambda q: q.tensor_scalar(out[0], in0[0], ap(s1), None, op0), [in0, s1], [out])
        else:
            op("v", lambda q: q.tensor_scalar(out[0], in0[0], ap(s1), ap(s2), op0, op1), [in0, s1, s2], [out])

    def tt(out, in0, in1, o):
        op("v", lambda q: q.tensor_tensor(out[0], in0[0], in1[0], o), [in0, in1], [out])

    def cp(out, in_):
        op("v", lambda q: q.tensor_copy(out[0], in_[0]), [in_], [out])

    def scatter(win, off, in_):
        op("v", lambda q: q.tensor_copy(win[0].indirect(off[0]), in_[0]), [in_, off], [win])

    def fill(out, c):
        op("v", lambda q: q.memset(out[0], c), [], [out])

    def scan(out, d0, d1, first, op0, op1):
        op("v", lambda q: q.tensor_tensor_scan(out[0], d0[0], d1[0], first, op0, op1), [d0, d1], [out])

    def quant(qb, sb, in_):
        op("v", lambda q: q.quantize_mx(qb[0], sb[0], in_[0]), [in_], [qb, sb])

    def act(out, in_, func=F.Identity, acc=None, after=(), **kw):
        more = {k: ap(v) for k, v in kw.items()}
        if acc is not None:
            more["accum_out"] = acc[0]
        return op("a", lambda q: q.activation(out[0], in_[0], func, **more), [in_] + list(kw.values()),
                  [out] + ([acc] if acc is not None else []), after)

    def iota(out, pattern, base, mult, whole=False, after=()):
        if whole:
            op("g", lambda q: q.iota(out[0], pattern, base, mult), [], [out], after)
        else:
            op("g", lambda q: q.iota(out[0], pattern, base, mult, allow_small_or_imprecise_dtypes=True), [], [out], after)

    def bank(b, n):
        return V("ps", 512 * b, 512 * b + n)

    def mm(b, n, lq, ls, rq, rs):
        out = bank(b, n)
        op("t", lambda q: q.matmul_mx(out[0], lq[0], ls[0], rq[0], rs[0], True, True), [lq, ls, rq, rs], [out])

    col = lambda i: V("col", i, i + 1)
    QC, GC, SC, PW0, PW1, PW, PH, CB4, CR4, CB16, CR16 = range(11)
    cols = lambda name, h: V(name, CC[h], CC[h + 1])
    wide = lambda name, h: V(name, 4 * CC[h], 4 * CC[h + 1])
    lst = lambda name, h: V(name, KC[h], KC[h + 1])
    half = lambda name, h, i: V(name, 2 * KC[h] + NK[h] * i, 2 * KC[h] + NK[h] * (i + 1))
    both = lambda name, h: V(name, 2 * KC[h], 2 * KC[h + 1])
    pair = lambda name, h, i: V(name, 2 * KC[h] + i, 2 * KC[h + 1], 2)
    slot = lambda name, k, lo=0, hi=K: V(name, TUP * lo + k, TUP * (hi - 1) + k + 1, TUP)
    addr = lambda name, h: half(name, h, 1 - h)
    entry = lambda name, h: half(name, h, h)
    beyond = lambda name, h: V(name, 2 * K + KC[h], 2 * K + KC[h + 1])
    za = lambda h: 8 * KC[h] + 4 * NK[h] * (1 - h)
    zaddr = lambda h: V("z4", za(h) + 3, za(h) + 4 * NK[h], 4)
    piece = lambda name, b: V(name, 128 * b, 128 * (b + 1))
    hbm = lambda t: (t, [])

    dma("s", wide("xin", 0), hbm(T.x[:, 0:4 * CC[1]]))
    dma("a", V("ut"), hbm(T.u[:]))
    dma("s", wide("xin", 1), hbm(T.x[:, 4 * CC[1]:4 * C]))
    dma("s", raw(V("wq")), hbm(T.wc[:]))
    dma("s", V("wp"), hbm(T.ws[:]))
    dma("s", V("vt"), hbm(T.v[:]))

    iota(V("pi", 0, 1), [[0, 1]], 0, 1, whole=True)
    iota(V("r16"), [[1, 16]], 0, 0)
    iota(V("gm"), [[1, 8], [0, 4]], 0, 0)
    iota(V("c16"), [[16, K]], 0, 0)
    iota(V("t4"), [[0, 2 * K], [2, 4]], 0, 0)
    iota(V("ramp", 0, 512), [[1, 512]], 0, 0)
    iota(V("ramp", 512, SLOTS), [[1, 512]], 512, 0)
    iota(V("r1"), [[0, WK], [1, 16]], 1, 0)
    iota(V("t16"), [[0, WK], [S16, 16]], 0, 0)
    fill(V("bits", CC[1], 512), 0.0)
    fill(V("ones"), 1.0)
    warm = act(V("warm"), V("bits", CC[1], CC[1] + 16), func=F.Tanh)
    fill(V("kt"), 0.0)
    ts(V("pi", 1, 2), V("pi", 0, 1), 15, A.bitwise_and)
    ts(V("pi", 2, 3), V("pi", 0, 1), 4, A.arith_shift_right)
    ts(V("pi", 3, 4), V("pi", 0, 1), 2, A.arith_shift_right, 3, A.bitwise_and)
    cp(V("col", 0, 3), V("pi", 1, 4))
    ts(V("k16"), V("r16"), col(QC), A.is_lt, 1.0, A.add)
    op("v", lambda q: q.tensor_reduce(T.col[:, PW0:PW0 + 1], T.k16[:], AxisListType.X, A.mult, negate=True), [V("k16")], [col(PW0)])
    ts(col(PW1), col(QC), 10.0, A.is_lt, 0.5 * UNIT, A.mult)
    ts(col(PW), col(PW1), col(PW0), A.mult)
    ts(col(PH), col(QC), 10.0, A.is_equal, -256.0 * UNIT, A.mult)
    for i, w in enumerate((PW, PH)):
        for r in range(4):
            ts(V("kt", 512 * i + 5 * r, 512 * (i + 1), 16), V("gm"), col(GC), A.is_equal, col(w), A.mult)
        quant(piece("kq", i), piece("ks", i), V("kt", 512 * i, 512 * (i + 1)))
    act(col(CB4), col(SC), scale=-2 * B4, bias=B4)
    act(col(CR4), col(SC), scale=B4, bias=-5 * B4)
    fill(V("jx", NK[0], NK[0] + K), 511.5)
    for h in range(2):
        ts(entry("jx", h), lst("c16", h), col(QC), A.add, 256.0 + BIAS, A.add)
    act(V("t5"), V("t4"), scale=B4, bias=col(CB4))
    ts(V("d4"), V("t5"), B4, A.min)
    act(V("jy"), V("jx"), scale=UNIT, bias=col(CR4))
    tt(V("d4", 3, 8 * K, 4), V("d4", 3, 8 * K, 4), V("jy"), A.add)
    quant(V("uq"), V("us"), V("ut"))
    quant(V("vq"), V("vs"), V("vt"))
    iota(V("acc"), [[0, TUP * K]], GRID, 0)
    for k, c in ((1, -WHOLE), (2, -WHOLE), (7, WHOLE)):
        iota(slot("acc", k), [[0, K]], c, 0)
    for h in range(2):
        act(slot("acc", 9, KC[h], KC[h + 1]), entry("jx", h), scale=UNIT, bias=(DUMP - 256.0 - BIAS) * UNIT - B4)
    fill(V("x3", 0, 2 * K, 2), 4096.0)
    act(col(CB16), col(QC), scale=-float(S16), bias=B16)
    act(col(CR16), col(QC), scale=B16, bias=-16 * B16 - DROP)
    ts(V("cl"), V("c16", 0, WK), 0.25, A.mult, 3.0, A.add)
    fill(V("dn", C, 4 * DW, DW), 0.0)
    fill(V("acc", 3, TUP * K, TUP * KC[1]), 0.0)
    ts(V("m1"), V("r1"), col(QC), A.is_equal, EPS / NEAR, A.mult)
    ts(V("mask"), V("m1"), 1.0, A.max)
    ts(V("mask", 14, WC, 16), V("mask", 14, WC, 16), NEAR, A.mult)
    fill(V("mask", 15, WC, 16), 0.0)
    ts(V("d16"), V("t16"), col(CB16), A.add, B16, A.min)
    ts(V("d16", 15, WC, 16), V("d16", 15, WC, 16), col(CR16), A.add)
    ts(V("d8"), V("d16"), 0.5, A.mult)
    op("g", lambda q: q.affine_select(T.et[:], T.ones[:], [[1, 516]], A.is_equal, 0.0, -3, -4), [V("ones")], [V("et")])
    for b in range(4):
        quant(piece("eq4", b), piece("es", b), V("et", 3 - b, 515 - b))

    def clear(t):
        for lo, n in ((0, 512), (512, 512), (STEP, 512), (STEP + 512, 513)):
            if t == 1 or lo in CLEAR_G:
                iota(V("tab%d" % t, lo, lo + n), [[0, n]], int(EMPTY), 0)
            else:
                act(V("tab%d" % t, lo, lo + n), V("ones", 0, n), scale=EMPTY)

    state = ["xin", "xa", "xb"]

    def quant_state(t, h):
        quant(cols("xq%d" % t, h), cols("xs%d" % t, h), wide(state[t], h))

    def keys(t, h):
        quant_state(t, h)
        mm(h, NC[h], V("uq"), V("us"), cols("xq%d" % t, h), cols("xs%d" % t, h))
        act(V("bits", 512 * h, 512 * h + NC[h]), bank(h, NC[h]), func=F.Sign, bias=TINY)
        bq, bs, pad = V("bq%d" % h), V("bs%d" % h), (128 - 4 * NK[h]) * h
        quant(bq, bs, V("bits", CC[h], CC[h] + 512))
        for i in range(2):
            lo = 8 * KC[h] + 4 * NK[h] * (i if h else 1 - i)
            mm(6 + i, 128, piece("kq", i), piece("ks", i), bq, bs)
            scan(V("z4", lo, lo + 4 * NK[h]), V("ps", 512 * (6 + i) + pad, 512 * (6 + i) + pad + 4 * NK[h]), V("d4", lo, lo + 4 * NK[h]), -B4, A.max, A.add)
            if SPLIT:
                ts((entry if i else addr)("msg%d" % t, h), V("z4", lo + 3, lo + 4 * NK[h], 4), B4, A.add, 1 / UNIT, A.mult)
        if not SPLIT:
            ts(both("msg%d" % t, h), V("z4", 8 * KC[h] + 3, 8 * KC[h + 1], 4), B4, A.add, 1 / UNIT, A.mult)
        if h == 1:
            ts(V("msg%d" % t, 2 * K), V("z4", za(0) + 3, za(1) + 4 * NK[1], 4), B4 + UNIT, A.add, 1 / UNIT, A.mult)
            send(1, V("key%d" % t), V("msg%d" % t))

    def layer(t, h):
        for b in range(4):
            mm(2 + b, NC[h], piece("wq", b), piece("wp", b), cols("xq%d" % t, h), cols("xs%d" % t, h))
            act(V("pt%d" % t, 4 * CC[h] + b, 4 * CC[h + 1], 4), bank(2 + b, NC[h]), scale=0.03125)
        quant(cols("pq%d" % t, h), cols("pp%d" % t, h), wide("pt%d" % t, h))
        send(-1, raw(cols("lq%d" % t, h)), raw(cols("pq%d" % t, h)))
        send(-1, cols("lp%d" % t, h), cols("pp%d" % t, h))

    def count(t, h):
        n = NC[h]
        act(cols("rep", h), by(V("ramp"), addr("msg%d" % t, h)), scale=UNIT, bias=-B4)
        ts(lst("nb", h), zaddr(h), -SHARP / UNIT, A.mult, -EPS, A.add)
        lo = 8 * NK[0] ** 2 * h
        split, w = NK[h] - ROWS[t][h], WC // 2
        for c in range(NK[h] - 1, split - 1, -1):
            e0, s0, z = WC * (8 * h + c - split), w * (8 * h + c - split + 1), za(h) + 4 * c + 3
            ts(V("eq", e0, e0 + 16 * c), V("rep", CC[h], CC[h] + 16 * c), V("z4", z, z + 1), A.is_equal, -EPS, A.mult)
            scan(V("sums", s0 - 8 * c, s0), V("eq", e0, e0 + 8 * c), V("eq", e0 + 8 * c, e0 + 16 * c), 0.0, A.add, A.add)
        for c in range(split - 1, 0, -1):
            k = KC[h] + c
            act(V("junk", lo, lo + 16 * c), V("rep", CC[h], CC[h] + 16 * c), func=F.Tanh, scale=SHARP / UNIT, bias=V("nb", k, k + 1),
                acc=slot("acc", 3, k, k + 1), after=[warm])
            lo += 16 * c
        tt(cols("cmp", h), by(V("z4", za(h), za(h) + 4 * NK[h]), V("cl", 0, NK[h])), cols("rep", h), A.is_equal)
        scan(cols("zs", h), cols("cmp", h), V("mask", 0, n), 0.0, A.add, A.mult)
        tt(slot("acc", 6, KC[h], KC[h + 1]), V("zs", CC[h] + 14, CC[h + 1], 16), zaddr(h), A.add)
        if split < NK[h]:
            cp(slot("acc", 3, KC[h] + split, KC[h + 1]), V("sums", w * (8 * h + 1) - 1, w * (8 * h + NK[h] - split), w))

    def build(t, h):
        tab, msg, n = "tab%d" % t, "msg%d" % t, NC[h]
        act(cols("val", h), by(V("ramp"), entry(msg, h)))
        if h == 1:
            act(V("cf", 0, n), by(V(tab, 0, SLOTS), addr(msg, h)), func=F.Sign)
            tt(V("cg", 0, n), by(V(tab, STEP, DUMP + 1), beyond(msg, h)), V("cf", 0, n), A.max)
            scan(V("cz", 0, n), V("cg", 0, n), V("d8", 0, n), -DROP, A.max, A.add)
            ts(slot("acc", 4, KC[h], KC[h + 1]), V("cz", 15, n, 16), EPS * DROP / (2 * DROP + 4), A.mult, GRID + EPS * DROP / 4, A.add)
        lo, hi = TUP * KC[h], TUP * KC[h + 1] - 3
        scan(V("pl", lo, hi), V("acc", lo, hi), V("acc", lo + 3, hi + 3), -float(WHOLE), A.subtract, A.min)
        ts(lst("so", h), slot("pl", 6, KC[h], KC[h + 1]), B4, A.add, GROW, A.mult)
        scatter(V(tab), lst("so", h), cols("val", h))
        if h == 1:
            cp(V(tab, SLOTS, STEP + 1, STEP - SLOTS), V(tab, 0, DUMP + 1, DUMP))

    def unpack(t):
        for h in range(2):
            for b in range(4):
                mm(2 + b, NC[h], piece("eq4", b), piece("es", b), cols("lq%d" % t, h), cols("lp%d" % t, h))
                (cp if 4 * h + b >= 8 - UNV[t] else act)(V("dn", DW * b + CC[h], DW * b + CC[h + 1]), bank(2 + b, NC[h]))

    def search(t):
        tab, key = "tab%d" % t, "key%d" % t
        ts(V("hb"), V(key, 0, 2 * K), 512.0, A.is_ge, 512.0, A.mult)
        for h in range(2):
            for i in range(2):
                at, lo, hi = (beyond if i else addr)(key, h), C * i + CC[h], C * i + CC[h + 1]
                act(V("tf", lo, hi), by(V(tab, 0, SLOTS + i), at), bias=float(SLOTS))
                tt(V("look", lo, hi), by(V(tab, STEP, DUMP + 1), at), V("tf", lo, hi), A.max)
                scan(V("z16", lo, hi), V("look", lo, hi), V("d16", 0, NC[h]), -DROP, A.max, A.add)
                tt(pair("x1", h, 1 - i), V("z16", lo + 15, hi, 16), entry("hb", h), A.add)
            ts(both("x2", h), both("x1", h), SLOTS - 1, A.bitwise_and)
            ts(pair("x3", h, 1), pair("x2", h, 1), float(C), A.is_lt, 4096.0, A.mult)
            ts(both("x4", h), both("x2", h), float(C), A.min)
            scan(both("x5", h), both("x3", h), both("x4", h), 0.0, A.max, A.min)
            cp(lst("fin%d" % t, h), pair("x5", h, 1))
            send(-1, lst("got%d" % t, h), lst("fin%d" % t, h))

    def renew(t):
        for h in range(2):
            for b in range(4):
                lo, hi = 4 * CC[h] + b, 4 * CC[h + 1]
                tt(V(state[t + 1], lo, hi, 4), by(V("dn", DW * b, DW * b + C + 1), lst("got%d" % t, h)), V("pt%d" % t, lo, hi, 4), A.add)

    def store(h):
        quant_state(2, h)
        dma("s", hbm(T.oc[:, 4 * CC[h]:4 * CC[h + 1]]), raw(cols("xq2", h)))
        if h == 1:
            for k in range(4):
                dma("sa"[k // 2], hbm(T.osc[4 * k:4 * k + 4, :]), (T.xs2[32 * k:32 * k + 4, :], V("xs2")[1]))
        mm(h, NC[h], V("vq"), V("vs"), cols("xq2", h), cols("xs2", h))
        act(cols("yo", h), bank(h, NC[h]))
        dma("a", hbm(T.y[:, CC[h]:CC[h + 1]]), cols("yo", h))

    clear(0)
    clear(1)
    for t in range(2):
        keys(t, 0)
        layer(t, 0)
        keys(t, 1)
        layer(t, 1)
        count(t, 0)
        count(t, 1)
        build(t, 0)
        build(t, 1)
        unpack(t)
        search(t)
        renew(t)
    store(0)
    store(1)
    op("g", None, [], [], after=ends)
    schedule(g, T, ops)
